import numpy as np
import ml_dtypes


def mxq(x, axis, fmt="e4m3"):
    dtype, down = {"e4m3": (ml_dtypes.float8_e4m3fn, 7), "e5m2": (ml_dtypes.float8_e5m2, 14)}[fmt]
    v = np.moveaxis(np.asarray(x, np.float32).astype(ml_dtypes.bfloat16).astype(np.float64), axis, -1)
    blocks = v.reshape(v.shape[:-1] + (-1, 32))
    amax = np.abs(blocks).max(-1, keepdims=True)
    byte = np.maximum(np.where(amax > 0, np.frexp(amax)[1] - 1 + 127, 0) - down, 1)
    scale = np.exp2(byte - 127.0)
    codes = (blocks / scale).astype(np.float32).astype(dtype).astype(np.float64)
    return np.moveaxis((codes * scale).reshape(v.shape), -1, axis)


WIDE = False


def mx_kscale(k):
    if not WIDE:
        return np.ones(k)
    levels = np.array([10, -10, 5, -5, 0])
    if k % 512:
        return np.exp2(np.random.permutation(np.resize(levels, k // 32))).repeat(32)
    a = np.empty((k // 512, 16))
    for p in range(k // 512):
        a[p, :8] = np.random.permutation(np.resize(levels, 8))
        for g in range(8):
            far = levels[np.abs(levels - a[p, g]) >= 10]
            a[p, g + 8] = far[np.random.randint(len(far))]
    return np.exp2(a.ravel()).repeat(32)


def f64(x):
    return np.asarray(x).astype(np.float64)


def striped(idx):
    return np.tile(idx.reshape(-1, 16).T, (8, 1)).astype(np.uint16)


def unstriped(offs):
    return offs[:16].T.reshape(-1).astype(np.int64)


E2M1 = np.array([0.0, 0.5, 1.0, 1.5, 2.0, 3.0, 4.0, 6.0, -0.0, -0.5, -1.0, -1.5, -2.0, -3.0, -4.0, -6.0])


def pack_weight(w, fmt):
    k, n = w.shape
    w = f64(np.asarray(w, np.float32).astype(ml_dtypes.bfloat16)).reshape(k // 32, 32, n)
    amax = np.abs(w).max(1)
    if fmt == "e4m3":
        byte = np.frexp(amax)[1] - 1 + 127 - 7
    else:
        mant, ex = np.frexp(amax / 6.0)
        byte = np.where(mant > 0.5, ex, ex - 1) + 127
    byte = np.clip(np.where(amax > 0, byte, 1), 1, 254)
    scaled = (w * np.exp2(127.0 - byte)[:, None, :]).reshape(k, n).astype(np.float32)
    by_word = np.ascontiguousarray(scaled.reshape(k // 512, 128, 4, n).transpose(0, 1, 3, 2))
    if fmt == "e4m3":
        words = by_word.astype(ml_dtypes.float8_e4m3fn).view(np.uint8)
    else:
        c = by_word.astype(ml_dtypes.float4_e2m1fn).view(np.uint8) & 0xF
        words = (c[..., 0::2] | (c[..., 1::2] << 4)).reshape(k // 512, 128, 2 * n)
    return np.ascontiguousarray(words), np.ascontiguousarray(byte.astype(np.uint8).reshape(k // 512, 16, n))


def unpack_weight(words, scales, fmt):
    g, _, n = scales.shape
    words = np.ascontiguousarray(words).reshape(g, 128, n, -1)
    if fmt == "e4m3":
        vals = words.view(ml_dtypes.float8_e4m3fn).astype(np.float64)
    else:
        nib = np.empty((g, 128, n, 4), np.uint8)
        nib[..., 0::2] = words & 0xF
        nib[..., 1::2] = words >> 4
        vals = E2M1[nib]
    vals = vals * np.repeat(np.exp2(scales.astype(np.float64) - 127.0), 8, axis=1)[..., None]
    return vals.transpose(0, 1, 3, 2).reshape(g * 512, n)


def gelu(v):
    return 0.5 * v * (1.0 + np.tanh(np.sqrt(2.0 / np.pi) * (v + 0.044715 * v**3)))


K, K2, T, S, H, N, T2 = 512, 1024, 2048, 1024, 1024, 256, 2048

def setup_inputs():
    n = np.random.standard_normal
    s, s2, u = mx_kscale(K)[:, None], mx_kscale(K2)[:, None], mx_kscale(H)[:, None]
    tab_words, tab_scales = pack_weight(n((K, T)) * s, "e4m3")
    tab2_words, tab2_scales = pack_weight(n((K2, T)) * s2, "e4m3")
    w2_words, w2_scales = pack_weight(n((K, H)) / np.sqrt(K) / s * u.T, "e2m1")
    w3_words, w3_scales = pack_weight(n((K2, H)) / np.sqrt(K2) / s2 * u.T, "e4m3")
    perm = np.random.permutation(T2)
    return {
        "tab_words": tab_words, "tab_scales": tab_scales,
        "tab2_words": tab2_words, "tab2_scales": tab2_scales,
        "w1": (n((K, H)) / np.sqrt(K) / s * u.T).astype(np.float32),
        "w2_words": w2_words, "w2_scales": w2_scales,
        "w3_words": w3_words, "w3_scales": w3_scales,
        "wo": (n((H, N)) / np.sqrt(H) / u).astype(np.float32),
        "cap": ((0.4 + 0.8 * n((H, S))) * u).astype(np.float32),
        "ref": (0.7 * n((H, T2)) * u).astype(np.float32),
        "wg1": np.exp(0.3 * n((128, S))).astype(np.float32),
        "wg2": np.exp(0.3 * n((128, S))).astype(np.float32),
        "offs": striped(np.random.permutation(T)[:S]),
        "offs2": striped(np.random.permutation(T)[:S]),
        "offs3": striped(perm[:S]), "offs4": striped(perm[S:])}

def reference(tab_words, tab_scales, tab2_words, tab2_scales, w1, w2_words, w2_scales, w3_words, w3_scales,
              wo, cap, ref, wg1, wg2, offs, offs2, offs3, offs4):
    v = unpack_weight(tab_words, tab_scales, "e4m3")[:, unstriped(offs)]
    v2 = unpack_weight(tab2_words, tab2_scales, "e4m3")[:, unstriped(offs2)]
    w2 = unpack_weight(w2_words, w2_scales, "e2m1")
    w3 = unpack_weight(w3_words, w3_scales, "e4m3")
    h1 = np.maximum(mxq(f64(w1), 0, "e4m3").T @ v, w2.T @ v)
    h2 = np.minimum(w3.T @ v2, f64(cap))
    page = np.zeros((H, T2))
    page[:, unstriped(offs3)] = np.tile(f64(wg1), (H // 128, 1)) * h1
    page[:, unstriped(offs4)] = np.tile(f64(wg2), (H // 128, 1)) * h2
    z = page - f64(ref)
    return mxq(f64(wo), 0, "e4m3").T @ mxq(z, 0, "e4m3")

@@ -1,0 +1,256 @@
+from contextlib import ExitStack
+
+import concourse.mybir as mybir
+from concourse.masks import make_identity
+
+K, K2, T, S, H, N, T2 = 512, 1024, 2048, 1024, 1024, 256, 2048
+FLOPS = 2 * (2 * K * H * S + K2 * H * S + H * N * T2)
+
+F32 = mybir.dt.float32
+BF16 = mybir.dt.bfloat16
+I32 = mybir.dt.int32
+U32 = mybir.dt.uint32
+U16 = mybir.dt.uint16
+U8 = mybir.dt.uint8
+FP8X4 = mybir.dt.float8_e4m3fn_x4
+FP4X4 = mybir.dt.float4_e2m1fn_x4
+ALU = mybir.AluOpType
+COPY = mybir.ActivationFunctionType.Copy
+
+P = 128
+PACK = 4
+BANK = 512
+PAGES = H // P
+CHUNKS = T2 // BANK
+W1_COLS = 256
+
+
+def tile_list_two_phase_weave_kernel(
+    tc, tab_words, tab_scales, tab2_words, tab2_scales, w1, w2_words, w2_scales, w3_words, w3_scales,
+    wo, cap, ref, wg1, wg2, offs, offs2, offs3, offs4, out,
+):
+    nc = tc.nc
+    with ExitStack() as ctx:
+        keep = ctx.enter_context(tc.tile_pool(name="keep", bufs=1))
+        ring = ctx.enter_context(tc.tile_pool(name="ring", bufs=2))
+        psum = ctx.enter_context(tc.psum_pool(name="psum", bufs=1))
+
+        def bank(k):
+            return psum.tile([P, BANK], F32, name="bank%d" % k)
+
+        def load_list(src, name):
+            t = keep.tile([P, S // 16], U16, name=name)
+            nc.sync.dma_start(t[:], src)
+            return t
+
+        def load_words(src, width, name):
+            t = keep.tile([P, width], U32, name=name, align_bytes=64)
+            nc.sync.dma_start(t[:].bitcast(I32), src.rearrange("p n t -> p (n t)").bitcast(I32))
+            return t
+
+        def load_scales(src, name):
+            passes, width = src.shape[0], src.shape[2]
+            t = keep.tile([P, width], U8, name=name, align_bytes=64)
+            nc.vector.memset(t[:].bitcast(I32), 0)
+            for q in range(4):
+                nc.scalar.dma_start(
+                    t[32 * q : 32 * q + 4 * passes, :].bitcast(I32), src[:, 4 * q : 4 * q + 4, :].bitcast(I32)
+                )
+            return t
+
+        def gather(window, lst, dtype, name):
+            t = keep.tile([P, S], dtype, name=name, align_bytes=64)
+            nc.vector.tensor_copy(t[:], window[:].indirect(lst[:]))
+            return t
+
+        def cast_rows(raw, grouped):
+            nc.scalar.copy(
+                grouped.rearrange("p (c i) j -> p c j i", i=4), raw.rearrange("p j (c i) -> p c j i", i=4)
+            )
+
+        idx = load_list(offs, "idx")
+        tab_s = load_scales(tab_scales, "tab_s")
+        tab_w = load_words(tab_words[0], T, "tab_w")
+        idx2 = load_list(offs2, "idx2")
+        tab2_s = load_scales(tab2_scales, "tab2_s")
+        tab2_w = [load_words(tab2_words[a], T, "tab2_w%d" % a) for a in range(2)]
+
+        v_s = gather(tab_s, idx, U8, "v_s")
+        v_w = gather(tab_w, idx, U32, "v_w")
+
+        w1_w = [keep.tile([P, W1_COLS], U32, name="w1_w%d" % g, align_bytes=64) for g in range(H // W1_COLS)]
+        w1_s = [keep.tile([P, W1_COLS], U8, name="w1_s%d" % g, align_bytes=64) for g in range(H // W1_COLS)]
+
+        def quantize_w1(g):
+            raw = ring.tile([P, PACK, W1_COLS], F32, name="w1_raw", tag="rows_1k", bufs=4)
+            nc.sync.dma_start(
+                raw[:], w1[:, g * W1_COLS : (g + 1) * W1_COLS].rearrange("(p j) c -> p j c", j=PACK)
+            )
+            grouped = ring.tile([P, W1_COLS, PACK], BF16, name="w1_grouped", align_bytes=64)
+            cast_rows(raw[:], grouped[:])
+            nc.vector.quantize_mx(
+                out=w1_w[g][:].bitcast(FP8X4), scales=w1_s[g][:], in_=grouped[:].rearrange("p c j -> p (c j)")
+            )
+
+        quantize_w1(0)
+        w2_w = keep.tile([P, 2 * H], U8, name="w2_w", align_bytes=64)
+        nc.sync.dma_start(w2_w[:].bitcast(I32), w2_words[0].bitcast(I32))
+        w2_s = load_scales(w2_scales, "w2_s")
+
+        v2_s = gather(tab2_s, idx2, U8, "v2_s")
+        v2_w = [gather(tab2_w[a], idx2, U32, "v2_w%d" % a) for a in range(2)]
+
+        def load_negated(src, name):
+            t = keep.tile([P, S], F32, name=name)
+            nc.sync.dma_start(t[:], src)
+            nc.scalar.activation(t[:], t[:], COPY, scale=-1.0)
+            return t
+
+        idx3 = load_list(offs3, "idx3")
+        neg_wg1 = load_negated(wg1, "neg_wg1")
+        w3_w = [load_words(w3_words[a], H, "w3_w%d" % a) for a in range(2)]
+        w3_s = load_scales(w3_scales, "w3_s")
+        idx4 = load_list(offs4, "idx4")
+        neg_wg2 = load_negated(wg2, "neg_wg2")
+
+        ident = keep.tile([P, P], F32, name="ident")
+        make_identity(nc, ident[:])
+
+        def liquid(i):
+            g, c0 = divmod(i * P, W1_COLS)
+            h1 = ring.tile([P, S], F32, name="h1")
+            for half in range(S // BANK):
+                cols = slice(half * BANK, (half + 1) * BANK)
+                second = bank(4)
+                nc.tensor.matmul_mx(
+                    second[:], lhsT=w2_w[:, 2 * i * P : 2 * (i + 1) * P].bitcast(FP4X4),
+                    lhsT_scale=w2_s[:, i * P : (i + 1) * P],
+                    rhs=v_w[:, cols].bitcast(FP8X4), rhs_scale=v_s[:, cols], start=True, stop=True,
+                )
+                second_sb = ring.tile([P, BANK], F32, name="second_sb", bufs=4)
+                nc.scalar.copy(second_sb[:], second[:])
+                first = bank(half)
+                nc.tensor.matmul_mx(
+                    first[:], lhsT=w1_w[g][:, c0 : c0 + P].bitcast(FP8X4), lhsT_scale=w1_s[g][:, c0 : c0 + P],
+                    rhs=v_w[:, cols].bitcast(FP8X4), rhs_scale=v_s[:, cols], start=True, stop=True,
+                )
+                nc.vector.tensor_tensor(h1[:, cols], first[:], second_sb[:], ALU.max)
+            return h1
+
+        def vapour(i):
+            cap_rows = ring.tile([P, S], F32, name="cap_rows", tag="rows_1k", bufs=4)
+            nc.sync.dma_start(cap_rows[:], cap[i * P : (i + 1) * P, :])
+            h2 = ring.tile([P, S], F32, name="h2")
+            for half in range(S // BANK):
+                cols = slice(half * BANK, (half + 1) * BANK)
+                acc = bank(2 + half)
+                for a in range(2):
+                    nc.tensor.matmul_mx(
+                        acc[:], lhsT=w3_w[a][:, i * P : (i + 1) * P].bitcast(FP8X4),
+                        lhsT_scale=w3_s[4 * a :, i * P : (i + 1) * P],
+                        rhs=v2_w[a][:, cols].bitcast(FP8X4), rhs_scale=v2_s[4 * a :, cols],
+                        start=(a == 0), stop=(a == 1),
+                    )
+                nc.vector.tensor_tensor(h2[:, cols], acc[:], cap_rows[:, cols], ALU.min)
+            return h2
+
+        wo_w = keep.tile([P, 2 * N], U32, name="wo_w", align_bytes=64)
+        wo_s = keep.tile([P, 2 * N], U8, name="wo_s", align_bytes=64)
+
+        def quantize_wo():
+            raw = ring.tile([P, 2, PACK, N], F32, name="wo_raw", tag="rows_2k", bufs=4)
+            nc.sync.dma_start(raw[:], wo.rearrange("(a p j) n -> p a j n", a=2, j=PACK))
+            grouped = ring.tile([P, 2, N, PACK], BF16, name="wo_grouped", tag="grouped", align_bytes=64)
+            for a in range(2):
+                cast_rows(raw[:, a], grouped[:, a])
+            nc.vector.quantize_mx(
+                out=wo_w[:].bitcast(FP8X4), scales=wo_s[:], in_=grouped[:].rearrange("p a n j -> p (a n j)")
+            )
+
+        z_turned = {}
+        z_w = {}
+        z_s = {}
+
+        def subtract_and_turn(i, neg_page, ref_rows, c):
+            last = i == PAGES - 1
+            a, quarter = divmod(i, PACK)
+            if quarter == 0:
+                z_turned[a, c] = ring.tile([P, 4, 2, P, 2], BF16, name="z_turned", bufs=5)
+            acc = bank(c if last else 5 + c % 2)
+            for src, first in ((ref_rows, True), (neg_page, False)):
+                for b in range(4):
+                    m0 = c * BANK + b * P
+                    nc.tensor.matmul(
+                        acc[:, b * P : (b + 1) * P], lhsT=src[:, m0 : m0 + P], rhs=ident[:], is_transpose=True,
+                        start=(first and b == 0), stop=(not first and b == 3),
+                    )
+            dst = z_turned[a, c][:, :, :, 32 * quarter : 32 * (quarter + 1), :].rearrange("m b u q e -> m u b q e")
+            src = acc[:].rearrange("m (b q u e) -> m u b q e", b=4, u=2, e=2)
+            if last and c % 2 == 1:
+                nc.vector.tensor_scalar_mul(dst, src, -1.0)
+            else:
+                nc.scalar.activation(dst, src, COPY, scale=-1.0)
+
+        def quantize_z(a, c, banks, copy_engines):
+            words = z_turned[a, c][:].rearrange("m b u p e -> m (b u p e)").bitcast(F32)
+            grouped = ring.tile([P, BANK, PACK], BF16, name="z_grouped", tag="grouped", align_bytes=64)
+            grouped_words = grouped[:].rearrange("p m j -> p (m j)").bitcast(F32)
+            for half in range(2):
+                acc = bank(banks[half])
+                for s in range(4):
+                    w0 = (4 * half + s) * P
+                    nc.tensor.transpose(acc[:, s * P : (s + 1) * P], words[:, w0 : w0 + P], ident[:])
+                copy_engines[half](
+                    grouped_words[:, half * BANK : (half + 1) * BANK].rearrange("p (b m u) -> p b m u", b=2, u=2),
+                    acc[:].rearrange("p (b u m) -> p b m u", b=2, u=2),
+                )
+            z_w[a, c] = keep.tile([P, BANK], U32, name="z_w%d_%d" % (a, c), align_bytes=64)
+            z_s[a, c] = keep.tile([P, BANK], U8, name="z_s%d_%d" % (a, c), align_bytes=64)
+            nc.vector.quantize_mx(
+                out=z_w[a, c][:].bitcast(FP8X4), scales=z_s[a, c][:], in_=grouped[:].rearrange("p m j -> p (m j)")
+            )
+
+        def project(c):
+            for half in range(N // P):
+                acc = bank((5, 2)[c % 2] + half)
+                for a in range(2):
+                    n0 = a * N + half * P
+                    nc.tensor.matmul_mx(
+                        acc[:], lhsT=wo_w[:, n0 : n0 + P].bitcast(FP8X4), lhsT_scale=wo_s[:, n0 : n0 + P],
+                        rhs=z_w[a, c][:].bitcast(FP8X4), rhs_scale=z_s[a, c][:], start=(a == 0), stop=(a == 1),
+                    )
+                result = ring.tile([P, BANK], F32, name="result", bufs=4)
+                (nc.vector.tensor_copy if half == 1 and c >= 2 else nc.scalar.copy)(result[:], acc[:])
+                nc.sync.dma_start(out[half * P : (half + 1) * P, c * BANK : (c + 1) * BANK], result[:])
+
+        def turn_page(i):
+            ref_rows = ring.tile([P, T2], F32, name="ref_rows", tag="rows_2k", bufs=4)
+            nc.sync.dma_start(ref_rows[:], ref[i * P : (i + 1) * P, :])
+            for c in range(CHUNKS):
+                subtract_and_turn(i, neg_pages[i], ref_rows, c)
+                if i == PACK - 1:
+                    quantize_z(0, c, (7, 4), (nc.scalar.copy, nc.scalar.copy))
+
+        neg_pages = []
+        h2 = None
+        for i in range(PAGES + 1):
+            if i < PAGES:
+                h1 = liquid(i)
+            if i + 1 < H // W1_COLS:
+                quantize_w1(i + 1)
+            if i > 0:
+                nc.vector.tensor_tensor(neg_pages[i - 1][:].indirect(idx4[:]), h2[:], neg_wg2[:], ALU.mult)
+            if i < PAGES:
+                h2 = vapour(i)
+                neg_pages.append(ring.tile([P, T2], F32, name="neg_page", bufs=3))
+                nc.vector.tensor_tensor(neg_pages[i][:].indirect(idx3[:]), h1[:], neg_wg1[:], ALU.mult)
+            if i == 3:
+                quantize_wo()
+            if i >= 2:
+                turn_page(i - 2)
+        turn_page(PAGES - 1)
+        for c in range(CHUNKS + 1):
+            if c < CHUNKS:
+                quantize_z(1, c, ((7, 4), (0, 1))[c % 2], (nc.scalar.copy, nc.vector.tensor_copy))
+            if c > 0:
+                project(c - 1)

@@ -23,6 +23,8 @@ BANK = 512
 PAGES = H // P
 CHUNKS = T2 // BANK
 W1_COLS = 256
+LAST_CUT = 768
+W3_HEAD = 256
 
 
 def tile_list_two_phase_weave_kernel(
@@ -43,17 +45,17 @@ def tile_list_two_phase_weave_kernel(
             nc.sync.dma_start(t[:], src)
             return t
 
-        def load_words(src, width, name):
-            t = keep.tile([P, width], U32, name=name, align_bytes=64)
+        def load_words(src, name):
+            t = keep.tile([P, src.shape[1]], U32, name=name, align_bytes=64)
             nc.sync.dma_start(t[:].bitcast(I32), src.rearrange("p n t -> p (n t)").bitcast(I32))
             return t
 
-        def load_scales(src, name):
+        def load_scales(src, name, clear_engine, queue):
             passes, width = src.shape[0], src.shape[2]
             t = keep.tile([P, width], U8, name=name, align_bytes=64)
-            nc.vector.memset(t[:].bitcast(I32), 0)
+            clear_engine.memset(t[:].bitcast(I32), 0)
             for q in range(4):
-                nc.scalar.dma_start(
+                queue.dma_start(
                     t[32 * q : 32 * q + 4 * passes, :].bitcast(I32), src[:, 4 * q : 4 * q + 4, :].bitcast(I32)
                 )
             return t
@@ -68,15 +70,19 @@ def tile_list_two_phase_weave_kernel(
                 grouped.rearrange("p (c i) j -> p c j i", i=4), raw.rearrange("p j (c i) -> p c j i", i=4)
             )
 
-        idx = load_list(offs, "idx")
-        tab_s = load_scales(tab_scales, "tab_s")
-        tab_w = load_words(tab_words[0], T, "tab_w")
         idx2 = load_list(offs2, "idx2")
-        tab2_s = load_scales(tab2_scales, "tab2_s")
-        tab2_w = [load_words(tab2_words[a], T, "tab2_w%d" % a) for a in range(2)]
+        tab2_w = [load_words(tab2_words[a], "tab2_w%d" % a) for a in range(2)]
+        tab2_s = load_scales(tab2_scales, "tab2_s", nc.vector, nc.scalar)
+        idx = load_list(offs, "idx")
+        tab_w = load_words(tab_words[0], "tab_w")
+        tab_s = load_scales(tab_scales, "tab_s", nc.vector, nc.scalar)
+        w3_s = load_scales(w3_scales, "w3_s", nc.gpsimd, nc.gpsimd)
+        w2_s = load_scales(w2_scales, "w2_s", nc.vector, nc.scalar)
 
-        v_s = gather(tab_s, idx, U8, "v_s")
+        v2_w = [gather(tab2_w[a], idx2, U32, "v2_w%d" % a) for a in range(2)]
+        v2_s = gather(tab2_s, idx2, U8, "v2_s")
         v_w = gather(tab_w, idx, U32, "v_w")
+        v_s = gather(tab_s, idx, U8, "v_s")
 
         w1_w = [keep.tile([P, W1_COLS], U32, name="w1_w%d" % g, align_bytes=64) for g in range(H // W1_COLS)]
         w1_s = [keep.tile([P, W1_COLS], U8, name="w1_s%d" % g, align_bytes=64) for g in range(H // W1_COLS)]
@@ -92,33 +98,32 @@ def tile_list_two_phase_weave_kernel(
                 out=w1_w[g][:].bitcast(FP8X4), scales=w1_s[g][:], in_=grouped[:].rearrange("p c j -> p (c j)")
             )
 
-        quantize_w1(0)
-        w2_w = keep.tile([P, 2 * H], U8, name="w2_w", align_bytes=64)
-        nc.sync.dma_start(w2_w[:].bitcast(I32), w2_words[0].bitcast(I32))
-        w2_s = load_scales(w2_scales, "w2_s")
-
-        v2_s = gather(tab2_s, idx2, U8, "v2_s")
-        v2_w = [gather(tab2_w[a], idx2, U32, "v2_w%d" % a) for a in range(2)]
-
         def load_negated(src, name):
             t = keep.tile([P, S], F32, name=name)
             nc.sync.dma_start(t[:], src)
             nc.scalar.activation(t[:], t[:], COPY, scale=-1.0)
             return t
 
-        idx3 = load_list(offs3, "idx3")
-        neg_wg1 = load_negated(wg1, "neg_wg1")
-        w3_w = [load_words(w3_words[a], H, "w3_w%d" % a) for a in range(2)]
-        w3_s = load_scales(w3_scales, "w3_s")
+        def load_cap(i):
+            t = ring.tile([P, S], F32, name="cap_rows", tag="rows_1k", bufs=4)
+            nc.sync.dma_start(t[:], cap[i * P : (i + 1) * P, :])
+            return t
+
+        w3_head = [load_words(w3_words[a, :, :W3_HEAD, :], "w3_head%d" % a) for a in range(2)]
+        cap_rows = load_cap(0)
+        quantize_w1(0)
         idx4 = load_list(offs4, "idx4")
         neg_wg2 = load_negated(wg2, "neg_wg2")
+        w2_w = keep.tile([P, 2 * H], U8, name="w2_w", align_bytes=64)
+        nc.sync.dma_start(w2_w[:].bitcast(I32), w2_words[0].bitcast(I32))
+        idx3 = load_list(offs3, "idx3")
+        neg_wg1 = load_negated(wg1, "neg_wg1")
 
         ident = keep.tile([P, P], F32, name="ident")
         make_identity(nc, ident[:])
 
-        def liquid(i):
+        def liquid(i, pieces):
             g, c0 = divmod(i * P, W1_COLS)
-            h1 = ring.tile([P, S], F32, name="h1")
             for half in range(S // BANK):
                 cols = slice(half * BANK, (half + 1) * BANK)
                 second = bank(4)
@@ -129,24 +134,29 @@ def tile_list_two_phase_weave_kernel(
                 )
                 second_sb = ring.tile([P, BANK], F32, name="second_sb", bufs=4)
                 nc.scalar.copy(second_sb[:], second[:])
-                first = bank(half)
+                first = bank(2 * (i % 2) + half)
                 nc.tensor.matmul_mx(
                     first[:], lhsT=w1_w[g][:, c0 : c0 + P].bitcast(FP8X4), lhsT_scale=w1_s[g][:, c0 : c0 + P],
                     rhs=v_w[:, cols].bitcast(FP8X4), rhs_scale=v_s[:, cols], start=True, stop=True,
                 )
-                nc.vector.tensor_tensor(h1[:, cols], first[:], second_sb[:], ALU.max)
-            return h1
+                for dst, j0, j1 in pieces:
+                    lo, hi = max(j0, cols.start), min(j1, cols.stop)
+                    if lo < hi:
+                        part = slice(lo - cols.start, hi - cols.start)
+                        nc.vector.tensor_tensor(dst[:, lo - j0 : hi - j0], first[:, part], second_sb[:, part], ALU.max)
 
-        def vapour(i):
-            cap_rows = ring.tile([P, S], F32, name="cap_rows", tag="rows_1k", bufs=4)
-            nc.sync.dma_start(cap_rows[:], cap[i * P : (i + 1) * P, :])
-            h2 = ring.tile([P, S], F32, name="h2")
+        def vapour(i, cap_rows):
+            h2 = ring.tile([P, S], F32, name="h2", bufs=1)
             for half in range(S // BANK):
                 cols = slice(half * BANK, (half + 1) * BANK)
-                acc = bank(2 + half)
+                acc = bank(2 * (i % 2) + half)
                 for a in range(2):
+                    if i * P < W3_HEAD:
+                        w3_cols = w3_head[a][:, i * P : (i + 1) * P]
+                    else:
+                        w3_cols = w3_rest[a][:, i * P - W3_HEAD : (i + 1) * P - W3_HEAD]
                     nc.tensor.matmul_mx(
-                        acc[:], lhsT=w3_w[a][:, i * P : (i + 1) * P].bitcast(FP8X4),
+                        acc[:], lhsT=w3_cols.bitcast(FP8X4),
                         lhsT_scale=w3_s[4 * a :, i * P : (i + 1) * P],
                         rhs=v2_w[a][:, cols].bitcast(FP8X4), rhs_scale=v2_s[4 * a :, cols],
                         start=(a == 0), stop=(a == 1),
@@ -168,6 +178,7 @@ def tile_list_two_phase_weave_kernel(
             )
 
         z_turned = {}
+        z_grouped = {}
         z_w = {}
         z_s = {}
 
@@ -191,7 +202,7 @@ def tile_list_two_phase_weave_kernel(
             else:
                 nc.scalar.activation(dst, src, COPY, scale=-1.0)
 
-        def quantize_z(a, c, banks, copy_engines):
+        def regroup_z(a, c, banks, copy_engines):
             words = z_turned[a, c][:].rearrange("m b u p e -> m (b u p e)").bitcast(F32)
             grouped = ring.tile([P, BANK, PACK], BF16, name="z_grouped", tag="grouped", align_bytes=64)
             grouped_words = grouped[:].rearrange("p m j -> p (m j)").bitcast(F32)
@@ -204,20 +215,26 @@ def tile_list_two_phase_weave_kernel(
                     grouped_words[:, half * BANK : (half + 1) * BANK].rearrange("p (b m u) -> p b m u", b=2, u=2),
                     acc[:].rearrange("p (b u m) -> p b m u", b=2, u=2),
                 )
-            z_w[a, c] = keep.tile([P, BANK], U32, name="z_w%d_%d" % (a, c), align_bytes=64)
+            z_grouped[a, c] = grouped
+
+        def quantize_z(a, c, codes=None):
+            grouped = z_grouped[a, c]
+            if codes is None:
+                codes = keep.tile([P, BANK], U32, name="z_w%d_%d" % (a, c), align_bytes=64)[:]
+            z_w[a, c] = codes
             z_s[a, c] = keep.tile([P, BANK], U8, name="z_s%d_%d" % (a, c), align_bytes=64)
             nc.vector.quantize_mx(
-                out=z_w[a, c][:].bitcast(FP8X4), scales=z_s[a, c][:], in_=grouped[:].rearrange("p m j -> p (m j)")
+                out=z_w[a, c].bitcast(FP8X4), scales=z_s[a, c][:], in_=grouped[:].rearrange("p m j -> p (m j)")
             )
 
         def project(c):
             for half in range(N // P):
-                acc = bank((5, 2)[c % 2] + half)
+                acc = bank(((5, 6), (7, 4))[c % 2][half])
                 for a in range(2):
                     n0 = a * N + half * P
                     nc.tensor.matmul_mx(
                         acc[:], lhsT=wo_w[:, n0 : n0 + P].bitcast(FP8X4), lhsT_scale=wo_s[:, n0 : n0 + P],
-                        rhs=z_w[a, c][:].bitcast(FP8X4), rhs_scale=z_s[a, c][:], start=(a == 0), stop=(a == 1),
+                        rhs=z_w[a, c].bitcast(FP8X4), rhs_scale=z_s[a, c][:], start=(a == 0), stop=(a == 1),
                     )
                 result = ring.tile([P, BANK], F32, name="result", bufs=4)
                 (nc.vector.tensor_copy if half == 1 and c >= 2 else nc.scalar.copy)(result[:], acc[:])
@@ -228,29 +245,48 @@ def tile_list_two_phase_weave_kernel(
             nc.sync.dma_start(ref_rows[:], ref[i * P : (i + 1) * P, :])
             for c in range(CHUNKS):
                 subtract_and_turn(i, neg_pages[i], ref_rows, c)
-                if i == PACK - 1:
-                    quantize_z(0, c, (7, 4), (nc.scalar.copy, nc.scalar.copy))
+            if i == PACK - 1:
+                for c in (2, 3, 0, 1):
+                    regroup_z(0, c, (7, 4), (nc.scalar.copy, nc.scalar.copy))
+                    if c >= 2:
+                        quantize_z(0, c)
+
+        def scatter(page, lst, values, weights, j0, j1):
+            nc.vector.tensor_tensor(
+                page[:].indirect(lst[:, j0 // 16 : j1 // 16]), values[:], weights[:, j0:j1], ALU.mult
+            )
 
         neg_pages = []
-        h2 = None
-        for i in range(PAGES + 1):
-            if i < PAGES:
-                h1 = liquid(i)
+        w3_rest = []
+        h2 = vapour(0, cap_rows)
+        for i in range(PAGES):
+            last = i == PAGES - 1
+            neg_pages.append(ring.tile([P, T2], F32, name="neg_page", bufs=4))
+            scatter(neg_pages[i], idx4, h2, neg_wg2, 0, S)
+            cut = LAST_CUT if last else S
+            pieces = [(ring.tile([P, cut], F32, name="h1", bufs=1, align_bytes=64), 0, cut)]
+            if last:
+                pieces.append((ring.tile([P, S - cut], F32, name="h1_end", bufs=1), cut, S))
+            liquid(i, pieces)
+            if not last:
+                h2 = vapour(i + 1, load_cap(i + 1))
+            scatter(neg_pages[i], idx3, pieces[0][0], neg_wg1, 0, cut)
+            if i == 0:
+                w3_rest.extend([load_words(w3_words[a, :, W3_HEAD:, :], "w3_rest%d" % a) for a in range(2)])
             if i + 1 < H // W1_COLS:
                 quantize_w1(i + 1)
-            if i > 0:
-                nc.vector.tensor_tensor(neg_pages[i - 1][:].indirect(idx4[:]), h2[:], neg_wg2[:], ALU.mult)
-            if i < PAGES:
-                h2 = vapour(i)
-                neg_pages.append(ring.tile([P, T2], F32, name="neg_page", bufs=3))
-                nc.vector.tensor_tensor(neg_pages[i][:].indirect(idx3[:]), h1[:], neg_wg1[:], ALU.mult)
             if i == 3:
                 quantize_wo()
-            if i >= 2:
-                turn_page(i - 2)
+            if i >= 1:
+                turn_page(i - 1)
+        late_codes = ring.tile([P, 2, BANK], U32, name="late_codes", tag="h1", bufs=1, align_bytes=64)
+        for c in range(2):
+            quantize_z(0, c, late_codes[:, c, :])
+        scatter(neg_pages[-1], idx3, pieces[1][0], neg_wg1, LAST_CUT, S)
         turn_page(PAGES - 1)
         for c in range(CHUNKS + 1):
             if c < CHUNKS:
-                quantize_z(1, c, ((7, 4), (0, 1))[c % 2], (nc.scalar.copy, nc.vector.tensor_copy))
+                regroup_z(1, c, ((0, 1), (2, 3))[c % 2], (nc.scalar.copy, nc.vector.tensor_copy))
+                quantize_z(1, c)
             if c > 0:
                 project(c - 1)

@@ -16,14 +16,16 @@ FP8X4 = mybir.dt.float8_e4m3fn_x4
 FP4X4 = mybir.dt.float4_e2m1fn_x4
 ALU = mybir.AluOpType
 COPY = mybir.ActivationFunctionType.Copy
+RELU = mybir.ActivationFunctionType.Relu
 
 P = 128
 PACK = 4
 BANK = 512
 PAGES = H // P
-CHUNKS = T2 // BANK
+HALF = T2 // 2
+COLS = 256
+PACKED = COLS + COLS // 4
 W1_COLS = 256
-LAST_CUT = 768
 W3_HEAD = 256
 
 
@@ -40,13 +42,22 @@ def tile_list_two_phase_weave_kernel(
         def bank(k):
             return psum.tile([P, BANK], F32, name="bank%d" % k)
 
+        turns = []
+
+        def next_bank():
+            turns.append(0)
+            return bank(2 + len(turns) % 6)
+
         def load_list(src, name):
             t = keep.tile([P, S // 16], U16, name=name)
             nc.sync.dma_start(t[:], src)
             return t
 
-        def load_words(src, name):
-            t = keep.tile([P, src.shape[1]], U32, name=name, align_bytes=64)
+        def load_words(src, name, window=False):
+            if window:
+                t = ring.tile([P, T], U32, name=name, tag="page", bufs=3, align_bytes=64)
+            else:
+                t = keep.tile([P, src.shape[1]], U32, name=name, align_bytes=64)
             nc.sync.dma_start(t[:].bitcast(I32), src.rearrange("p n t -> p (n t)").bitcast(I32))
             return t
 
@@ -71,10 +82,10 @@ def tile_list_two_phase_weave_kernel(
             )
 
         idx2 = load_list(offs2, "idx2")
-        tab2_w = [load_words(tab2_words[a], "tab2_w%d" % a) for a in range(2)]
+        tab2_w = [load_words(tab2_words[a], "tab2_w%d" % a, True) for a in range(2)]
         tab2_s = load_scales(tab2_scales, "tab2_s", nc.vector, nc.scalar)
         idx = load_list(offs, "idx")
-        tab_w = load_words(tab_words[0], "tab_w")
+        tab_w = load_words(tab_words[0], "tab_w", True)
         tab_s = load_scales(tab_scales, "tab_s", nc.vector, nc.scalar)
         w3_s = load_scales(w3_scales, "w3_s", nc.gpsimd, nc.gpsimd)
         w2_s = load_scales(w2_scales, "w2_s", nc.vector, nc.scalar)
@@ -88,11 +99,11 @@ def tile_list_two_phase_weave_kernel(
         w1_s = [keep.tile([P, W1_COLS], U8, name="w1_s%d" % g, align_bytes=64) for g in range(H // W1_COLS)]
 
         def quantize_w1(g):
-            raw = ring.tile([P, PACK, W1_COLS], F32, name="w1_raw", tag="rows_1k", bufs=4)
+            raw = ring.tile([P, PACK, W1_COLS], F32, name="w1_raw", bufs=2)
             nc.sync.dma_start(
                 raw[:], w1[:, g * W1_COLS : (g + 1) * W1_COLS].rearrange("(p j) c -> p j c", j=PACK)
             )
-            grouped = ring.tile([P, W1_COLS, PACK], BF16, name="w1_grouped", align_bytes=64)
+            grouped = ring.tile([P, W1_COLS, PACK], BF16, name="w1_grouped", tag="w1_grouped", align_bytes=64)
             cast_rows(raw[:], grouped[:])
             nc.vector.quantize_mx(
                 out=w1_w[g][:].bitcast(FP8X4), scales=w1_s[g][:], in_=grouped[:].rearrange("p c j -> p (c j)")
@@ -105,51 +116,61 @@ def tile_list_two_phase_weave_kernel(
             return t
 
         def load_cap(i):
-            t = ring.tile([P, S], F32, name="cap_rows", tag="rows_1k", bufs=4)
+            t = ring.tile([P, S], F32, name="cap_rows", bufs=3)
             nc.sync.dma_start(t[:], cap[i * P : (i + 1) * P, :])
             return t
 
         w3_head = [load_words(w3_words[a, :, :W3_HEAD, :], "w3_head%d" % a) for a in range(2)]
         cap_rows = load_cap(0)
         quantize_w1(0)
-        idx4 = load_list(offs4, "idx4")
-        neg_wg2 = load_negated(wg2, "neg_wg2")
         w2_w = keep.tile([P, 2 * H], U8, name="w2_w", align_bytes=64)
         nc.sync.dma_start(w2_w[:].bitcast(I32), w2_words[0].bitcast(I32))
         idx3 = load_list(offs3, "idx3")
         neg_wg1 = load_negated(wg1, "neg_wg1")
+        idx4 = load_list(offs4, "idx4")
+        wg2_sb = keep.tile([P, S], F32, name="wg2_sb")
+        nc.sync.dma_start(wg2_sb[:], wg2)
 
         ident = keep.tile([P, P], F32, name="ident")
         make_identity(nc, ident[:])
 
-        def liquid(i, pieces):
+        def liquid(i):
             g, c0 = divmod(i * P, W1_COLS)
+            sums = []
             for half in range(S // BANK):
                 cols = slice(half * BANK, (half + 1) * BANK)
-                second = bank(4)
+                second = next_bank()
                 nc.tensor.matmul_mx(
                     second[:], lhsT=w2_w[:, 2 * i * P : 2 * (i + 1) * P].bitcast(FP4X4),
                     lhsT_scale=w2_s[:, i * P : (i + 1) * P],
                     rhs=v_w[:, cols].bitcast(FP8X4), rhs_scale=v_s[:, cols], start=True, stop=True,
                 )
-                second_sb = ring.tile([P, BANK], F32, name="second_sb", bufs=4)
+                if i == PAGES - 1 and half == 1:
+                    second_sb = ring.tile([P, BANK], F32, name="second_end", bufs=1, align_bytes=64)
+                else:
+                    second_sb = ring.tile([P, BANK], F32, name="second_sb", bufs=3)
                 nc.scalar.copy(second_sb[:], second[:])
-                first = bank(2 * (i % 2) + half)
+                first = bank(half)
                 nc.tensor.matmul_mx(
                     first[:], lhsT=w1_w[g][:, c0 : c0 + P].bitcast(FP8X4), lhsT_scale=w1_s[g][:, c0 : c0 + P],
                     rhs=v_w[:, cols].bitcast(FP8X4), rhs_scale=v_s[:, cols], start=True, stop=True,
                 )
-                for dst, j0, j1 in pieces:
-                    lo, hi = max(j0, cols.start), min(j1, cols.stop)
-                    if lo < hi:
-                        part = slice(lo - cols.start, hi - cols.start)
-                        nc.vector.tensor_tensor(dst[:, lo - j0 : hi - j0], first[:, part], second_sb[:, part], ALU.max)
+                sums.append((first, second_sb))
+            return sums
+
+        def turn_sum(acc, sources):
+            for k, src in enumerate(sources):
+                for b in range(4):
+                    nc.tensor.matmul(
+                        acc[:, b * P : (b + 1) * P], lhsT=src[:, b * P : (b + 1) * P], rhs=ident[:], is_transpose=True,
+                        start=(k == 0 and b == 0), stop=(k == len(sources) - 1 and b == 3),
+                    )
 
         def vapour(i, cap_rows):
-            h2 = ring.tile([P, S], F32, name="h2", bufs=1)
+            neg_h2 = ring.tile([P, S], F32, name="neg_h2", bufs=2)
             for half in range(S // BANK):
                 cols = slice(half * BANK, (half + 1) * BANK)
-                acc = bank(2 * (i % 2) + half)
+                acc = next_bank()
                 for a in range(2):
                     if i * P < W3_HEAD:
                         w3_cols = w3_head[a][:, i * P : (i + 1) * P]
@@ -161,116 +182,174 @@ def tile_list_two_phase_weave_kernel(
                         rhs=v2_w[a][:, cols].bitcast(FP8X4), rhs_scale=v2_s[4 * a :, cols],
                         start=(a == 0), stop=(a == 1),
                     )
-                nc.vector.tensor_tensor(h2[:, cols], acc[:], cap_rows[:, cols], ALU.min)
-            return h2
+                neg_sum = ring.tile([P, BANK], F32, name="neg_sum", bufs=2)
+                nc.scalar.activation(neg_sum[:], acc[:], COPY, scale=-1.0)
+                room = next_bank()
+                turn_sum(room, [cap_rows[:, cols], neg_sum])
+                excess_t = ring.tile([P, BANK], F32, name="excess_t", tag="turned_a", bufs=4)
+                nc.scalar.activation(excess_t[:], room[:], RELU, scale=-1.0)
+                plain = next_bank()
+                turn_sum(plain, [neg_sum])
+                neg_sum_t = ring.tile([P, BANK], F32, name="neg_sum_t", tag="turned_b", bufs=4)
+                nc.scalar.copy(neg_sum_t[:], plain[:])
+                bounded = next_bank()
+                turn_sum(bounded, [neg_sum_t, excess_t])
+                nc.scalar.copy(neg_h2[:, cols], bounded[:])
+            return neg_h2
 
-        wo_w = keep.tile([P, 2 * N], U32, name="wo_w", align_bytes=64)
-        wo_s = keep.tile([P, 2 * N], U8, name="wo_s", align_bytes=64)
+        def packed_tile(name, cleared, parts=1):
+            t = keep.tile([P, parts * PACKED], U32, name=name, align_bytes=64)
+            if cleared:
+                for h in range(parts):
+                    nc.gpsimd.memset(part(t, h)[:, COLS:].bitcast(I32), 0)
+            return t
+
+        def part(t, h):
+            return t[:, h * PACKED : (h + 1) * PACKED]
+
+        def codes_of(t, c0=0, c1=COLS):
+            return t[:, c0:c1].bitcast(FP8X4)
+
+        def scales_of(t, c0=0, c1=COLS):
+            return t[:, COLS:].bitcast(U8)[:, c0:c1]
+
+        def quadrant(t, q):
+            return t[32 * q : 32 * (q + 1), :].bitcast(I32)
+
+        def place(i, c):
+            a, quarter = divmod(i, PACK)
+            if a == 1 and quarter == 3:
+                return c
+            if a == 1 and quarter == c:
+                return 3
+            return quarter
+
+        wo_q = {1: packed_tile("wo_q1", True)}
+        wo_grouped = {}
+        wo_last = [packed_tile("wo_last%d" % c, False) for c in range(3)] + [wo_q[1]]
+        page_q = [packed_tile("page_q%d" % k, True, 2) for k in range(2)]
+        z_q = {(a, c): packed_tile("z_q%d%d" % (a, c), False, 2) for a in range(2) for c in range(4)}
+
+        def quantize_wo_pass(a):
+            nc.vector.quantize_mx(
+                out=codes_of(wo_q[a]), scales=scales_of(wo_q[a]), in_=wo_grouped[a][:].rearrange("p n j -> p (n j)")
+            )
 
         def quantize_wo():
             raw = ring.tile([P, 2, PACK, N], F32, name="wo_raw", tag="rows_2k", bufs=4)
             nc.sync.dma_start(raw[:], wo.rearrange("(a p j) n -> p a j n", a=2, j=PACK))
-            grouped = ring.tile([P, 2, N, PACK], BF16, name="wo_grouped", tag="grouped", align_bytes=64)
             for a in range(2):
-                cast_rows(raw[:, a], grouped[:, a])
-            nc.vector.quantize_mx(
-                out=wo_w[:].bitcast(FP8X4), scales=wo_s[:], in_=grouped[:].rearrange("p a n j -> p (a n j)")
-            )
+                wo_grouped[a] = keep.tile([P, N, PACK], BF16, name="wo_grouped%d" % a, align_bytes=64)
+                cast_rows(raw[:, a], wo_grouped[a][:])
+            quantize_wo_pass(1)
+            for c in range(3):
+                for quarter in range(PACK):
+                    nc.sync.dma_start(quadrant(wo_last[c], place(PACK + quarter, c)), quadrant(wo_q[1], quarter))
 
-        z_turned = {}
-        z_grouped = {}
-        z_w = {}
-        z_s = {}
+        def turn_onto(acc, src, h, b, first):
+            for c in range(4):
+                m0 = h * HALF + c * COLS + b * P
+                nc.tensor.matmul(
+                    acc[:, c * P : (c + 1) * P], lhsT=src[:, m0 : m0 + P], rhs=ident[:], is_transpose=True,
+                    start=(first and c == 0), stop=(not first and c == 3),
+                )
 
-        def subtract_and_turn(i, neg_page, ref_rows, c):
-            last = i == PAGES - 1
-            a, quarter = divmod(i, PACK)
-            if quarter == 0:
-                z_turned[a, c] = ring.tile([P, 4, 2, P, 2], BF16, name="z_turned", bufs=5)
-            acc = bank(c if last else 5 + c % 2)
-            for src, first in ((ref_rows, True), (neg_page, False)):
-                for b in range(4):
-                    m0 = c * BANK + b * P
-                    nc.tensor.matmul(
-                        acc[:, b * P : (b + 1) * P], lhsT=src[:, m0 : m0 + P], rhs=ident[:], is_transpose=True,
-                        start=(first and b == 0), stop=(not first and b == 3),
-                    )
-            dst = z_turned[a, c][:, :, :, 32 * quarter : 32 * (quarter + 1), :].rearrange("m b u q e -> m u b q e")
-            src = acc[:].rearrange("m (b q u e) -> m u b q e", b=4, u=2, e=2)
-            if last and c % 2 == 1:
+        def round_z(acc, turned, b, on_vector):
+            dst = turned[:, b, :].rearrange("m (u cq e) -> m u cq e", u=2, e=2)
+            src = acc[:].rearrange("m (cq u e) -> m u cq e", u=2, e=2)
+            if on_vector:
                 nc.vector.tensor_scalar_mul(dst, src, -1.0)
             else:
                 nc.scalar.activation(dst, src, COPY, scale=-1.0)
 
-        def regroup_z(a, c, banks, copy_engines):
-            words = z_turned[a, c][:].rearrange("m b u p e -> m (b u p e)").bitcast(F32)
-            grouped = ring.tile([P, BANK, PACK], BF16, name="z_grouped", tag="grouped", align_bytes=64)
-            grouped_words = grouped[:].rearrange("p m j -> p (m j)").bitcast(F32)
-            for half in range(2):
-                acc = bank(banks[half])
-                for s in range(4):
-                    w0 = (4 * half + s) * P
-                    nc.tensor.transpose(acc[:, s * P : (s + 1) * P], words[:, w0 : w0 + P], ident[:])
-                copy_engines[half](
-                    grouped_words[:, half * BANK : (half + 1) * BANK].rearrange("p (b m u) -> p b m u", b=2, u=2),
-                    acc[:].rearrange("p (b u m) -> p b m u", b=2, u=2),
-                )
-            z_grouped[a, c] = grouped
-
-        def quantize_z(a, c, codes=None):
-            grouped = z_grouped[a, c]
-            if codes is None:
-                codes = keep.tile([P, BANK], U32, name="z_w%d_%d" % (a, c), align_bytes=64)[:]
-            z_w[a, c] = codes
-            z_s[a, c] = keep.tile([P, BANK], U8, name="z_s%d_%d" % (a, c), align_bytes=64)
-            nc.vector.quantize_mx(
-                out=z_w[a, c].bitcast(FP8X4), scales=z_s[a, c][:], in_=grouped[:].rearrange("p m j -> p (m j)")
+        def turn_back(turned, acc, grouped):
+            words = turned[:].rearrange("m b x -> m (b x)").bitcast(F32)
+            for s in range(4):
+                nc.tensor.transpose(acc[:, s * P : (s + 1) * P], words[:, s * P : (s + 1) * P], ident[:])
+            nc.scalar.copy(
+                grouped.bitcast(F32).rearrange("p (b m u) -> p b m u", b=2, u=2),
+                acc[:].rearrange("p (b u m) -> p b m u", b=2, u=2),
             )
 
-        def project(c):
-            for half in range(N // P):
-                acc = bank(((5, 6), (7, 4))[c % 2][half])
-                for a in range(2):
-                    n0 = a * N + half * P
-                    nc.tensor.matmul_mx(
-                        acc[:], lhsT=wo_w[:, n0 : n0 + P].bitcast(FP8X4), lhsT_scale=wo_s[:, n0 : n0 + P],
-                        rhs=z_w[a, c].bitcast(FP8X4), rhs_scale=z_s[a, c][:], start=(a == 0), stop=(a == 1),
-                    )
-                result = ring.tile([P, BANK], F32, name="result", bufs=4)
-                (nc.vector.tensor_copy if half == 1 and c >= 2 else nc.scalar.copy)(result[:], acc[:])
-                nc.sync.dma_start(out[half * P : (half + 1) * P, c * BANK : (c + 1) * BANK], result[:])
+        def quantize_z(i, h, grouped):
+            packed = part(page_q[i % 2], h)
+            nc.vector.quantize_mx(out=codes_of(packed), scales=scales_of(packed), in_=grouped)
+
+        def load_ref(i):
+            t = ring.tile([P, T2], F32, name="ref_rows", tag="rows_2k", bufs=4)
+            nc.sync.dma_start(t[:], ref[i * P : (i + 1) * P, :])
+            return t
 
         def turn_page(i):
-            ref_rows = ring.tile([P, T2], F32, name="ref_rows", tag="rows_2k", bufs=4)
-            nc.sync.dma_start(ref_rows[:], ref[i * P : (i + 1) * P, :])
-            for c in range(CHUNKS):
-                subtract_and_turn(i, neg_pages[i], ref_rows, c)
-            if i == PACK - 1:
-                for c in (2, 3, 0, 1):
-                    regroup_z(0, c, (7, 4), (nc.scalar.copy, nc.scalar.copy))
-                    if c >= 2:
-                        quantize_z(0, c)
+            ref_rows = load_ref(i)
+            turned = []
+            for h in range(2):
+                turned.append(ring.tile([P, 2, BANK], BF16, name="z_turned", bufs=4))
+                for b in range(2):
+                    acc = next_bank()
+                    turn_onto(acc, ref_rows, h, b, True)
+                    turn_onto(acc, neg_pages[i], h, b, False)
+                    round_z(acc, turned[h], b, False)
+            grouped = ring.tile([P, 2 * HALF], BF16, name="z_grouped", tag="slot%d" % ((i + 2) % 3), bufs=1, align_bytes=64)
+            for h in range(2):
+                turn_back(turned[h], next_bank(), grouped[:, h * HALF : (h + 1) * HALF])
+            for h in range(2):
+                quantize_z(i, h, grouped[:, h * HALF : (h + 1) * HALF])
+            for c in range(4):
+                nc.sync.dma_start(quadrant(z_q[i // PACK, c], place(i, c)), quadrant(page_q[i % 2], c))
+
+        def project(acc, a, h, pair, half):
+            for s in range(2):
+                c = 2 * pair + s
+                wo_cols = wo_last[c] if a == 1 else wo_q[0]
+                nc.tensor.matmul_mx(
+                    acc[:, s * COLS : (s + 1) * COLS],
+                    lhsT=codes_of(wo_cols, half * P, (half + 1) * P),
+                    lhsT_scale=scales_of(wo_cols, half * P, (half + 1) * P),
+                    rhs=codes_of(part(z_q[a, c], h)), rhs_scale=scales_of(part(z_q[a, c], h)),
+                    start=(a == 0 and s == 0), stop=(a == 1 and s == 1),
+                )
+
+        def store(acc, h, pair, half, copy):
+            result = ring.tile([P, BANK], F32, name="result", tag=("turned_a", "turned_b")[half], bufs=4)
+            copy(result[:], acc[:])
+            m0 = h * HALF + pair * BANK
+            nc.sync.dma_start(out[half * P : (half + 1) * P, m0 : m0 + BANK], result[:])
 
         def scatter(page, lst, values, weights, j0, j1):
             nc.vector.tensor_tensor(
-                page[:].indirect(lst[:, j0 // 16 : j1 // 16]), values[:], weights[:, j0:j1], ALU.mult
+                page[:].indirect(lst[:, j0 // 16 : j1 // 16]), values, weights[:, j0:j1], ALU.mult
             )
 
         neg_pages = []
         w3_rest = []
-        h2 = vapour(0, cap_rows)
+        def greater(i):
+            h1 = ring.tile([P, S], F32, name="h1", tag="slot%d" % (i % 3), bufs=1, align_bytes=64)
+            for half, (first, second_sb) in enumerate(liquid(i)):
+                if i == PAGES - 1 and half == 1:
+                    held.append((first, second_sb))
+                else:
+                    nc.vector.tensor_tensor(h1[:, half * BANK : (half + 1) * BANK], first[:], second_sb[:], ALU.max)
+            return h1
+
+        held = []
+        h1 = {0: greater(0)}
+        neg_h2 = vapour(0, cap_rows)
         for i in range(PAGES):
             last = i == PAGES - 1
-            neg_pages.append(ring.tile([P, T2], F32, name="neg_page", bufs=4))
-            scatter(neg_pages[i], idx4, h2, neg_wg2, 0, S)
-            cut = LAST_CUT if last else S
-            pieces = [(ring.tile([P, cut], F32, name="h1", bufs=1, align_bytes=64), 0, cut)]
-            if last:
-                pieces.append((ring.tile([P, S - cut], F32, name="h1_end", bufs=1), cut, S))
-            liquid(i, pieces)
+            neg_pages.append(ring.tile([P, T2], F32, name="neg_page", tag="page", bufs=3, align_bytes=64))
+            if i < 2:
+                scatter(neg_pages[i], idx3, h1[i][:], neg_wg1, 0, S)
+            if i == 0:
+                h1[1] = greater(1)
+            if i >= 2:
+                h1[i] = greater(i)
+            scatter(neg_pages[i], idx4, neg_h2[:], wg2_sb, 0, S)
             if not last:
-                h2 = vapour(i + 1, load_cap(i + 1))
-            scatter(neg_pages[i], idx3, pieces[0][0], neg_wg1, 0, cut)
+                neg_h2 = vapour(i + 1, load_cap(i + 1))
+            if i >= 2:
+                cut = BANK if last else S
+                scatter(neg_pages[i], idx3, h1[i][:, :cut], neg_wg1, 0, cut)
             if i == 0:
                 w3_rest.extend([load_words(w3_words[a, :, W3_HEAD:, :], "w3_rest%d" % a) for a in range(2)])
             if i + 1 < H // W1_COLS:
@@ -279,14 +358,37 @@ def tile_list_two_phase_weave_kernel(
                 quantize_wo()
             if i >= 1:
                 turn_page(i - 1)
-        late_codes = ring.tile([P, 2, BANK], U32, name="late_codes", tag="h1", bufs=1, align_bytes=64)
-        for c in range(2):
-            quantize_z(0, c, late_codes[:, c, :])
-        scatter(neg_pages[-1], idx3, pieces[1][0], neg_wg1, LAST_CUT, S)
-        turn_page(PAGES - 1)
-        for c in range(CHUNKS + 1):
-            if c < CHUNKS:
-                regroup_z(1, c, ((0, 1), (2, 3))[c % 2], (nc.scalar.copy, nc.vector.tensor_copy))
-                quantize_z(1, c)
-            if c > 0:
-                project(c - 1)
+
+        i = PAGES - 1
+        h1_end = ring.tile([P, BANK], F32, name="h1_end", tag="slot%d" % ((i + 1) % 3), bufs=1, align_bytes=64)
+        nc.vector.tensor_tensor(h1_end[:], held[0][0][:], held[0][1][:], ALU.max)
+        wo_q[0] = ring.tile([P, PACKED], U32, name="wo_q0", tag="second_end", bufs=1, align_bytes=64)
+        quantize_wo_pass(0)
+        scatter(neg_pages[i], idx3, h1_end[:], neg_wg1, BANK, S)
+        blocks = [(h, b) for h in range(2) for b in range(2)]
+        tiles = [(pair, half) for pair in range(2) for half in range(2)]
+        ref_rows = load_ref(i)
+        sums = [bank(k) for k in range(4)]
+        for k, (h, b) in enumerate(blocks):
+            turn_onto(sums[k], ref_rows, h, b, True)
+        accs = {}
+        for k, (pair, half) in enumerate(tiles):
+            accs[0, k] = bank(4 + k)
+            project(accs[0, k], 0, 0, pair, half)
+        for h in range(2):
+            turned = ring.tile([P, 2, BANK], BF16, name="z_turned", bufs=4)
+            for b in range(2):
+                turn_onto(sums[2 * h + b], neg_pages[i], h, b, False)
+                round_z(sums[2 * h + b], turned, b, b == 1)
+            grouped = ring.tile([P, HALF], BF16, name="z_grouped_last", bufs=2, align_bytes=64)
+            turn_back(turned, bank(h), grouped[:])
+            if h == 1:
+                for k, (pair, half) in enumerate(tiles):
+                    accs[1, k] = bank((2, 3, 0, 1)[k])
+                    project(accs[1, k], 0, 1, pair, half)
+            quantize_z(i, h, grouped[:])
+            for c in range(4):
+                nc.vector.tensor_copy(quadrant(part(z_q[1, c], h), c), quadrant(part(page_q[i % 2], h), c))
+            for k, (pair, half) in enumerate(tiles):
+                project(accs[h, k], 1, h, pair, half)
+                store(accs[h, k], h, pair, half, nc.vector.tensor_copy if h == 1 and k != 1 else nc.scalar.copy)

@@ -122,41 +122,45 @@ def tile_list_two_phase_weave_kernel(
 
         w3_head = [load_words(w3_words[a, :, :W3_HEAD, :], "w3_head%d" % a) for a in range(2)]
         cap_rows = load_cap(0)
+        neg_cap = cap_rows
+        nc.scalar.activation(neg_cap[:], cap_rows[:], COPY, scale=-1.0)
         quantize_w1(0)
+        idx4 = load_list(offs4, "idx4")
+        wg2_sb = keep.tile([P, S], F32, name="wg2_sb")
+        nc.sync.dma_start(wg2_sb[:], wg2)
         w2_w = keep.tile([P, 2 * H], U8, name="w2_w", align_bytes=64)
         nc.sync.dma_start(w2_w[:].bitcast(I32), w2_words[0].bitcast(I32))
         idx3 = load_list(offs3, "idx3")
         neg_wg1 = load_negated(wg1, "neg_wg1")
-        idx4 = load_list(offs4, "idx4")
-        wg2_sb = keep.tile([P, S], F32, name="wg2_sb")
-        nc.sync.dma_start(wg2_sb[:], wg2)
 
         ident = keep.tile([P, P], F32, name="ident")
         make_identity(nc, ident[:])
 
-        def liquid(i):
+        firsts = {}
+        seconds = {}
+
+        def liquid_second(i, half):
+            cols = slice(half * BANK, (half + 1) * BANK)
+            acc = bank(half)
+            nc.tensor.matmul_mx(
+                acc[:], lhsT=w2_w[:, 2 * i * P : 2 * (i + 1) * P].bitcast(FP4X4),
+                lhsT_scale=w2_s[:, i * P : (i + 1) * P],
+                rhs=v_w[:, cols].bitcast(FP8X4), rhs_scale=v_s[:, cols], start=True, stop=True,
+            )
+            if i == PAGES - 1 and half == 1:
+                seconds[i, half] = ring.tile([P, BANK], F32, name="second_end", bufs=1, align_bytes=64)
+            else:
+                seconds[i, half] = ring.tile([P, BANK], F32, name="second_sb", bufs=3)
+            nc.scalar.copy(seconds[i, half][:], acc[:])
+
+        def liquid_first(i, half):
             g, c0 = divmod(i * P, W1_COLS)
-            sums = []
-            for half in range(S // BANK):
-                cols = slice(half * BANK, (half + 1) * BANK)
-                second = next_bank()
-                nc.tensor.matmul_mx(
-                    second[:], lhsT=w2_w[:, 2 * i * P : 2 * (i + 1) * P].bitcast(FP4X4),
-                    lhsT_scale=w2_s[:, i * P : (i + 1) * P],
-                    rhs=v_w[:, cols].bitcast(FP8X4), rhs_scale=v_s[:, cols], start=True, stop=True,
-                )
-                if i == PAGES - 1 and half == 1:
-                    second_sb = ring.tile([P, BANK], F32, name="second_end", bufs=1, align_bytes=64)
-                else:
-                    second_sb = ring.tile([P, BANK], F32, name="second_sb", bufs=3)
-                nc.scalar.copy(second_sb[:], second[:])
-                first = bank(half)
-                nc.tensor.matmul_mx(
-                    first[:], lhsT=w1_w[g][:, c0 : c0 + P].bitcast(FP8X4), lhsT_scale=w1_s[g][:, c0 : c0 + P],
-                    rhs=v_w[:, cols].bitcast(FP8X4), rhs_scale=v_s[:, cols], start=True, stop=True,
-                )
-                sums.append((first, second_sb))
-            return sums
+            cols = slice(half * BANK, (half + 1) * BANK)
+            firsts[i, half] = bank(half)
+            nc.tensor.matmul_mx(
+                firsts[i, half][:], lhsT=w1_w[g][:, c0 : c0 + P].bitcast(FP8X4), lhsT_scale=w1_s[g][:, c0 : c0 + P],
+                rhs=v_w[:, cols].bitcast(FP8X4), rhs_scale=v_s[:, cols], start=True, stop=True,
+            )
 
         def turn_sum(acc, sources):
             for k, src in enumerate(sources):
@@ -166,36 +170,51 @@ def tile_list_two_phase_weave_kernel(
                         start=(k == 0 and b == 0), stop=(k == len(sources) - 1 and b == 3),
                     )
 
-        def vapour(i, cap_rows):
-            neg_h2 = ring.tile([P, S], F32, name="neg_h2", bufs=2)
-            for half in range(S // BANK):
-                cols = slice(half * BANK, (half + 1) * BANK)
-                acc = next_bank()
-                for a in range(2):
-                    if i * P < W3_HEAD:
-                        w3_cols = w3_head[a][:, i * P : (i + 1) * P]
-                    else:
-                        w3_cols = w3_rest[a][:, i * P - W3_HEAD : (i + 1) * P - W3_HEAD]
-                    nc.tensor.matmul_mx(
-                        acc[:], lhsT=w3_cols.bitcast(FP8X4),
-                        lhsT_scale=w3_s[4 * a :, i * P : (i + 1) * P],
-                        rhs=v2_w[a][:, cols].bitcast(FP8X4), rhs_scale=v2_s[4 * a :, cols],
-                        start=(a == 0), stop=(a == 1),
-                    )
-                neg_sum = ring.tile([P, BANK], F32, name="neg_sum", bufs=2)
-                nc.scalar.activation(neg_sum[:], acc[:], COPY, scale=-1.0)
-                room = next_bank()
-                turn_sum(room, [cap_rows[:, cols], neg_sum])
-                excess_t = ring.tile([P, BANK], F32, name="excess_t", tag="turned_a", bufs=4)
-                nc.scalar.activation(excess_t[:], room[:], RELU, scale=-1.0)
-                plain = next_bank()
-                turn_sum(plain, [neg_sum])
-                neg_sum_t = ring.tile([P, BANK], F32, name="neg_sum_t", tag="turned_b", bufs=4)
-                nc.scalar.copy(neg_sum_t[:], plain[:])
-                bounded = next_bank()
-                turn_sum(bounded, [neg_sum_t, excess_t])
-                nc.scalar.copy(neg_h2[:, cols], bounded[:])
-            return neg_h2
+        neg_h2 = {}
+        caps = {0: cap_rows}
+        neg_sum = {}
+        turned_parts = {}
+
+        def vapour_product(i, half):
+            cols = slice(half * BANK, (half + 1) * BANK)
+            if half == 0:
+                neg_h2[i] = ring.tile([P, S], F32, name="neg_h2", bufs=3)
+                if i > 0:
+                    caps[i] = load_cap(i)
+            acc = next_bank()
+            for a in range(2):
+                if i * P < W3_HEAD:
+                    w3_cols = w3_head[a][:, i * P : (i + 1) * P]
+                else:
+                    w3_cols = w3_rest[a][:, i * P - W3_HEAD : (i + 1) * P - W3_HEAD]
+                nc.tensor.matmul_mx(
+                    acc[:], lhsT=w3_cols.bitcast(FP8X4),
+                    lhsT_scale=w3_s[4 * a :, i * P : (i + 1) * P],
+                    rhs=v2_w[a][:, cols].bitcast(FP8X4), rhs_scale=v2_s[4 * a :, cols],
+                    start=(a == 0), stop=(a == 1),
+                )
+            if i == 0:
+                nc.vector.scalar_tensor_tensor(neg_h2[i][:, cols], acc[:], -1.0, neg_cap[:, cols], ALU.mult, ALU.max)
+            else:
+                neg_sum[i, half] = ring.tile([P, BANK], F32, name="neg_sum", bufs=2)
+                nc.scalar.activation(neg_sum[i, half][:], acc[:], COPY, scale=-1.0)
+
+        def vapour_turn(i, half):
+            cols = slice(half * BANK, (half + 1) * BANK)
+            room = next_bank()
+            turn_sum(room, [caps[i][:, cols], neg_sum[i, half]])
+            excess_t = ring.tile([P, BANK], F32, name="excess_t", tag="turned_a", bufs=4)
+            nc.scalar.activation(excess_t[:], room[:], RELU, scale=-1.0)
+            plain = next_bank()
+            turn_sum(plain, [neg_sum[i, half]])
+            neg_sum_t = ring.tile([P, BANK], F32, name="neg_sum_t", tag="turned_b", bufs=4)
+            nc.scalar.copy(neg_sum_t[:], plain[:])
+            turned_parts[i, half] = [neg_sum_t, excess_t]
+
+        def vapour_join(i, half):
+            bounded = next_bank()
+            turn_sum(bounded, turned_parts[i, half])
+            nc.scalar.copy(neg_h2[i][:, half * BANK : (half + 1) * BANK], bounded[:])
 
         def packed_tile(name, cleared, parts=1):
             t = keep.tile([P, parts * PACKED], U32, name=name, align_bytes=64)
@@ -224,10 +243,10 @@ def tile_list_two_phase_weave_kernel(
                 return 3
             return quarter
 
-        wo_q = {1: packed_tile("wo_q1", True)}
+        wo_q = {1: packed_tile("wo_q1", False)}
         wo_grouped = {}
         wo_last = [packed_tile("wo_last%d" % c, False) for c in range(3)] + [wo_q[1]]
-        page_q = [packed_tile("page_q%d" % k, True, 2) for k in range(2)]
+        page_q = {PAGES - 1: packed_tile("page_q_last", False, 2)}
         z_q = {(a, c): packed_tile("z_q%d%d" % (a, c), False, 2) for a in range(2) for c in range(4)}
 
         def quantize_wo_pass(a):
@@ -272,7 +291,7 @@ def tile_list_two_phase_weave_kernel(
             )
 
         def quantize_z(i, h, grouped):
-            packed = part(page_q[i % 2], h)
+            packed = part(page_q[i], h)
             nc.vector.quantize_mx(out=codes_of(packed), scales=scales_of(packed), in_=grouped)
 
         def load_ref(i):
@@ -280,23 +299,50 @@ def tile_list_two_phase_weave_kernel(
             nc.sync.dma_start(t[:], ref[i * P : (i + 1) * P, :])
             return t
 
-        def turn_page(i):
-            ref_rows = load_ref(i)
-            turned = []
+        refs = {}
+        z_turned = {}
+        z_grouped = {}
+
+        def depart(i, h, b, acc):
+            if h == 0 and b == 0:
+                refs[i] = load_ref(i)
+            if b == 0:
+                z_turned[i, h] = ring.tile([P, 2, BANK], BF16, name="z_turned", bufs=4)
+            turn_onto(acc, refs[i], h, b, True)
+            turn_onto(acc, neg_pages[i], h, b, False)
+            round_z(acc, z_turned[i, h], b, False)
+
+        def regroup(i, h):
+            if h == 0:
+                z_grouped[i] = ring.tile(
+                    [P, 2 * HALF], BF16, name="z_grouped", tag="slot%d" % ((i + 3) % 4), bufs=1, align_bytes=64
+                )
+            turn_back(z_turned[i, h], next_bank(), z_grouped[i][:, h * HALF : (h + 1) * HALF])
+
+        def quantize_page(i):
+            page_q[i] = ring.tile([P, 2 * PACKED], U32, name="page_q", tag="slot%d" % ((i + 1) % 4), bufs=1, align_bytes=64)
             for h in range(2):
-                turned.append(ring.tile([P, 2, BANK], BF16, name="z_turned", bufs=4))
-                for b in range(2):
-                    acc = next_bank()
-                    turn_onto(acc, ref_rows, h, b, True)
-                    turn_onto(acc, neg_pages[i], h, b, False)
-                    round_z(acc, turned[h], b, False)
-            grouped = ring.tile([P, 2 * HALF], BF16, name="z_grouped", tag="slot%d" % ((i + 2) % 3), bufs=1, align_bytes=64)
-            for h in range(2):
-                turn_back(turned[h], next_bank(), grouped[:, h * HALF : (h + 1) * HALF])
-            for h in range(2):
-                quantize_z(i, h, grouped[:, h * HALF : (h + 1) * HALF])
+                quantize_z(i, h, z_grouped[i][:, h * HALF : (h + 1) * HALF])
             for c in range(4):
-                nc.sync.dma_start(quadrant(z_q[i // PACK, c], place(i, c)), quadrant(page_q[i % 2], c))
+                nc.sync.dma_start(quadrant(z_q[i // PACK, c], place(i, c)), quadrant(page_q[i], c))
+
+        def side_work(r):
+            liq, dep, vap = r + 1, r - 1, r + 2
+            steps = [
+                (liquid_second, liq, 0), (liquid_second, liq, 1),
+                (depart, dep, 0, 0, 0), (depart, dep, 0, 1, 1),
+                (liquid_first, liq, 0), (liquid_first, liq, 1),
+                (depart, dep, 1, 0, None), (vapour_product, vap, 0), (depart, dep, 1, 1, None), (vapour_turn, vap, 0),
+                (regroup, dep, 0), (vapour_product, vap, 1), (vapour_join, vap, 0), (regroup, dep, 1),
+                (vapour_turn, vap, 1), (vapour_join, vap, 1),
+            ]
+            for step in steps:
+                if 0 <= step[1] < PAGES:
+                    if step[0] is depart:
+                        held_bank = step[4] is not None and r < PAGES - 1
+                        depart(*step[1:4], bank(step[4]) if held_bank else next_bank())
+                    else:
+                        step[0](*step[1:])
 
         def project(acc, a, h, pair, half):
             for s in range(2):
@@ -322,46 +368,39 @@ def tile_list_two_phase_weave_kernel(
             )
 
         neg_pages = []
-        w3_rest = []
-        def greater(i):
-            h1 = ring.tile([P, S], F32, name="h1", tag="slot%d" % (i % 3), bufs=1, align_bytes=64)
-            for half, (first, second_sb) in enumerate(liquid(i)):
-                if i == PAGES - 1 and half == 1:
-                    held.append((first, second_sb))
-                else:
-                    nc.vector.tensor_tensor(h1[:, half * BANK : (half + 1) * BANK], first[:], second_sb[:], ALU.max)
-            return h1
-
-        held = []
-        h1 = {0: greater(0)}
-        neg_h2 = vapour(0, cap_rows)
+        for half in range(2):
+            vapour_product(0, half)
+        for half in range(2):
+            liquid_second(0, half)
+            liquid_first(0, half)
+        for half in range(2):
+            vapour_product(1, half)
+            vapour_turn(1, half)
+        for half in range(2):
+            vapour_join(1, half)
+        w3_rest = [load_words(w3_words[a, :, W3_HEAD:, :], "w3_rest%d" % a) for a in range(2)]
         for i in range(PAGES):
             last = i == PAGES - 1
             neg_pages.append(ring.tile([P, T2], F32, name="neg_page", tag="page", bufs=3, align_bytes=64))
-            if i < 2:
-                scatter(neg_pages[i], idx3, h1[i][:], neg_wg1, 0, S)
-            if i == 0:
-                h1[1] = greater(1)
-            if i >= 2:
-                h1[i] = greater(i)
-            scatter(neg_pages[i], idx4, neg_h2[:], wg2_sb, 0, S)
-            if not last:
-                neg_h2 = vapour(i + 1, load_cap(i + 1))
-            if i >= 2:
-                cut = BANK if last else S
-                scatter(neg_pages[i], idx3, h1[i][:, :cut], neg_wg1, 0, cut)
-            if i == 0:
-                w3_rest.extend([load_words(w3_words[a, :, W3_HEAD:, :], "w3_rest%d" % a) for a in range(2)])
+            h1 = ring.tile([P, S], F32, name="h1", tag="slot%d" % (i % 4), bufs=1, align_bytes=64)
+            for half in range(1 if last else 2):
+                nc.vector.tensor_tensor(
+                    h1[:, half * BANK : (half + 1) * BANK], firsts[i, half][:], seconds[i, half][:], ALU.max
+                )
+            scatter(neg_pages[i], idx4, neg_h2[i][:], wg2_sb, 0, S)
+            cut = BANK if last else S
+            scatter(neg_pages[i], idx3, h1[:, :cut], neg_wg1, 0, cut)
             if i + 1 < H // W1_COLS:
                 quantize_w1(i + 1)
             if i == 3:
                 quantize_wo()
+            side_work(i)
             if i >= 1:
-                turn_page(i - 1)
+                quantize_page(i - 1)
 
         i = PAGES - 1
-        h1_end = ring.tile([P, BANK], F32, name="h1_end", tag="slot%d" % ((i + 1) % 3), bufs=1, align_bytes=64)
-        nc.vector.tensor_tensor(h1_end[:], held[0][0][:], held[0][1][:], ALU.max)
+        h1_end = ring.tile([P, BANK], F32, name="h1_end", tag="slot%d" % ((i + 2) % 4), bufs=1, align_bytes=64)
+        nc.vector.tensor_tensor(h1_end[:], firsts[i, 1][:], seconds[i, 1][:], ALU.max)
         wo_q[0] = ring.tile([P, PACKED], U32, name="wo_q0", tag="second_end", bufs=1, align_bytes=64)
         quantize_wo_pass(0)
         scatter(neg_pages[i], idx3, h1_end[:], neg_wg1, BANK, S)
@@ -388,7 +427,7 @@ def tile_list_two_phase_weave_kernel(
                     project(accs[1, k], 0, 1, pair, half)
             quantize_z(i, h, grouped[:])
             for c in range(4):
-                nc.vector.tensor_copy(quadrant(part(z_q[1, c], h), c), quadrant(part(page_q[i % 2], h), c))
+                nc.vector.tensor_copy(quadrant(part(z_q[1, c], h), c), quadrant(part(page_q[i], h), c))
             for k, (pair, half) in enumerate(tiles):
                 project(accs[h, k], 1, h, pair, half)
                 store(accs[h, k], h, pair, half, nc.vector.tensor_copy if h == 1 and k != 1 else nc.scalar.copy)

@@ -27,6 +27,7 @@ COLS = 256
 PACKED = COLS + COLS // 4
 W1_COLS = 256
 W3_HEAD = 256
+TURNED_PAGES = (2, 4, 5, 6)
 
 
 def tile_list_two_phase_weave_kernel(
@@ -104,7 +105,12 @@ def tile_list_two_phase_weave_kernel(
                 raw[:], w1[:, g * W1_COLS : (g + 1) * W1_COLS].rearrange("(p j) c -> p j c", j=PACK)
             )
             grouped = ring.tile([P, W1_COLS, PACK], BF16, name="w1_grouped", tag="w1_grouped", align_bytes=64)
-            cast_rows(raw[:], grouped[:])
+            for k in range(W1_COLS // P):
+                sign = -1.0 if g * W1_COLS // P + k in TURNED_PAGES else 1.0
+                nc.scalar.activation(
+                    grouped[:, k * P : (k + 1) * P, :].rearrange("p (c i) j -> p c j i", i=4),
+                    raw[:, :, k * P : (k + 1) * P].rearrange("p j (c i) -> p c j i", i=4), COPY, scale=sign,
+                )
             nc.vector.quantize_mx(
                 out=w1_w[g][:].bitcast(FP8X4), scales=w1_s[g][:], in_=grouped[:].rearrange("p c j -> p (c j)")
             )
@@ -150,7 +156,7 @@ def tile_list_two_phase_weave_kernel(
             if i == PAGES - 1 and half == 1:
                 seconds[i, half] = ring.tile([P, BANK], F32, name="second_end", bufs=1, align_bytes=64)
             else:
-                seconds[i, half] = ring.tile([P, BANK], F32, name="second_sb", bufs=3)
+                seconds[i, half] = ring.tile([P, BANK], F32, name="second_sb", bufs=4)
             nc.scalar.copy(seconds[i, half][:], acc[:])
 
         def liquid_first(i, half):
@@ -169,6 +175,45 @@ def tile_list_two_phase_weave_kernel(
                         acc[:, b * P : (b + 1) * P], lhsT=src[:, b * P : (b + 1) * P], rhs=ident[:], is_transpose=True,
                         start=(k == 0 and b == 0), stop=(k == len(sources) - 1 and b == 3),
                     )
+
+        h1 = {}
+        liquid_parts = {}
+
+        def h1_tile(i):
+            h1[i] = ring.tile([P, S], F32, name="h1", tag="slot%d" % (i % 4), bufs=1, align_bytes=64)
+
+        def cells_times(acc, half, operands):
+            for b in range(4):
+                cells = slice(half * BANK + b * P, half * BANK + (b + 1) * P)
+                for k, (words, scales) in enumerate(operands):
+                    nc.tensor.matmul_mx(
+                        acc[:, b * P : (b + 1) * P], lhsT=v_w[:, cells].bitcast(FP8X4), lhsT_scale=v_s[:, cells],
+                        rhs=words, rhs_scale=scales, start=(k == 0), stop=(k == len(operands) - 1),
+                    )
+
+        def neg_w1_cols(i):
+            g, c0 = divmod(i * P, W1_COLS)
+            return w1_w[g][:, c0 : c0 + P].bitcast(FP8X4), w1_s[g][:, c0 : c0 + P]
+
+        def liquid_lead(i, half, acc):
+            w2_cols = (w2_w[:, 2 * i * P : 2 * (i + 1) * P].bitcast(FP4X4), w2_s[:, i * P : (i + 1) * P])
+            cells_times(acc, half, [neg_w1_cols(i), w2_cols])
+            lead_t = ring.tile([P, BANK], F32, name="lead_t", tag="second_sb", bufs=4)
+            nc.scalar.activation(lead_t[:], acc[:], RELU)
+            liquid_parts[i, half] = [lead_t]
+
+        def liquid_base(i, half, acc):
+            cells_times(acc, half, [neg_w1_cols(i)])
+            base_t = ring.tile([P, BANK], F32, name="base_t", tag="second_sb", bufs=4)
+            nc.scalar.activation(base_t[:], acc[:], COPY, scale=-1.0)
+            liquid_parts[i, half].append(base_t)
+
+        def liquid_join(i, half):
+            if half == 0:
+                h1_tile(i)
+            both = next_bank()
+            turn_sum(both, liquid_parts[i, half])
+            nc.scalar.copy(h1[i][:, half * BANK : (half + 1) * BANK], both[:])
 
         neg_h2 = {}
         caps = {0: cap_rows}
@@ -328,21 +373,43 @@ def tile_list_two_phase_weave_kernel(
 
         def side_work(r):
             liq, dep, vap = r + 1, r - 1, r + 2
-            steps = [
-                (liquid_second, liq, 0), (liquid_second, liq, 1),
-                (depart, dep, 0, 0, 0), (depart, dep, 0, 1, 1),
-                (liquid_first, liq, 0), (liquid_first, liq, 1),
-                (depart, dep, 1, 0, None), (vapour_product, vap, 0), (depart, dep, 1, 1, None), (vapour_turn, vap, 0),
-                (regroup, dep, 0), (vapour_product, vap, 1), (vapour_join, vap, 0), (regroup, dep, 1),
-                (vapour_turn, vap, 1), (vapour_join, vap, 1),
-            ]
-            for step in steps:
-                if 0 <= step[1] < PAGES:
-                    if step[0] is depart:
-                        held_bank = step[4] is not None and r < PAGES - 1
-                        depart(*step[1:4], bank(step[4]) if held_bank else next_bank())
-                    else:
-                        step[0](*step[1:])
+            has_liq, has_dep, has_vap = liq < PAGES, dep >= 0, vap < PAGES
+            turned = liq in TURNED_PAGES
+            for half in range(2):
+                if turned:
+                    liquid_lead(liq, half, bank(half))
+                elif has_liq:
+                    liquid_second(liq, half)
+            for b in range(2):
+                if has_dep:
+                    depart(dep, 0, b, bank(b) if has_liq else next_bank())
+                if turned:
+                    liquid_base(liq, b, bank(b))
+                elif has_liq:
+                    liquid_first(liq, b)
+            if has_dep:
+                depart(dep, 1, 0, next_bank())
+            if has_vap:
+                vapour_product(vap, 0)
+            if turned:
+                liquid_join(liq, 0)
+            if has_dep:
+                depart(dep, 1, 1, next_bank())
+            if has_vap:
+                vapour_turn(vap, 0)
+            if turned:
+                liquid_join(liq, 1)
+            if has_vap:
+                vapour_product(vap, 1)
+            if has_dep:
+                regroup(dep, 0)
+            if has_vap:
+                vapour_join(vap, 0)
+            if has_dep:
+                regroup(dep, 1)
+            if has_vap:
+                vapour_turn(vap, 1)
+                vapour_join(vap, 1)
 
         def project(acc, a, h, pair, half):
             for s in range(2):
@@ -382,14 +449,15 @@ def tile_list_two_phase_weave_kernel(
         for i in range(PAGES):
             last = i == PAGES - 1
             neg_pages.append(ring.tile([P, T2], F32, name="neg_page", tag="page", bufs=3, align_bytes=64))
-            h1 = ring.tile([P, S], F32, name="h1", tag="slot%d" % (i % 4), bufs=1, align_bytes=64)
-            for half in range(1 if last else 2):
-                nc.vector.tensor_tensor(
-                    h1[:, half * BANK : (half + 1) * BANK], firsts[i, half][:], seconds[i, half][:], ALU.max
-                )
+            if i not in TURNED_PAGES:
+                h1_tile(i)
+                for half in range(1 if last else 2):
+                    nc.vector.tensor_tensor(
+                        h1[i][:, half * BANK : (half + 1) * BANK], firsts[i, half][:], seconds[i, half][:], ALU.max
+                    )
             scatter(neg_pages[i], idx4, neg_h2[i][:], wg2_sb, 0, S)
             cut = BANK if last else S
-            scatter(neg_pages[i], idx3, h1[:, :cut], neg_wg1, 0, cut)
+            scatter(neg_pages[i], idx3, h1[i][:, :cut], neg_wg1, 0, cut)
             if i + 1 < H // W1_COLS:
                 quantize_w1(i + 1)
             if i == 3:

@@ -27,7 +27,9 @@ COLS = 256
 PACKED = COLS + COLS // 4
 W1_COLS = 256
 W3_HEAD = 256
-TURNED_PAGES = (2, 4, 5, 6)
+LAST_CUT = 640
+TURNED_PAGES = (1, 2, 3, 4)
+COPIED_PAGES = (5, 6)
 
 
 def tile_list_two_phase_weave_kernel(
@@ -44,10 +46,11 @@ def tile_list_two_phase_weave_kernel(
             return psum.tile([P, BANK], F32, name="bank%d" % k)
 
         turns = []
+        turning = list(range(2, 8))
 
         def next_bank():
             turns.append(0)
-            return bank(2 + len(turns) % 6)
+            return bank(turning[len(turns) % len(turning)])
 
         def load_list(src, name):
             t = keep.tile([P, S // 16], U16, name=name)
@@ -147,7 +150,7 @@ def tile_list_two_phase_weave_kernel(
 
         def liquid_second(i, half):
             cols = slice(half * BANK, (half + 1) * BANK)
-            acc = bank(half)
+            acc = next_bank()
             nc.tensor.matmul_mx(
                 acc[:], lhsT=w2_w[:, 2 * i * P : 2 * (i + 1) * P].bitcast(FP4X4),
                 lhsT_scale=w2_s[:, i * P : (i + 1) * P],
@@ -156,13 +159,13 @@ def tile_list_two_phase_weave_kernel(
             if i == PAGES - 1 and half == 1:
                 seconds[i, half] = ring.tile([P, BANK], F32, name="second_end", bufs=1, align_bytes=64)
             else:
-                seconds[i, half] = ring.tile([P, BANK], F32, name="second_sb", bufs=4)
-            nc.scalar.copy(seconds[i, half][:], acc[:])
+                seconds[i, half] = ring.tile([P, BANK], F32, name="second_sb", bufs=4, align_bytes=64)
+            nc.scalar.activation(seconds[i, half][:], acc[:], COPY, scale=-1.0 if i in COPIED_PAGES else 1.0)
 
         def liquid_first(i, half):
             g, c0 = divmod(i * P, W1_COLS)
             cols = slice(half * BANK, (half + 1) * BANK)
-            firsts[i, half] = bank(half)
+            firsts[i, half] = next_bank() if i in COPIED_PAGES else bank(half)
             nc.tensor.matmul_mx(
                 firsts[i, half][:], lhsT=w1_w[g][:, c0 : c0 + P].bitcast(FP8X4), lhsT_scale=w1_s[g][:, c0 : c0 + P],
                 rhs=v_w[:, cols].bitcast(FP8X4), rhs_scale=v_s[:, cols], start=True, stop=True,
@@ -198,13 +201,13 @@ def tile_list_two_phase_weave_kernel(
         def liquid_lead(i, half, acc):
             w2_cols = (w2_w[:, 2 * i * P : 2 * (i + 1) * P].bitcast(FP4X4), w2_s[:, i * P : (i + 1) * P])
             cells_times(acc, half, [neg_w1_cols(i), w2_cols])
-            lead_t = ring.tile([P, BANK], F32, name="lead_t", tag="second_sb", bufs=4)
+            lead_t = ring.tile([P, BANK], F32, name="lead_t", tag="second_sb", bufs=4, align_bytes=64)
             nc.scalar.activation(lead_t[:], acc[:], RELU)
             liquid_parts[i, half] = [lead_t]
 
         def liquid_base(i, half, acc):
             cells_times(acc, half, [neg_w1_cols(i)])
-            base_t = ring.tile([P, BANK], F32, name="base_t", tag="second_sb", bufs=4)
+            base_t = ring.tile([P, BANK], F32, name="base_t", tag="second_sb", bufs=4, align_bytes=64)
             nc.scalar.activation(base_t[:], acc[:], COPY, scale=-1.0)
             liquid_parts[i, half].append(base_t)
 
@@ -241,20 +244,22 @@ def tile_list_two_phase_weave_kernel(
             if i == 0:
                 nc.vector.scalar_tensor_tensor(neg_h2[i][:, cols], acc[:], -1.0, neg_cap[:, cols], ALU.mult, ALU.max)
             else:
-                neg_sum[i, half] = ring.tile([P, BANK], F32, name="neg_sum", bufs=2)
+                neg_sum[i, half] = ring.tile([P, BANK], F32, name="neg_sum", bufs=4)
                 nc.scalar.activation(neg_sum[i, half][:], acc[:], COPY, scale=-1.0)
 
         def vapour_turn(i, half):
-            cols = slice(half * BANK, (half + 1) * BANK)
+            turned_parts[i, half] = bound_turn(caps[i][:, half * BANK : (half + 1) * BANK], neg_sum[i, half])
+
+        def bound_turn(bound, neg_value):
             room = next_bank()
-            turn_sum(room, [caps[i][:, cols], neg_sum[i, half]])
+            turn_sum(room, [bound, neg_value])
             excess_t = ring.tile([P, BANK], F32, name="excess_t", tag="turned_a", bufs=4)
             nc.scalar.activation(excess_t[:], room[:], RELU, scale=-1.0)
             plain = next_bank()
-            turn_sum(plain, [neg_sum[i, half]])
+            turn_sum(plain, [neg_value])
             neg_sum_t = ring.tile([P, BANK], F32, name="neg_sum_t", tag="turned_b", bufs=4)
             nc.scalar.copy(neg_sum_t[:], plain[:])
-            turned_parts[i, half] = [neg_sum_t, excess_t]
+            return [neg_sum_t, excess_t]
 
         def vapour_join(i, half):
             bounded = next_bank()
@@ -360,7 +365,7 @@ def tile_list_two_phase_weave_kernel(
         def regroup(i, h):
             if h == 0:
                 z_grouped[i] = ring.tile(
-                    [P, 2 * HALF], BF16, name="z_grouped", tag="slot%d" % ((i + 3) % 4), bufs=1, align_bytes=64
+                    [P, 2 * HALF], BF16, name="z_grouped", tag="grouped%d" % (i % 2), bufs=1, align_bytes=64
                 )
             turn_back(z_turned[i, h], next_bank(), z_grouped[i][:, h * HALF : (h + 1) * HALF])
 
@@ -371,33 +376,40 @@ def tile_list_two_phase_weave_kernel(
             for c in range(4):
                 nc.sync.dma_start(quadrant(z_q[i // PACK, c], place(i, c)), quadrant(page_q[i], c))
 
+        def liquid_turn(i, half):
+            first_sb = ring.tile([P, BANK], F32, name="first_sb", tag="neg_sum", bufs=4)
+            nc.scalar.copy(first_sb[:], firsts[i, half][:])
+            liquid_parts[i, half] = bound_turn(seconds[i, half], first_sb)
+
         def side_work(r):
             liq, dep, vap = r + 1, r - 1, r + 2
             has_liq, has_dep, has_vap = liq < PAGES, dep >= 0, vap < PAGES
             turned = liq in TURNED_PAGES
             for half in range(2):
                 if turned:
-                    liquid_lead(liq, half, bank(half))
+                    liquid_lead(liq, half, next_bank())
                 elif has_liq:
                     liquid_second(liq, half)
             for b in range(2):
                 if has_dep:
-                    depart(dep, 0, b, bank(b) if has_liq else next_bank())
+                    depart(dep, 0, b, next_bank())
                 if turned:
-                    liquid_base(liq, b, bank(b))
+                    liquid_base(liq, b, next_bank())
                 elif has_liq:
                     liquid_first(liq, b)
+                if liq in COPIED_PAGES:
+                    liquid_turn(liq, b)
             if has_dep:
                 depart(dep, 1, 0, next_bank())
             if has_vap:
                 vapour_product(vap, 0)
-            if turned:
+            if turned or liq in COPIED_PAGES:
                 liquid_join(liq, 0)
             if has_dep:
                 depart(dep, 1, 1, next_bank())
             if has_vap:
                 vapour_turn(vap, 0)
-            if turned:
+            if turned or liq in COPIED_PAGES:
                 liquid_join(liq, 1)
             if has_vap:
                 vapour_product(vap, 1)
@@ -449,29 +461,36 @@ def tile_list_two_phase_weave_kernel(
         for i in range(PAGES):
             last = i == PAGES - 1
             neg_pages.append(ring.tile([P, T2], F32, name="neg_page", tag="page", bufs=3, align_bytes=64))
-            if i not in TURNED_PAGES:
+            if i not in TURNED_PAGES + COPIED_PAGES:
                 h1_tile(i)
-                for half in range(1 if last else 2):
+                for half in range(2):
+                    width = LAST_CUT - BANK if last and half == 1 else BANK
                     nc.vector.tensor_tensor(
-                        h1[i][:, half * BANK : (half + 1) * BANK], firsts[i, half][:], seconds[i, half][:], ALU.max
+                        h1[i][:, half * BANK : half * BANK + width], firsts[i, half][:, :width],
+                        seconds[i, half][:, :width], ALU.max,
                     )
             scatter(neg_pages[i], idx4, neg_h2[i][:], wg2_sb, 0, S)
-            cut = BANK if last else S
+            cut = LAST_CUT if last else S
             scatter(neg_pages[i], idx3, h1[i][:, :cut], neg_wg1, 0, cut)
             if i + 1 < H // W1_COLS:
                 quantize_w1(i + 1)
             if i == 3:
                 quantize_wo()
+            if i == 1:
+                turning.extend([0, 1])
+            if i == PAGES - 2:
+                turning.remove(0)
+                turning.remove(1)
             side_work(i)
             if i >= 1:
                 quantize_page(i - 1)
 
         i = PAGES - 1
-        h1_end = ring.tile([P, BANK], F32, name="h1_end", tag="slot%d" % ((i + 2) % 4), bufs=1, align_bytes=64)
-        nc.vector.tensor_tensor(h1_end[:], firsts[i, 1][:], seconds[i, 1][:], ALU.max)
+        h1_end = ring.tile([P, S - LAST_CUT], F32, name="h1_end", tag="grouped%d" % ((i - 1) % 2), bufs=1, align_bytes=64)
+        nc.vector.tensor_tensor(h1_end[:], firsts[i, 1][:, LAST_CUT - BANK :], seconds[i, 1][:, LAST_CUT - BANK :], ALU.max)
         wo_q[0] = ring.tile([P, PACKED], U32, name="wo_q0", tag="second_end", bufs=1, align_bytes=64)
         quantize_wo_pass(0)
-        scatter(neg_pages[i], idx3, h1_end[:], neg_wg1, BANK, S)
+        scatter(neg_pages[i], idx3, h1_end[:], neg_wg1, LAST_CUT, S)
         blocks = [(h, b) for h in range(2) for b in range(2)]
         tiles = [(pair, half) for pair in range(2) for half in range(2)]
         ref_rows = load_ref(i)
@@ -487,7 +506,7 @@ def tile_list_two_phase_weave_kernel(
             for b in range(2):
                 turn_onto(sums[2 * h + b], neg_pages[i], h, b, False)
                 round_z(sums[2 * h + b], turned, b, b == 1)
-            grouped = ring.tile([P, HALF], BF16, name="z_grouped_last", bufs=2, align_bytes=64)
+            grouped = ring.tile([P, HALF], BF16, name="z_grouped_last", tag="second_sb", bufs=4, align_bytes=64)
             turn_back(turned, bank(h), grouped[:])
             if h == 1:
                 for k, (pair, half) in enumerate(tiles):

@@ -20,16 +20,20 @@ RELU = mybir.ActivationFunctionType.Relu
 
 P = 128
 PACK = 4
+QUAD = P // PACK
 BANK = 512
+BANKS = 8
 PAGES = H // P
+LAST = PAGES - 1
 HALF = T2 // 2
 COLS = 256
-PACKED = COLS + COLS // 4
-W1_COLS = 256
-W3_HEAD = 256
+PACKED = COLS + COLS // PACK
+HEAD_PAGES = 2
+W_COLS = HEAD_PAGES * P
+TURNED_PAGES = 4
 LAST_CUT = 640
-TURNED_PAGES = (1, 2, 3, 4)
-COPIED_PAGES = (5, 6)
+HELD_BANK = 1
+H1_SLOTS = 4
 
 
 def tile_list_two_phase_weave_kernel(
@@ -40,38 +44,38 @@ def tile_list_two_phase_weave_kernel(
     with ExitStack() as ctx:
         keep = ctx.enter_context(tc.tile_pool(name="keep", bufs=1))
         ring = ctx.enter_context(tc.tile_pool(name="ring", bufs=2))
+        placed = ctx.enter_context(tc.tile_pool(name="placed", bufs=1))
         psum = ctx.enter_context(tc.psum_pool(name="psum", bufs=1))
 
         def bank(k):
             return psum.tile([P, BANK], F32, name="bank%d" % k)
 
-        turns = []
-        turning = list(range(2, 8))
+        taken = []
+        turning = list(range(BANKS))
 
         def next_bank():
-            turns.append(0)
-            return bank(turning[len(turns) % len(turning)])
+            taken.append(0)
+            return bank(turning[len(taken) % len(turning)])
 
         def load_list(src, name):
             t = keep.tile([P, S // 16], U16, name=name)
             nc.sync.dma_start(t[:], src)
             return t
 
-        def load_words(src, name, window=False):
-            if window:
-                t = ring.tile([P, T], U32, name=name, tag="page", bufs=3, align_bytes=64)
-            else:
-                t = keep.tile([P, src.shape[1]], U32, name=name, align_bytes=64)
+        def load_words(t, src):
             nc.sync.dma_start(t[:].bitcast(I32), src.rearrange("p n t -> p (n t)").bitcast(I32))
             return t
+
+        def page_bytes(dtype, name):
+            return ring.tile([P, T2], dtype, name=name, tag="page", bufs=3, align_bytes=64)
 
         def load_scales(src, name, clear_engine, queue):
             passes, width = src.shape[0], src.shape[2]
             t = keep.tile([P, width], U8, name=name, align_bytes=64)
             clear_engine.memset(t[:].bitcast(I32), 0)
-            for q in range(4):
+            for q in range(PACK):
                 queue.dma_start(
-                    t[32 * q : 32 * q + 4 * passes, :].bitcast(I32), src[:, 4 * q : 4 * q + 4, :].bitcast(I32)
+                    t[QUAD * q : QUAD * q + 4 * passes, :].bitcast(I32), src[:, 4 * q : 4 * q + 4, :].bitcast(I32)
                 )
             return t
 
@@ -80,48 +84,27 @@ def tile_list_two_phase_weave_kernel(
             nc.vector.tensor_copy(t[:], window[:].indirect(lst[:]))
             return t
 
-        def cast_rows(raw, grouped):
-            nc.scalar.copy(
-                grouped.rearrange("p (c i) j -> p c j i", i=4), raw.rearrange("p j (c i) -> p c j i", i=4)
+        def round_rows(raw, grouped, sign):
+            nc.scalar.activation(
+                grouped.rearrange("p (c i) j -> p c j i", i=4), raw.rearrange("p j (c i) -> p c j i", i=4),
+                COPY, scale=sign,
             )
 
-        idx2 = load_list(offs2, "idx2")
-        tab2_w = [load_words(tab2_words[a], "tab2_w%d" % a, True) for a in range(2)]
-        tab2_s = load_scales(tab2_scales, "tab2_s", nc.vector, nc.scalar)
-        idx = load_list(offs, "idx")
-        tab_w = load_words(tab_words[0], "tab_w", True)
-        tab_s = load_scales(tab_scales, "tab_s", nc.vector, nc.scalar)
-        w3_s = load_scales(w3_scales, "w3_s", nc.gpsimd, nc.gpsimd)
-        w2_s = load_scales(w2_scales, "w2_s", nc.vector, nc.scalar)
-
-        v2_w = [gather(tab2_w[a], idx2, U32, "v2_w%d" % a) for a in range(2)]
-        v2_s = gather(tab2_s, idx2, U8, "v2_s")
-        v_w = gather(tab_w, idx, U32, "v_w")
-        v_s = gather(tab_s, idx, U8, "v_s")
-
-        w1_w = [keep.tile([P, W1_COLS], U32, name="w1_w%d" % g, align_bytes=64) for g in range(H // W1_COLS)]
-        w1_s = [keep.tile([P, W1_COLS], U8, name="w1_s%d" % g, align_bytes=64) for g in range(H // W1_COLS)]
+        w1_w = [keep.tile([P, W_COLS], U32, name="w1_w%d" % g, align_bytes=64) for g in range(H // W_COLS)]
+        w1_s = [keep.tile([P, W_COLS], U8, name="w1_s%d" % g, align_bytes=64) for g in range(H // W_COLS)]
 
         def quantize_w1(g):
-            raw = ring.tile([P, PACK, W1_COLS], F32, name="w1_raw", bufs=2)
-            nc.sync.dma_start(
-                raw[:], w1[:, g * W1_COLS : (g + 1) * W1_COLS].rearrange("(p j) c -> p j c", j=PACK)
-            )
-            grouped = ring.tile([P, W1_COLS, PACK], BF16, name="w1_grouped", tag="w1_grouped", align_bytes=64)
-            for k in range(W1_COLS // P):
-                sign = -1.0 if g * W1_COLS // P + k in TURNED_PAGES else 1.0
-                nc.scalar.activation(
-                    grouped[:, k * P : (k + 1) * P, :].rearrange("p (c i) j -> p c j i", i=4),
-                    raw[:, :, k * P : (k + 1) * P].rearrange("p j (c i) -> p c j i", i=4), COPY, scale=sign,
-                )
+            raw = ring.tile([P, PACK, W_COLS], F32, name="w1_raw")
+            nc.sync.dma_start(raw[:], w1[:, g * W_COLS : (g + 1) * W_COLS].rearrange("(p j) c -> p j c", j=PACK))
+            grouped = ring.tile([P, W_COLS, PACK], BF16, name="w1_grouped", align_bytes=64)
+            round_rows(raw[:], grouped[:], -1.0 if g * HEAD_PAGES < TURNED_PAGES else 1.0)
             nc.vector.quantize_mx(
                 out=w1_w[g][:].bitcast(FP8X4), scales=w1_s[g][:], in_=grouped[:].rearrange("p c j -> p (c j)")
             )
 
-        def load_negated(src, name):
+        def load_weights(src, name):
             t = keep.tile([P, S], F32, name=name)
             nc.sync.dma_start(t[:], src)
-            nc.scalar.activation(t[:], t[:], COPY, scale=-1.0)
             return t
 
         def load_cap(i):
@@ -129,151 +112,166 @@ def tile_list_two_phase_weave_kernel(
             nc.sync.dma_start(t[:], cap[i * P : (i + 1) * P, :])
             return t
 
-        w3_head = [load_words(w3_words[a, :, :W3_HEAD, :], "w3_head%d" % a) for a in range(2)]
-        cap_rows = load_cap(0)
-        neg_cap = cap_rows
-        nc.scalar.activation(neg_cap[:], cap_rows[:], COPY, scale=-1.0)
+        def load_ref(i):
+            t = ring.tile([P, T2], F32, name="ref_rows", tag="rows_2k", bufs=4)
+            nc.sync.dma_start(t[:], ref[i * P : (i + 1) * P, :])
+            return t
+
+        def load_w3(c0, c1, name):
+            tiles = [keep.tile([P, c1 - c0], U32, name="%s%d" % (name, a), align_bytes=64) for a in range(2)]
+            return [load_words(tiles[a], w3_words[a, :, c0:c1, :]) for a in range(2)]
+
+        idx = load_list(offs, "idx")
+        tab_w = load_words(page_bytes(U32, "tab_w"), tab_words[0])
+        tab_s = load_scales(tab_scales, "tab_s", nc.vector, nc.sync)
+        w3_s = load_scales(w3_scales, "w3_s", nc.gpsimd, nc.gpsimd)
+        v_w = gather(tab_w, idx, U32, "v_w")
+        v_s = gather(tab_s, idx, U8, "v_s")
         quantize_w1(0)
-        idx4 = load_list(offs4, "idx4")
-        wg2_sb = keep.tile([P, S], F32, name="wg2_sb")
-        nc.sync.dma_start(wg2_sb[:], wg2)
         w2_w = keep.tile([P, 2 * H], U8, name="w2_w", align_bytes=64)
         nc.sync.dma_start(w2_w[:].bitcast(I32), w2_words[0].bitcast(I32))
+        w2_s = load_scales(w2_scales, "w2_s", nc.vector, nc.sync)
+        idx2 = load_list(offs2, "idx2")
+        tab2_s = load_scales(tab2_scales, "tab2_s", nc.vector, nc.scalar)
+        tab2_w = [load_words(page_bytes(U32, "tab2_w%d" % a), tab2_words[a]) for a in range(2)]
+        v2_w = [gather(tab2_w[a], idx2, U32, "v2_w%d" % a) for a in range(2)]
+        v2_s = gather(tab2_s, idx2, U8, "v2_s")
         idx3 = load_list(offs3, "idx3")
-        neg_wg1 = load_negated(wg1, "neg_wg1")
+        wg1_sb = load_weights(wg1, "wg1_sb")
+        w3_head = load_w3(0, W_COLS, "w3_head")
+        caps = {0: load_cap(0)}
+        idx4 = load_list(offs4, "idx4")
+        wg2_sb = load_weights(wg2, "wg2_sb")
 
         ident = keep.tile([P, P], F32, name="ident")
         make_identity(nc, ident[:])
 
-        firsts = {}
-        seconds = {}
-
-        def liquid_second(i, half):
-            cols = slice(half * BANK, (half + 1) * BANK)
-            acc = next_bank()
-            nc.tensor.matmul_mx(
-                acc[:], lhsT=w2_w[:, 2 * i * P : 2 * (i + 1) * P].bitcast(FP4X4),
-                lhsT_scale=w2_s[:, i * P : (i + 1) * P],
-                rhs=v_w[:, cols].bitcast(FP8X4), rhs_scale=v_s[:, cols], start=True, stop=True,
-            )
-            if i == PAGES - 1 and half == 1:
-                seconds[i, half] = ring.tile([P, BANK], F32, name="second_end", bufs=1, align_bytes=64)
-            else:
-                seconds[i, half] = ring.tile([P, BANK], F32, name="second_sb", bufs=4, align_bytes=64)
-            nc.scalar.activation(seconds[i, half][:], acc[:], COPY, scale=-1.0 if i in COPIED_PAGES else 1.0)
-
-        def liquid_first(i, half):
-            g, c0 = divmod(i * P, W1_COLS)
-            cols = slice(half * BANK, (half + 1) * BANK)
-            firsts[i, half] = next_bank() if i in COPIED_PAGES else bank(half)
-            nc.tensor.matmul_mx(
-                firsts[i, half][:], lhsT=w1_w[g][:, c0 : c0 + P].bitcast(FP8X4), lhsT_scale=w1_s[g][:, c0 : c0 + P],
-                rhs=v_w[:, cols].bitcast(FP8X4), rhs_scale=v_s[:, cols], start=True, stop=True,
+        def turn(acc, slot, src, start, stop):
+            nc.tensor.matmul(
+                acc[:, slot * P : (slot + 1) * P], lhsT=src, rhs=ident[:], is_transpose=True, start=start, stop=stop
             )
 
         def turn_sum(acc, sources):
             for k, src in enumerate(sources):
-                for b in range(4):
-                    nc.tensor.matmul(
-                        acc[:, b * P : (b + 1) * P], lhsT=src[:, b * P : (b + 1) * P], rhs=ident[:], is_transpose=True,
-                        start=(k == 0 and b == 0), stop=(k == len(sources) - 1 and b == 3),
-                    )
+                for b in range(PACK):
+                    turn(acc, b, src[:, b * P : (b + 1) * P], k == 0 and b == 0, k == len(sources) - 1 and b == PACK - 1)
 
-        h1 = {}
+        def bound_parts(bound, neg_value):
+            room = next_bank()
+            turn_sum(room, [bound, neg_value])
+            excess_t = ring.tile([P, BANK], F32, name="excess_t", tag="parts_a", bufs=4)
+            nc.scalar.activation(excess_t[:], room[:], RELU, scale=-1.0)
+            plain = next_bank()
+            turn_sum(plain, [neg_value])
+            neg_value_t = ring.tile([P, BANK], F32, name="neg_value_t", tag="parts_b", bufs=4)
+            nc.scalar.copy(neg_value_t[:], plain[:])
+            return [neg_value_t, excess_t]
+
+        neg_h1 = {}
         liquid_parts = {}
+        neg_b = {}
+        held = []
 
-        def h1_tile(i):
-            h1[i] = ring.tile([P, S], F32, name="h1", tag="slot%d" % (i % 4), bufs=1, align_bytes=64)
+        def w1_cols(i):
+            g, c0 = divmod(i * P, W_COLS)
+            return w1_w[g][:, c0 : c0 + P].bitcast(FP8X4), w1_s[g][:, c0 : c0 + P]
 
-        def cells_times(acc, half, operands):
-            for b in range(4):
-                cells = slice(half * BANK + b * P, half * BANK + (b + 1) * P)
+        def w2_cols(i):
+            return w2_w[:, 2 * i * P : 2 * (i + 1) * P].bitcast(FP4X4), w2_s[:, i * P : (i + 1) * P]
+
+        def liquid_tile(name):
+            return ring.tile([P, BANK], F32, name=name, tag="liquid", bufs=4, align_bytes=64)
+
+        def cells_times(s, operands):
+            acc = next_bank()
+            for b in range(PACK):
+                cells = slice(s * BANK + b * P, s * BANK + (b + 1) * P)
                 for k, (words, scales) in enumerate(operands):
                     nc.tensor.matmul_mx(
                         acc[:, b * P : (b + 1) * P], lhsT=v_w[:, cells].bitcast(FP8X4), lhsT_scale=v_s[:, cells],
                         rhs=words, rhs_scale=scales, start=(k == 0), stop=(k == len(operands) - 1),
                     )
+            return acc
 
-        def neg_w1_cols(i):
-            g, c0 = divmod(i * P, W1_COLS)
-            return w1_w[g][:, c0 : c0 + P].bitcast(FP8X4), w1_s[g][:, c0 : c0 + P]
+        def times_cells(s, words, scales):
+            acc = next_bank()
+            cells = slice(s * BANK, (s + 1) * BANK)
+            nc.tensor.matmul_mx(
+                acc[:], lhsT=words, lhsT_scale=scales,
+                rhs=v_w[:, cells].bitcast(FP8X4), rhs_scale=v_s[:, cells], start=True, stop=True,
+            )
+            return acc
 
-        def liquid_lead(i, half, acc):
-            w2_cols = (w2_w[:, 2 * i * P : 2 * (i + 1) * P].bitcast(FP4X4), w2_s[:, i * P : (i + 1) * P])
-            cells_times(acc, half, [neg_w1_cols(i), w2_cols])
-            lead_t = ring.tile([P, BANK], F32, name="lead_t", tag="second_sb", bufs=4, align_bytes=64)
-            nc.scalar.activation(lead_t[:], acc[:], RELU)
-            liquid_parts[i, half] = [lead_t]
+        def liquid_open(i, s):
+            if i < TURNED_PAGES:
+                acc = cells_times(s, [w1_cols(i), w2_cols(i)])
+                lead_t = liquid_tile("lead_t")
+                nc.scalar.activation(lead_t[:], acc[:], RELU)
+                liquid_parts[i, s] = [lead_t]
+            else:
+                acc = times_cells(s, *w2_cols(i))
+                neg_b[i, s] = liquid_tile("neg_b")
+                nc.scalar.activation(neg_b[i, s][:], acc[:], COPY, scale=-1.0)
 
-        def liquid_base(i, half, acc):
-            cells_times(acc, half, [neg_w1_cols(i)])
-            base_t = ring.tile([P, BANK], F32, name="base_t", tag="second_sb", bufs=4, align_bytes=64)
-            nc.scalar.activation(base_t[:], acc[:], COPY, scale=-1.0)
-            liquid_parts[i, half].append(base_t)
+        def liquid_close(i, s):
+            if i < TURNED_PAGES:
+                acc = cells_times(s, [w1_cols(i)])
+                a_t = liquid_tile("a_t")
+                nc.scalar.activation(a_t[:], acc[:], COPY, scale=-1.0)
+                liquid_parts[i, s].append(a_t)
+            else:
+                acc = times_cells(s, *w1_cols(i))
+                a_sb = ring.tile([P, BANK], F32, name="a_sb", tag="sums", bufs=4)
+                nc.scalar.copy(a_sb[:], acc[:])
+                liquid_parts[i, s] = bound_parts(neg_b[i, s], a_sb)
 
-        def liquid_join(i, half):
-            if half == 0:
-                h1_tile(i)
-            both = next_bank()
-            turn_sum(both, liquid_parts[i, half])
-            nc.scalar.copy(h1[i][:, half * BANK : (half + 1) * BANK], both[:])
+        def liquid_join(i, s):
+            if s == 0:
+                neg_h1[i] = ring.tile([P, S], F32, name="neg_h1", tag="slot%d" % (i % H1_SLOTS), bufs=1, align_bytes=64)
+            very_last = i == LAST and s == 1
+            both = bank(HELD_BANK) if very_last else next_bank()
+            turn_sum(both, liquid_parts[i, s])
+            width = LAST_CUT - BANK if very_last else BANK
+            nc.scalar.activation(neg_h1[i][:, s * BANK : s * BANK + width], both[:, :width], COPY, scale=-1.0)
+            if very_last:
+                held.append(both)
 
         neg_h2 = {}
-        caps = {0: cap_rows}
         neg_sum = {}
-        turned_parts = {}
+        vapour_parts = {}
 
-        def vapour_product(i, half):
-            cols = slice(half * BANK, (half + 1) * BANK)
-            if half == 0:
+        def vapour_product(i, s):
+            cells = slice(s * BANK, (s + 1) * BANK)
+            if s == 0:
                 neg_h2[i] = ring.tile([P, S], F32, name="neg_h2", bufs=3)
-                if i > 0:
+                if i not in caps:
                     caps[i] = load_cap(i)
             acc = next_bank()
             for a in range(2):
-                if i * P < W3_HEAD:
+                if i < HEAD_PAGES:
                     w3_cols = w3_head[a][:, i * P : (i + 1) * P]
                 else:
-                    w3_cols = w3_rest[a][:, i * P - W3_HEAD : (i + 1) * P - W3_HEAD]
+                    w3_cols = w3_rest[a][:, i * P - W_COLS : (i + 1) * P - W_COLS]
                 nc.tensor.matmul_mx(
-                    acc[:], lhsT=w3_cols.bitcast(FP8X4),
-                    lhsT_scale=w3_s[4 * a :, i * P : (i + 1) * P],
-                    rhs=v2_w[a][:, cols].bitcast(FP8X4), rhs_scale=v2_s[4 * a :, cols],
+                    acc[:], lhsT=w3_cols.bitcast(FP8X4), lhsT_scale=w3_s[4 * a :, i * P : (i + 1) * P],
+                    rhs=v2_w[a][:, cells].bitcast(FP8X4), rhs_scale=v2_s[4 * a :, cells],
                     start=(a == 0), stop=(a == 1),
                 )
-            if i == 0:
-                nc.vector.scalar_tensor_tensor(neg_h2[i][:, cols], acc[:], -1.0, neg_cap[:, cols], ALU.mult, ALU.max)
-            else:
-                neg_sum[i, half] = ring.tile([P, BANK], F32, name="neg_sum", bufs=4)
-                nc.scalar.activation(neg_sum[i, half][:], acc[:], COPY, scale=-1.0)
+            neg_sum[i, s] = ring.tile([P, BANK], F32, name="neg_sum", tag="sums", bufs=4)
+            nc.scalar.activation(neg_sum[i, s][:], acc[:], COPY, scale=-1.0)
 
-        def vapour_turn(i, half):
-            turned_parts[i, half] = bound_turn(caps[i][:, half * BANK : (half + 1) * BANK], neg_sum[i, half])
+        def vapour_turn(i, s):
+            vapour_parts[i, s] = bound_parts(caps[i][:, s * BANK : (s + 1) * BANK], neg_sum[i, s])
 
-        def bound_turn(bound, neg_value):
-            room = next_bank()
-            turn_sum(room, [bound, neg_value])
-            excess_t = ring.tile([P, BANK], F32, name="excess_t", tag="turned_a", bufs=4)
-            nc.scalar.activation(excess_t[:], room[:], RELU, scale=-1.0)
-            plain = next_bank()
-            turn_sum(plain, [neg_value])
-            neg_sum_t = ring.tile([P, BANK], F32, name="neg_sum_t", tag="turned_b", bufs=4)
-            nc.scalar.copy(neg_sum_t[:], plain[:])
-            return [neg_sum_t, excess_t]
+        def vapour_join(i, s):
+            both = next_bank()
+            turn_sum(both, vapour_parts[i, s])
+            nc.scalar.copy(neg_h2[i][:, s * BANK : (s + 1) * BANK], both[:])
 
-        def vapour_join(i, half):
-            bounded = next_bank()
-            turn_sum(bounded, turned_parts[i, half])
-            nc.scalar.copy(neg_h2[i][:, half * BANK : (half + 1) * BANK], bounded[:])
+        def packed_tile(name, halves):
+            return keep.tile([P, halves * PACKED], U32, name=name, align_bytes=64)
 
-        def packed_tile(name, cleared, parts=1):
-            t = keep.tile([P, parts * PACKED], U32, name=name, align_bytes=64)
-            if cleared:
-                for h in range(parts):
-                    nc.gpsimd.memset(part(t, h)[:, COLS:].bitcast(I32), 0)
-            return t
-
-        def part(t, h):
+        def half_of(t, h):
             return t[:, h * PACKED : (h + 1) * PACKED]
 
         def codes_of(t, c0=0, c1=COLS):
@@ -283,238 +281,206 @@ def tile_list_two_phase_weave_kernel(
             return t[:, COLS:].bitcast(U8)[:, c0:c1]
 
         def quadrant(t, q):
-            return t[32 * q : 32 * (q + 1), :].bitcast(I32)
+            return t[QUAD * q : QUAD * (q + 1), :].bitcast(I32)
 
         def place(i, c):
-            a, quarter = divmod(i, PACK)
-            if a == 1 and quarter == 3:
+            if i == LAST:
                 return c
-            if a == 1 and quarter == c:
-                return 3
-            return quarter
+            if i == PACK + c:
+                return PACK - 1
+            return i % PACK
 
-        wo_q = {1: packed_tile("wo_q1", False)}
+        wo_q = {1: packed_tile("wo_q1", 1)}
         wo_grouped = {}
-        wo_last = [packed_tile("wo_last%d" % c, False) for c in range(3)] + [wo_q[1]]
-        page_q = {PAGES - 1: packed_tile("page_q_last", False, 2)}
-        z_q = {(a, c): packed_tile("z_q%d%d" % (a, c), False, 2) for a in range(2) for c in range(4)}
+        wo_last = [packed_tile("wo_last%d" % c, 1) for c in range(PACK - 1)] + [wo_q[1]]
+        page_q = {LAST: packed_tile("page_q_last", 2)}
+        z_q = {(a, c): packed_tile("z_q%d%d" % (a, c), 2) for a in range(2) for c in range(PACK)}
 
-        def quantize_wo_pass(a):
+        def quantize_wo(a):
             nc.vector.quantize_mx(
                 out=codes_of(wo_q[a]), scales=scales_of(wo_q[a]), in_=wo_grouped[a][:].rearrange("p n j -> p (n j)")
             )
 
-        def quantize_wo():
+        def prepare_wo():
             raw = ring.tile([P, 2, PACK, N], F32, name="wo_raw", tag="rows_2k", bufs=4)
             nc.sync.dma_start(raw[:], wo.rearrange("(a p j) n -> p a j n", a=2, j=PACK))
             for a in range(2):
                 wo_grouped[a] = keep.tile([P, N, PACK], BF16, name="wo_grouped%d" % a, align_bytes=64)
-                cast_rows(raw[:, a], wo_grouped[a][:])
-            quantize_wo_pass(1)
-            for c in range(3):
-                for quarter in range(PACK):
-                    nc.sync.dma_start(quadrant(wo_last[c], place(PACK + quarter, c)), quadrant(wo_q[1], quarter))
+                round_rows(raw[:, a], wo_grouped[a][:], 1.0)
+            quantize_wo(1)
+            for c in range(PACK - 1):
+                for q in range(PACK):
+                    nc.sync.dma_start(quadrant(wo_last[c], place(PACK + q, c)), quadrant(wo_q[1], q))
 
-        def turn_onto(acc, src, h, b, first):
-            for c in range(4):
+        neg_pages = []
+        refs = {}
+        z_t = {}
+        z_grouped = {}
+
+        def turn_onto(acc, src, h, b, opens):
+            for c in range(PACK):
                 m0 = h * HALF + c * COLS + b * P
-                nc.tensor.matmul(
-                    acc[:, c * P : (c + 1) * P], lhsT=src[:, m0 : m0 + P], rhs=ident[:], is_transpose=True,
-                    start=(first and c == 0), stop=(not first and c == 3),
-                )
+                turn(acc, c, src[:, m0 : m0 + P], opens and c == 0, not opens and c == PACK - 1)
 
-        def round_z(acc, turned, b, on_vector):
-            dst = turned[:, b, :].rearrange("m (u cq e) -> m u cq e", u=2, e=2)
+        def z_t_tile():
+            return ring.tile([P, BANK], BF16, name="z_t", bufs=8)
+
+        def round_z(acc, dst, on_vector):
+            dst = dst[:].rearrange("m (u cq e) -> m u cq e", u=2, e=2)
             src = acc[:].rearrange("m (cq u e) -> m u cq e", u=2, e=2)
             if on_vector:
                 nc.vector.tensor_scalar_mul(dst, src, -1.0)
             else:
                 nc.scalar.activation(dst, src, COPY, scale=-1.0)
 
-        def turn_back(turned, acc, grouped):
-            words = turned[:].rearrange("m b x -> m (b x)").bitcast(F32)
-            for s in range(4):
-                nc.tensor.transpose(acc[:, s * P : (s + 1) * P], words[:, s * P : (s + 1) * P], ident[:])
+        def turn_back(blocks_t, acc, grouped):
+            for slot in range(PACK):
+                b, u = divmod(slot, 2)
+                words = blocks_t[b][:].bitcast(F32)
+                nc.tensor.transpose(acc[:, slot * P : (slot + 1) * P], words[:, u * P : (u + 1) * P], ident[:])
             nc.scalar.copy(
-                grouped.bitcast(F32).rearrange("p (b m u) -> p b m u", b=2, u=2),
-                acc[:].rearrange("p (b u m) -> p b m u", b=2, u=2),
+                grouped[:].bitcast(F32).rearrange("p (b n u) -> p b n u", b=2, u=2),
+                acc[:].rearrange("p (b u n) -> p b n u", b=2, u=2),
             )
 
-        def quantize_z(i, h, grouped):
-            packed = part(page_q[i], h)
-            nc.vector.quantize_mx(out=codes_of(packed), scales=scales_of(packed), in_=grouped)
-
-        def load_ref(i):
-            t = ring.tile([P, T2], F32, name="ref_rows", tag="rows_2k", bufs=4)
-            nc.sync.dma_start(t[:], ref[i * P : (i + 1) * P, :])
-            return t
-
-        refs = {}
-        z_turned = {}
-        z_grouped = {}
-
-        def depart(i, h, b, acc):
-            if h == 0 and b == 0:
+        def depart(i, h, b):
+            acc = next_bank()
+            if i not in refs:
                 refs[i] = load_ref(i)
-            if b == 0:
-                z_turned[i, h] = ring.tile([P, 2, BANK], BF16, name="z_turned", bufs=4)
+            z_t[i, h, b] = z_t_tile()
             turn_onto(acc, refs[i], h, b, True)
             turn_onto(acc, neg_pages[i], h, b, False)
-            round_z(acc, z_turned[i, h], b, False)
+            round_z(acc, z_t[i, h, b], False)
+
+        def grouped_offset(i, h):
+            return (2 * ((LAST - i) % 2) + h) * 2 * HALF
 
         def regroup(i, h):
-            if h == 0:
-                z_grouped[i] = ring.tile(
-                    [P, 2 * HALF], BF16, name="z_grouped", tag="grouped%d" % (i % 2), bufs=1, align_bytes=64
-                )
-            turn_back(z_turned[i, h], next_bank(), z_grouped[i][:, h * HALF : (h + 1) * HALF])
+            spot = grouped_offset(i, h)
+            z_grouped[i, h] = placed.tile([P, HALF], BF16, name="z_grouped%d" % spot, offset=spot, align_bytes=64)
+            turn_back([z_t[i, h, b] for b in range(2)], next_bank(), z_grouped[i, h])
+
+        def quantize_z(i, h, grouped):
+            packed = half_of(page_q[i], h)
+            nc.vector.quantize_mx(out=codes_of(packed), scales=scales_of(packed), in_=grouped[:])
 
         def quantize_page(i):
-            page_q[i] = ring.tile([P, 2 * PACKED], U32, name="page_q", tag="slot%d" % ((i + 1) % 4), bufs=1, align_bytes=64)
+            page_q[i] = ring.tile(
+                [P, 2 * PACKED], U32, name="page_q", tag="slot%d" % ((i + 1) % H1_SLOTS), bufs=1, align_bytes=64
+            )
             for h in range(2):
-                quantize_z(i, h, z_grouped[i][:, h * HALF : (h + 1) * HALF])
-            for c in range(4):
+                quantize_z(i, h, z_grouped[i, h])
+            for c in range(PACK):
                 nc.sync.dma_start(quadrant(z_q[i // PACK, c], place(i, c)), quadrant(page_q[i], c))
-
-        def liquid_turn(i, half):
-            first_sb = ring.tile([P, BANK], F32, name="first_sb", tag="neg_sum", bufs=4)
-            nc.scalar.copy(first_sb[:], firsts[i, half][:])
-            liquid_parts[i, half] = bound_turn(seconds[i, half], first_sb)
 
         def side_work(r):
             liq, dep, vap = r + 1, r - 1, r + 2
-            has_liq, has_dep, has_vap = liq < PAGES, dep >= 0, vap < PAGES
-            turned = liq in TURNED_PAGES
-            for half in range(2):
-                if turned:
-                    liquid_lead(liq, half, next_bank())
-                elif has_liq:
-                    liquid_second(liq, half)
-            for b in range(2):
-                if has_dep:
-                    depart(dep, 0, b, next_bank())
-                if turned:
-                    liquid_base(liq, b, next_bank())
-                elif has_liq:
-                    liquid_first(liq, b)
-                if liq in COPIED_PAGES:
-                    liquid_turn(liq, b)
-            if has_dep:
-                depart(dep, 1, 0, next_bank())
-            if has_vap:
-                vapour_product(vap, 0)
-            if turned or liq in COPIED_PAGES:
-                liquid_join(liq, 0)
-            if has_dep:
-                depart(dep, 1, 1, next_bank())
-            if has_vap:
-                vapour_turn(vap, 0)
-            if turned or liq in COPIED_PAGES:
-                liquid_join(liq, 1)
-            if has_vap:
-                vapour_product(vap, 1)
-            if has_dep:
-                regroup(dep, 0)
-            if has_vap:
-                vapour_join(vap, 0)
-            if has_dep:
-                regroup(dep, 1)
-            if has_vap:
-                vapour_turn(vap, 1)
-                vapour_join(vap, 1)
+            steps = [
+                (liquid_open, liq, 0), (liquid_open, liq, 1),
+                (depart, dep, 0, 0), (liquid_close, liq, 0), (depart, dep, 0, 1), (liquid_close, liq, 1),
+                (depart, dep, 1, 0), (vapour_product, vap, 0), (liquid_join, liq, 0),
+                (depart, dep, 1, 1), (vapour_turn, vap, 0), (liquid_join, liq, 1),
+                (vapour_product, vap, 1), (regroup, dep, 0), (vapour_join, vap, 0), (regroup, dep, 1),
+                (vapour_turn, vap, 1), (vapour_join, vap, 1),
+            ]
+            for step in steps:
+                first = 0 if step[0] in (depart, regroup) else HEAD_PAGES
+                if first <= step[1] < PAGES:
+                    step[0](*step[1:])
 
-        def project(acc, a, h, pair, half):
-            for s in range(2):
-                c = 2 * pair + s
-                wo_cols = wo_last[c] if a == 1 else wo_q[0]
-                nc.tensor.matmul_mx(
-                    acc[:, s * COLS : (s + 1) * COLS],
-                    lhsT=codes_of(wo_cols, half * P, (half + 1) * P),
-                    lhsT_scale=scales_of(wo_cols, half * P, (half + 1) * P),
-                    rhs=codes_of(part(z_q[a, c], h)), rhs_scale=scales_of(part(z_q[a, c], h)),
-                    start=(a == 0 and s == 0), stop=(a == 1 and s == 1),
-                )
-
-        def store(acc, h, pair, half, copy):
-            result = ring.tile([P, BANK], F32, name="result", tag=("turned_a", "turned_b")[half], bufs=4)
-            copy(result[:], acc[:])
-            m0 = h * HALF + pair * BANK
-            nc.sync.dma_start(out[half * P : (half + 1) * P, m0 : m0 + BANK], result[:])
-
-        def scatter(page, lst, values, weights, j0, j1):
+        def scatter(i, lst, values, weights, j0, j1):
             nc.vector.tensor_tensor(
-                page[:].indirect(lst[:, j0 // 16 : j1 // 16]), values, weights[:, j0:j1], ALU.mult
+                neg_pages[i][:].indirect(lst[:, j0 // 16 : j1 // 16]), values, weights[:, j0:j1], ALU.mult
             )
 
-        neg_pages = []
-        for half in range(2):
-            vapour_product(0, half)
-        for half in range(2):
-            liquid_second(0, half)
-            liquid_first(0, half)
-        for half in range(2):
-            vapour_product(1, half)
-            vapour_turn(1, half)
-        for half in range(2):
-            vapour_join(1, half)
-        w3_rest = [load_words(w3_words[a, :, W3_HEAD:, :], "w3_rest%d" % a) for a in range(2)]
+        def project(acc, a, h, pair, nh):
+            for k in range(2):
+                c = 2 * pair + k
+                wo_cols = wo_last[c] if a == 1 else wo_q[0]
+                nc.tensor.matmul_mx(
+                    acc[:, k * COLS : (k + 1) * COLS],
+                    lhsT=codes_of(wo_cols, nh * P, (nh + 1) * P), lhsT_scale=scales_of(wo_cols, nh * P, (nh + 1) * P),
+                    rhs=codes_of(half_of(z_q[a, c], h)), rhs_scale=scales_of(half_of(z_q[a, c], h)),
+                    start=(a == 0 and k == 0), stop=(a == 1 and k == 1),
+                )
+
+        def store(acc, h, pair, nh, copy):
+            result = ring.tile([P, BANK], F32, name="result", tag=("parts_a", "parts_b")[nh], bufs=4)
+            copy(result[:], acc[:])
+            m0 = h * HALF + pair * BANK
+            nc.sync.dma_start(out[nh * P : (nh + 1) * P, m0 : m0 + BANK], result[:])
+
+        for s in range(2):
+            liquid_open(0, s)
+            liquid_close(0, s)
+        for s in range(2):
+            liquid_join(0, s)
+        for s in range(2):
+            liquid_open(1, s)
+            liquid_close(1, s)
+            vapour_product(0, s)
+        for s in range(2):
+            liquid_join(1, s)
+            vapour_turn(0, s)
+        for s in range(2):
+            vapour_product(1, s)
+            vapour_join(0, s)
+        for s in range(2):
+            vapour_turn(1, s)
+        for s in range(2):
+            vapour_join(1, s)
+        for i in range(HEAD_PAGES):
+            neg_pages.append(page_bytes(F32, "neg_page"))
+            scatter(i, idx3, neg_h1[i][:], wg1_sb, 0, S)
+        w3_rest = load_w3(W_COLS, H, "w3_rest")
+
         for i in range(PAGES):
-            last = i == PAGES - 1
-            neg_pages.append(ring.tile([P, T2], F32, name="neg_page", tag="page", bufs=3, align_bytes=64))
-            if i not in TURNED_PAGES + COPIED_PAGES:
-                h1_tile(i)
-                for half in range(2):
-                    width = LAST_CUT - BANK if last and half == 1 else BANK
-                    nc.vector.tensor_tensor(
-                        h1[i][:, half * BANK : half * BANK + width], firsts[i, half][:, :width],
-                        seconds[i, half][:, :width], ALU.max,
-                    )
-            scatter(neg_pages[i], idx4, neg_h2[i][:], wg2_sb, 0, S)
-            cut = LAST_CUT if last else S
-            scatter(neg_pages[i], idx3, h1[i][:, :cut], neg_wg1, 0, cut)
-            if i + 1 < H // W1_COLS:
+            if i >= HEAD_PAGES:
+                neg_pages.append(page_bytes(F32, "neg_page"))
+            scatter(i, idx4, neg_h2[i][:], wg2_sb, 0, S)
+            if i >= HEAD_PAGES:
+                cut = LAST_CUT if i == LAST else S
+                scatter(i, idx3, neg_h1[i][:, :cut], wg1_sb, 0, cut)
+            if i + 1 < H // W_COLS:
                 quantize_w1(i + 1)
-            if i == 3:
-                quantize_wo()
-            if i == 1:
-                turning.extend([0, 1])
-            if i == PAGES - 2:
-                turning.remove(0)
-                turning.remove(1)
+            if i + 1 == H // W_COLS:
+                prepare_wo()
+            if i + 1 == LAST:
+                turning.remove(HELD_BANK)
             side_work(i)
             if i >= 1:
                 quantize_page(i - 1)
 
-        i = PAGES - 1
-        h1_end = ring.tile([P, S - LAST_CUT], F32, name="h1_end", tag="grouped%d" % ((i - 1) % 2), bufs=1, align_bytes=64)
-        nc.vector.tensor_tensor(h1_end[:], firsts[i, 1][:, LAST_CUT - BANK :], seconds[i, 1][:, LAST_CUT - BANK :], ALU.max)
-        wo_q[0] = ring.tile([P, PACKED], U32, name="wo_q0", tag="second_end", bufs=1, align_bytes=64)
-        quantize_wo_pass(0)
-        scatter(neg_pages[i], idx3, h1_end[:], neg_wg1, LAST_CUT, S)
-        blocks = [(h, b) for h in range(2) for b in range(2)]
-        tiles = [(pair, half) for pair in range(2) for half in range(2)]
-        ref_rows = load_ref(i)
-        sums = [bank(k) for k in range(4)]
-        for k, (h, b) in enumerate(blocks):
-            turn_onto(sums[k], ref_rows, h, b, True)
-        accs = {}
-        for k, (pair, half) in enumerate(tiles):
-            accs[0, k] = bank(4 + k)
-            project(accs[0, k], 0, 0, pair, half)
+        spot = grouped_offset(LAST - 1, 1)
+        neg_h1_end = placed.tile([P, S - LAST_CUT], F32, name="neg_h1_end", offset=spot + 4 * PACKED, align_bytes=64)
+        nc.scalar.activation(neg_h1_end[:], held[0][:, LAST_CUT - BANK :], COPY, scale=-1.0)
+        wo_q[0] = placed.tile([P, PACKED], U32, name="wo_q0", offset=spot, align_bytes=64)
+        quantize_wo(0)
+        scatter(LAST, idx3, neg_h1_end[:], wg1_sb, LAST_CUT, S)
+
+        tiles = [(pair, nh) for pair in range(2) for nh in range(N // P)]
+        refs[LAST] = load_ref(LAST)
+        sums = {(h, b): bank(2 * h + b) for h in range(2) for b in range(2)}
+        for (h, b), acc in sums.items():
+            turn_onto(acc, refs[LAST], h, b, True)
+        results = {}
+        for k, (pair, nh) in enumerate(tiles):
+            results[0, k] = bank(PACK + k)
+            project(results[0, k], 0, 0, pair, nh)
         for h in range(2):
-            turned = ring.tile([P, 2, BANK], BF16, name="z_turned", bufs=4)
+            blocks_t = [z_t_tile() for b in range(2)]
             for b in range(2):
-                turn_onto(sums[2 * h + b], neg_pages[i], h, b, False)
-                round_z(sums[2 * h + b], turned, b, b == 1)
-            grouped = ring.tile([P, HALF], BF16, name="z_grouped_last", tag="second_sb", bufs=4, align_bytes=64)
-            turn_back(turned, bank(h), grouped[:])
+                turn_onto(sums[h, b], neg_pages[LAST], h, b, False)
+                round_z(sums[h, b], blocks_t[b], b == 1)
+            grouped = ring.tile([P, HALF], BF16, name="z_grouped_last", tag="liquid", bufs=4, align_bytes=64)
+            turn_back(blocks_t, bank(h), grouped)
             if h == 1:
-                for k, (pair, half) in enumerate(tiles):
-                    accs[1, k] = bank((2, 3, 0, 1)[k])
-                    project(accs[1, k], 0, 1, pair, half)
-            quantize_z(i, h, grouped[:])
-            for c in range(4):
-                nc.vector.tensor_copy(quadrant(part(z_q[1, c], h), c), quadrant(part(page_q[i], h), c))
-            for k, (pair, half) in enumerate(tiles):
-                project(accs[h, k], 1, h, pair, half)
-                store(accs[h, k], h, pair, half, nc.vector.tensor_copy if h == 1 and k != 1 else nc.scalar.copy)
+                for k, (pair, nh) in enumerate(tiles):
+                    results[1, k] = bank((k + 2) % PACK)
+                    project(results[1, k], 0, 1, pair, nh)
+            quantize_z(LAST, h, grouped)
+            for c in range(PACK):
+                nc.vector.tensor_copy(quadrant(half_of(z_q[1, c], h), c), quadrant(half_of(page_q[LAST], h), c))
+            for k, (pair, nh) in enumerate(tiles):
+                project(results[h, k], 1, h, pair, nh)
+                store(results[h, k], h, pair, nh, nc.vector.tensor_copy if h == 1 and k != 1 else nc.scalar.copy)

@@ -30,10 +30,8 @@ COLS = 256
 PACKED = COLS + COLS // PACK
 HEAD_PAGES = 2
 W_COLS = HEAD_PAGES * P
-TURNED_PAGES = 4
-LAST_CUT = 640
-HELD_BANK = 1
-H1_SLOTS = 4
+TURNED_PAGES = (0, 3, 4, 5)
+LAST_CUT = BANK
 
 
 def tile_list_two_phase_weave_kernel(
@@ -51,11 +49,13 @@ def tile_list_two_phase_weave_kernel(
             return psum.tile([P, BANK], F32, name="bank%d" % k)
 
         taken = []
-        turning = list(range(BANKS))
+
+        def next_number():
+            taken.append(0)
+            return len(taken) % BANKS
 
         def next_bank():
-            taken.append(0)
-            return bank(turning[len(taken) % len(turning)])
+            return bank(next_number())
 
         def load_list(src, name):
             t = keep.tile([P, S // 16], U16, name=name)
@@ -66,8 +66,8 @@ def tile_list_two_phase_weave_kernel(
             nc.sync.dma_start(t[:].bitcast(I32), src.rearrange("p n t -> p (n t)").bitcast(I32))
             return t
 
-        def page_bytes(dtype, name):
-            return ring.tile([P, T2], dtype, name=name, tag="page", bufs=3, align_bytes=64)
+        def page_bytes(dtype, name, k):
+            return ring.tile([P, T2], dtype, name=name, tag="page%d" % (k % 3), bufs=1, align_bytes=64)
 
         def load_scales(src, name, clear_engine, queue):
             passes, width = src.shape[0], src.shape[2]
@@ -79,8 +79,11 @@ def tile_list_two_phase_weave_kernel(
                 )
             return t
 
-        def gather(window, lst, dtype, name):
-            t = keep.tile([P, S], dtype, name=name, align_bytes=64)
+        def quadrant(t, q):
+            return t[QUAD * q : QUAD * (q + 1), :].bitcast(I32)
+
+        def gather(window, lst, dtype, name, tag=None):
+            t = keep.tile([P, S], dtype, name=name, tag=tag or name, align_bytes=64)
             nc.vector.tensor_copy(t[:], window[:].indirect(lst[:]))
             return t
 
@@ -96,8 +99,11 @@ def tile_list_two_phase_weave_kernel(
         def quantize_w1(g):
             raw = ring.tile([P, PACK, W_COLS], F32, name="w1_raw")
             nc.sync.dma_start(raw[:], w1[:, g * W_COLS : (g + 1) * W_COLS].rearrange("(p j) c -> p j c", j=PACK))
-            grouped = ring.tile([P, W_COLS, PACK], BF16, name="w1_grouped", align_bytes=64)
-            round_rows(raw[:], grouped[:], -1.0 if g * HEAD_PAGES < TURNED_PAGES else 1.0)
+            if g == 0:
+                grouped = keep.tile([P, W_COLS, PACK], BF16, name="w1_first", tag="first", align_bytes=64)
+            else:
+                grouped = ring.tile([P, W_COLS, PACK], BF16, name="w1_grouped", align_bytes=64)
+            round_rows(raw[:], grouped[:], -1.0)
             nc.vector.quantize_mx(
                 out=w1_w[g][:].bitcast(FP8X4), scales=w1_s[g][:], in_=grouped[:].rearrange("p c j -> p (c j)")
             )
@@ -108,12 +114,15 @@ def tile_list_two_phase_weave_kernel(
             return t
 
         def load_cap(i):
-            t = ring.tile([P, S], F32, name="cap_rows", bufs=3)
+            if i == LAST:
+                t = ring.tile([P, S], F32, name="cap_last", tag="late", bufs=1, align_bytes=64)
+            else:
+                t = ring.tile([P, S], F32, name="cap_rows", bufs=2)
             nc.sync.dma_start(t[:], cap[i * P : (i + 1) * P, :])
             return t
 
         def load_ref(i):
-            t = ring.tile([P, T2], F32, name="ref_rows", tag="rows_2k", bufs=4)
+            t = ring.tile([P, T2], F32, name="ref_rows", tag="rows_2k", bufs=3)
             nc.sync.dma_start(t[:], ref[i * P : (i + 1) * P, :])
             return t
 
@@ -122,29 +131,31 @@ def tile_list_two_phase_weave_kernel(
             return [load_words(tiles[a], w3_words[a, :, c0:c1, :]) for a in range(2)]
 
         idx = load_list(offs, "idx")
-        tab_w = load_words(page_bytes(U32, "tab_w"), tab_words[0])
-        tab_s = load_scales(tab_scales, "tab_s", nc.vector, nc.sync)
-        w3_s = load_scales(w3_scales, "w3_s", nc.gpsimd, nc.gpsimd)
-        v_w = gather(tab_w, idx, U32, "v_w")
+        tab_s = keep.tile([P, T], U8, name="tab_s", tag="tab_s", align_bytes=64)
+        for q in range(PACK):
+            rows = tab_scales[:, 4 * q : 4 * q + 4, :].bitcast(I32)
+            nc.sync.dma_start(quadrant(tab_s, q), rows.broadcast_to([QUAD // 4, 4, T // 4]))
+        tab_w = load_words(page_bytes(U32, "tab_w", 2), tab_words[0])
         v_s = gather(tab_s, idx, U8, "v_s")
+        v_w = gather(tab_w, idx, U32, "v_w")
         quantize_w1(0)
+        idx2 = load_list(offs2, "idx2")
+        tab2_s = load_scales(tab2_scales, "tab2_s", nc.vector, nc.sync)
         w2_w = keep.tile([P, 2 * H], U8, name="w2_w", align_bytes=64)
         nc.sync.dma_start(w2_w[:].bitcast(I32), w2_words[0].bitcast(I32))
         w2_s = load_scales(w2_scales, "w2_s", nc.vector, nc.sync)
-        idx2 = load_list(offs2, "idx2")
-        tab2_s = load_scales(tab2_scales, "tab2_s", nc.vector, nc.scalar)
-        tab2_w = [load_words(page_bytes(U32, "tab2_w%d" % a), tab2_words[a]) for a in range(2)]
+        tab2_w = [load_words(page_bytes(U32, "tab2_w%d" % a, 1 - a), tab2_words[a]) for a in range(2)]
+        v2_s = gather(tab2_s, idx2, U8, "v2_s", "first")
         v2_w = [gather(tab2_w[a], idx2, U32, "v2_w%d" % a) for a in range(2)]
-        v2_s = gather(tab2_s, idx2, U8, "v2_s")
         idx3 = load_list(offs3, "idx3")
         wg1_sb = load_weights(wg1, "wg1_sb")
+        ident = keep.tile([P, P], F32, name="ident")
+        make_identity(nc, ident[:])
         w3_head = load_w3(0, W_COLS, "w3_head")
+        w3_s = load_scales(w3_scales, "w3_s", nc.vector, nc.sync)
         caps = {0: load_cap(0)}
         idx4 = load_list(offs4, "idx4")
         wg2_sb = load_weights(wg2, "wg2_sb")
-
-        ident = keep.tile([P, P], F32, name="ident")
-        make_identity(nc, ident[:])
 
         def turn(acc, slot, src, start, stop):
             nc.tensor.matmul(
@@ -156,21 +167,24 @@ def tile_list_two_phase_weave_kernel(
                 for b in range(PACK):
                     turn(acc, b, src[:, b * P : (b + 1) * P], k == 0 and b == 0, k == len(sources) - 1 and b == PACK - 1)
 
-        def bound_parts(bound, neg_value):
-            room = next_bank()
-            turn_sum(room, [bound, neg_value])
-            excess_t = ring.tile([P, BANK], F32, name="excess_t", tag="parts_a", bufs=4)
-            nc.scalar.activation(excess_t[:], room[:], RELU, scale=-1.0)
-            plain = next_bank()
-            turn_sum(plain, [neg_value])
-            neg_value_t = ring.tile([P, BANK], F32, name="neg_value_t", tag="parts_b", bufs=4)
-            nc.scalar.copy(neg_value_t[:], plain[:])
-            return [neg_value_t, excess_t]
+        def gap_part(terms, sign):
+            acc = next_bank()
+            turn_sum(acc, terms)
+            gap_t = ring.tile([P, BANK], F32, name="gap_t", tag="parts_a", bufs=4)
+            nc.scalar.activation(gap_t[:], acc[:], RELU, scale=sign)
+            return gap_t
+
+        def base_part(term, sign):
+            acc = next_bank()
+            turn_sum(acc, [term])
+            base_t = ring.tile([P, BANK], F32, name="base_t", tag="parts_b", bufs=4)
+            nc.scalar.activation(base_t[:], acc[:], COPY, scale=sign)
+            return base_t
 
         neg_h1 = {}
         liquid_parts = {}
-        neg_b = {}
-        held = []
+        b_sb = {}
+        neg_a = {}
 
         def w1_cols(i):
             g, c0 = divmod(i * P, W_COLS)
@@ -180,7 +194,7 @@ def tile_list_two_phase_weave_kernel(
             return w2_w[:, 2 * i * P : 2 * (i + 1) * P].bitcast(FP4X4), w2_s[:, i * P : (i + 1) * P]
 
         def liquid_tile(name):
-            return ring.tile([P, BANK], F32, name=name, tag="liquid", bufs=4, align_bytes=64)
+            return ring.tile([P, BANK], F32, name=name, tag="liquid", bufs=6, align_bytes=64)
 
         def cells_times(s, operands):
             acc = next_bank()
@@ -203,38 +217,42 @@ def tile_list_two_phase_weave_kernel(
             return acc
 
         def liquid_open(i, s):
-            if i < TURNED_PAGES:
+            if i in TURNED_PAGES:
                 acc = cells_times(s, [w1_cols(i), w2_cols(i)])
                 lead_t = liquid_tile("lead_t")
                 nc.scalar.activation(lead_t[:], acc[:], RELU)
                 liquid_parts[i, s] = [lead_t]
             else:
                 acc = times_cells(s, *w2_cols(i))
-                neg_b[i, s] = liquid_tile("neg_b")
-                nc.scalar.activation(neg_b[i, s][:], acc[:], COPY, scale=-1.0)
+                b_sb[i, s] = liquid_tile("b_sb")
+                nc.scalar.copy(b_sb[i, s][:], acc[:])
+                liquid_parts[i, s] = []
 
         def liquid_close(i, s):
-            if i < TURNED_PAGES:
+            if i in TURNED_PAGES:
                 acc = cells_times(s, [w1_cols(i)])
                 a_t = liquid_tile("a_t")
                 nc.scalar.activation(a_t[:], acc[:], COPY, scale=-1.0)
                 liquid_parts[i, s].append(a_t)
             else:
                 acc = times_cells(s, *w1_cols(i))
-                a_sb = ring.tile([P, BANK], F32, name="a_sb", tag="sums", bufs=4)
-                nc.scalar.copy(a_sb[:], acc[:])
-                liquid_parts[i, s] = bound_parts(neg_b[i, s], a_sb)
+                neg_a[i, s] = ring.tile([P, BANK], F32, name="neg_a", tag="sums", bufs=4)
+                nc.scalar.copy(neg_a[i, s][:], acc[:])
+
+        def liquid_gap(i, s):
+            if i not in TURNED_PAGES:
+                liquid_parts[i, s].append(gap_part([b_sb[i, s], neg_a[i, s]], 1.0))
+
+        def liquid_base(i, s):
+            if i not in TURNED_PAGES:
+                liquid_parts[i, s].append(base_part(neg_a[i, s], -1.0))
 
         def liquid_join(i, s):
             if s == 0:
-                neg_h1[i] = ring.tile([P, S], F32, name="neg_h1", tag="slot%d" % (i % H1_SLOTS), bufs=1, align_bytes=64)
-            very_last = i == LAST and s == 1
-            both = bank(HELD_BANK) if very_last else next_bank()
+                neg_h1[i] = ring.tile([P, S], F32, name="neg_h1", bufs=3)
+            both = next_bank()
             turn_sum(both, liquid_parts[i, s])
-            width = LAST_CUT - BANK if very_last else BANK
-            nc.scalar.activation(neg_h1[i][:, s * BANK : s * BANK + width], both[:, :width], COPY, scale=-1.0)
-            if very_last:
-                held.append(both)
+            nc.scalar.activation(neg_h1[i][:, s * BANK : (s + 1) * BANK], both[:], COPY, scale=-1.0)
 
         neg_h2 = {}
         neg_sum = {}
@@ -260,8 +278,11 @@ def tile_list_two_phase_weave_kernel(
             neg_sum[i, s] = ring.tile([P, BANK], F32, name="neg_sum", tag="sums", bufs=4)
             nc.scalar.activation(neg_sum[i, s][:], acc[:], COPY, scale=-1.0)
 
-        def vapour_turn(i, s):
-            vapour_parts[i, s] = bound_parts(caps[i][:, s * BANK : (s + 1) * BANK], neg_sum[i, s])
+        def vapour_gap(i, s):
+            vapour_parts[i, s] = [gap_part([caps[i][:, s * BANK : (s + 1) * BANK], neg_sum[i, s]], -1.0)]
+
+        def vapour_base(i, s):
+            vapour_parts[i, s].append(base_part(neg_sum[i, s], 1.0))
 
         def vapour_join(i, s):
             both = next_bank()
@@ -280,9 +301,6 @@ def tile_list_two_phase_weave_kernel(
         def scales_of(t, c0=0, c1=COLS):
             return t[:, COLS:].bitcast(U8)[:, c0:c1]
 
-        def quadrant(t, q):
-            return t[QUAD * q : QUAD * (q + 1), :].bitcast(I32)
-
         def place(i, c):
             if i == LAST:
                 return c
@@ -298,15 +316,16 @@ def tile_list_two_phase_weave_kernel(
 
         def quantize_wo(a):
             nc.vector.quantize_mx(
-                out=codes_of(wo_q[a]), scales=scales_of(wo_q[a]), in_=wo_grouped[a][:].rearrange("p n j -> p (n j)")
+                out=codes_of(wo_q[a]), scales=scales_of(wo_q[a]), in_=wo_grouped[a].rearrange("p n j -> p (n j)")
             )
 
         def prepare_wo():
-            raw = ring.tile([P, 2, PACK, N], F32, name="wo_raw", tag="rows_2k", bufs=4)
+            raw = ring.tile([P, 2, PACK, N], F32, name="wo_raw", tag="rows_2k", bufs=3)
             nc.sync.dma_start(raw[:], wo.rearrange("(a p j) n -> p a j n", a=2, j=PACK))
-            for a in range(2):
-                wo_grouped[a] = keep.tile([P, N, PACK], BF16, name="wo_grouped%d" % a, align_bytes=64)
-                round_rows(raw[:, a], wo_grouped[a][:], 1.0)
+            both = ring.tile([P, 2, N, PACK], BF16, name="wo_grouped", tag="late", bufs=1, align_bytes=64)
+            for a in (1, 0):
+                wo_grouped[a] = both[:, a]
+                round_rows(raw[:, a], wo_grouped[a], 1.0)
             quantize_wo(1)
             for c in range(PACK - 1):
                 for q in range(PACK):
@@ -365,27 +384,29 @@ def tile_list_two_phase_weave_kernel(
             nc.vector.quantize_mx(out=codes_of(packed), scales=scales_of(packed), in_=grouped[:])
 
         def quantize_page(i):
-            page_q[i] = ring.tile(
-                [P, 2 * PACKED], U32, name="page_q", tag="slot%d" % ((i + 1) % H1_SLOTS), bufs=1, align_bytes=64
-            )
+            page_q[i] = ring.tile([P, 2 * PACKED], U32, name="page_q", bufs=2, align_bytes=64)
             for h in range(2):
                 quantize_z(i, h, z_grouped[i, h])
             for c in range(PACK):
                 nc.sync.dma_start(quadrant(z_q[i // PACK, c], place(i, c)), quadrant(page_q[i], c))
 
         def side_work(r):
-            liq, dep, vap = r + 1, r - 1, r + 2
+            ahead, dep = r + 2, r - 1
             steps = [
-                (liquid_open, liq, 0), (liquid_open, liq, 1),
-                (depart, dep, 0, 0), (liquid_close, liq, 0), (depart, dep, 0, 1), (liquid_close, liq, 1),
-                (depart, dep, 1, 0), (vapour_product, vap, 0), (liquid_join, liq, 0),
-                (depart, dep, 1, 1), (vapour_turn, vap, 0), (liquid_join, liq, 1),
-                (vapour_product, vap, 1), (regroup, dep, 0), (vapour_join, vap, 0), (regroup, dep, 1),
-                (vapour_turn, vap, 1), (vapour_join, vap, 1),
+                (liquid_open, ahead, 0), (vapour_join, r + 1, 1), (depart, dep, 0, 0),
+                (liquid_close, ahead, 0), (depart, dep, 0, 1), (depart, dep, 1, 0),
+                (liquid_open, ahead, 1), (depart, dep, 1, 1), (liquid_gap, ahead, 0), (regroup, dep, 0),
+                (liquid_close, ahead, 1), (liquid_base, ahead, 0), (regroup, dep, 1),
+                (vapour_product, ahead, 0), (liquid_join, r + 1, 0 if r + 1 == LAST else 1), (liquid_gap, ahead, 1),
+                (liquid_join, ahead, 0), (vapour_gap, ahead, 0),
+                (vapour_product, ahead, 1), (liquid_base, ahead, 1), (vapour_base, ahead, 0),
+                (vapour_gap, ahead, 1), (vapour_base, ahead, 1), (vapour_join, ahead, 0),
             ]
-            for step in steps:
+            for k, step in enumerate(steps):
                 first = 0 if step[0] in (depart, regroup) else HEAD_PAGES
-                if first <= step[1] < PAGES:
+                if step == (vapour_join, 1, 1):
+                    first = 1
+                if first <= step[1] < PAGES and not (r + 2 == LAST and step == (liquid_join, LAST, 0)):
                     step[0](*step[1:])
 
         def scatter(i, lst, values, weights, j0, j1):
@@ -410,73 +431,65 @@ def tile_list_two_phase_weave_kernel(
             m0 = h * HALF + pair * BANK
             nc.sync.dma_start(out[nh * P : (nh + 1) * P, m0 : m0 + BANK], result[:])
 
-        for s in range(2):
-            liquid_open(0, s)
-            liquid_close(0, s)
-        for s in range(2):
-            liquid_join(0, s)
-        for s in range(2):
-            liquid_open(1, s)
-            liquid_close(1, s)
-            vapour_product(0, s)
-        for s in range(2):
-            liquid_join(1, s)
-            vapour_turn(0, s)
-        for s in range(2):
-            vapour_product(1, s)
-            vapour_join(0, s)
-        for s in range(2):
-            vapour_turn(1, s)
-        for s in range(2):
-            vapour_join(1, s)
+        head = [
+            (liquid_open, 0, 0), (liquid_close, 0, 0), (liquid_open, 0, 1), (liquid_open, 1, 0),
+            (liquid_close, 0, 1), (liquid_close, 1, 0), (liquid_join, 0, 0), (liquid_open, 1, 1),
+            (liquid_join, 0, 1), (liquid_close, 1, 1), (liquid_gap, 1, 0), (vapour_product, 0, 0),
+            (liquid_base, 1, 0), (liquid_gap, 1, 1), (vapour_product, 0, 1), (liquid_base, 1, 1),
+            (liquid_join, 1, 0), (vapour_gap, 0, 0), (liquid_join, 1, 1), (vapour_base, 0, 0),
+            (vapour_product, 1, 0), (vapour_gap, 0, 1), (vapour_base, 0, 1), (vapour_join, 0, 0),
+            (vapour_product, 1, 1), (vapour_gap, 1, 0), (vapour_join, 0, 1), (vapour_base, 1, 0),
+            (vapour_gap, 1, 1), (vapour_base, 1, 1), (vapour_join, 1, 0),
+        ]
+        for step in head:
+            step[0](*step[1:])
         for i in range(HEAD_PAGES):
-            neg_pages.append(page_bytes(F32, "neg_page"))
+            neg_pages.append(page_bytes(F32, "neg_page", i))
             scatter(i, idx3, neg_h1[i][:], wg1_sb, 0, S)
         w3_rest = load_w3(W_COLS, H, "w3_rest")
 
         for i in range(PAGES):
             if i >= HEAD_PAGES:
-                neg_pages.append(page_bytes(F32, "neg_page"))
+                neg_pages.append(page_bytes(F32, "neg_page", i))
             scatter(i, idx4, neg_h2[i][:], wg2_sb, 0, S)
             if i >= HEAD_PAGES:
+                quantize_page(i - 2)
                 cut = LAST_CUT if i == LAST else S
                 scatter(i, idx3, neg_h1[i][:, :cut], wg1_sb, 0, cut)
             if i + 1 < H // W_COLS:
                 quantize_w1(i + 1)
-            if i + 1 == H // W_COLS:
-                prepare_wo()
-            if i + 1 == LAST:
-                turning.remove(HELD_BANK)
             side_work(i)
-            if i >= 1:
-                quantize_page(i - 1)
+            if i + 1 == LAST:
+                prepare_wo()
 
+        liquid_join(LAST, 1)
+        quantize_page(LAST - 1)
         spot = grouped_offset(LAST - 1, 1)
-        neg_h1_end = placed.tile([P, S - LAST_CUT], F32, name="neg_h1_end", offset=spot + 4 * PACKED, align_bytes=64)
-        nc.scalar.activation(neg_h1_end[:], held[0][:, LAST_CUT - BANK :], COPY, scale=-1.0)
         wo_q[0] = placed.tile([P, PACKED], U32, name="wo_q0", offset=spot, align_bytes=64)
         quantize_wo(0)
-        scatter(LAST, idx3, neg_h1_end[:], wg1_sb, LAST_CUT, S)
+        scatter(LAST, idx3, neg_h1[LAST][:, LAST_CUT:], wg1_sb, LAST_CUT, S)
 
         tiles = [(pair, nh) for pair in range(2) for nh in range(N // P)]
         refs[LAST] = load_ref(LAST)
-        sums = {(h, b): bank(2 * h + b) for h in range(2) for b in range(2)}
+        first = [next_number() for k in range(PACK)]
+        second = [next_number() for k in range(PACK)]
+        sums = {(h, b): bank(first[2 * h + b]) for h in range(2) for b in range(2)}
         for (h, b), acc in sums.items():
             turn_onto(acc, refs[LAST], h, b, True)
         results = {}
         for k, (pair, nh) in enumerate(tiles):
-            results[0, k] = bank(PACK + k)
+            results[0, k] = bank(second[k])
             project(results[0, k], 0, 0, pair, nh)
         for h in range(2):
             blocks_t = [z_t_tile() for b in range(2)]
             for b in range(2):
                 turn_onto(sums[h, b], neg_pages[LAST], h, b, False)
                 round_z(sums[h, b], blocks_t[b], b == 1)
-            grouped = ring.tile([P, HALF], BF16, name="z_grouped_last", tag="liquid", bufs=4, align_bytes=64)
-            turn_back(blocks_t, bank(h), grouped)
+            grouped = ring.tile([P, HALF], BF16, name="z_grouped_last", tag="liquid", bufs=6, align_bytes=64)
+            turn_back(blocks_t, bank(first[h]), grouped)
             if h == 1:
                 for k, (pair, nh) in enumerate(tiles):
-                    results[1, k] = bank((k + 2) % PACK)
+                    results[1, k] = bank(first[(k + 2) % PACK])
                     project(results[1, k], 0, 1, pair, nh)
             quantize_z(LAST, h, grouped)
             for c in range(PACK):

@@ -30,8 +30,11 @@ COLS = 256
 PACKED = COLS + COLS // PACK
 HEAD_PAGES = 2
 W_COLS = HEAD_PAGES * P
-TURNED_PAGES = (0, 3, 4, 5)
-LAST_CUT = BANK
+TURNED_PAGES = (0, 2, 3, 4)
+TURN = 5
+LAST_CUT = 640
+HELD_BANK = BANKS - 1
+LATE = 4 * 2 * HALF
 
 
 def tile_list_two_phase_weave_kernel(
@@ -52,7 +55,7 @@ def tile_list_two_phase_weave_kernel(
 
         def next_number():
             taken.append(0)
-            return len(taken) % BANKS
+            return len(taken) % TURN
 
         def next_bank():
             return bank(next_number())
@@ -97,12 +100,12 @@ def tile_list_two_phase_weave_kernel(
         w1_s = [keep.tile([P, W_COLS], U8, name="w1_s%d" % g, align_bytes=64) for g in range(H // W_COLS)]
 
         def quantize_w1(g):
-            raw = ring.tile([P, PACK, W_COLS], F32, name="w1_raw")
+            raw = ring.tile([P, PACK, W_COLS], F32, name="w1_raw", bufs=1)
             nc.sync.dma_start(raw[:], w1[:, g * W_COLS : (g + 1) * W_COLS].rearrange("(p j) c -> p j c", j=PACK))
             if g == 0:
                 grouped = keep.tile([P, W_COLS, PACK], BF16, name="w1_first", tag="first", align_bytes=64)
             else:
-                grouped = ring.tile([P, W_COLS, PACK], BF16, name="w1_grouped", align_bytes=64)
+                grouped = ring.tile([P, W_COLS, PACK], BF16, name="w1_grouped", bufs=1, align_bytes=64)
             round_rows(raw[:], grouped[:], -1.0)
             nc.vector.quantize_mx(
                 out=w1_w[g][:].bitcast(FP8X4), scales=w1_s[g][:], in_=grouped[:].rearrange("p c j -> p (c j)")
@@ -117,12 +120,12 @@ def tile_list_two_phase_weave_kernel(
             if i == LAST:
                 t = ring.tile([P, S], F32, name="cap_last", tag="late", bufs=1, align_bytes=64)
             else:
-                t = ring.tile([P, S], F32, name="cap_rows", bufs=2)
+                t = ring.tile([P, S], F32, name="cap_rows", bufs=3)
             nc.sync.dma_start(t[:], cap[i * P : (i + 1) * P, :])
             return t
 
         def load_ref(i):
-            t = ring.tile([P, T2], F32, name="ref_rows", tag="rows_2k", bufs=3)
+            t = ring.tile([P, T2], F32, name="ref_rows", tag="rows_2k", bufs=4)
             nc.sync.dma_start(t[:], ref[i * P : (i + 1) * P, :])
             return t
 
@@ -185,6 +188,7 @@ def tile_list_two_phase_weave_kernel(
         liquid_parts = {}
         b_sb = {}
         neg_a = {}
+        held = []
 
         def w1_cols(i):
             g, c0 = divmod(i * P, W_COLS)
@@ -194,7 +198,7 @@ def tile_list_two_phase_weave_kernel(
             return w2_w[:, 2 * i * P : 2 * (i + 1) * P].bitcast(FP4X4), w2_s[:, i * P : (i + 1) * P]
 
         def liquid_tile(name):
-            return ring.tile([P, BANK], F32, name=name, tag="liquid", bufs=6, align_bytes=64)
+            return ring.tile([P, BANK], F32, name=name, tag="liquid", bufs=4, align_bytes=64)
 
         def cells_times(s, operands):
             acc = next_bank()
@@ -249,10 +253,14 @@ def tile_list_two_phase_weave_kernel(
 
         def liquid_join(i, s):
             if s == 0:
-                neg_h1[i] = ring.tile([P, S], F32, name="neg_h1", bufs=3)
-            both = next_bank()
+                neg_h1[i] = ring.tile([P, S], F32, name="neg_h1", bufs=2)
+            very_last = i == LAST and s == 1
+            both = bank(HELD_BANK) if very_last else next_bank()
             turn_sum(both, liquid_parts[i, s])
-            nc.scalar.activation(neg_h1[i][:, s * BANK : (s + 1) * BANK], both[:], COPY, scale=-1.0)
+            width = LAST_CUT - BANK if very_last else BANK
+            nc.scalar.activation(neg_h1[i][:, s * BANK : s * BANK + width], both[:, :width], COPY, scale=-1.0)
+            if very_last:
+                held.append(both)
 
         neg_h2 = {}
         neg_sum = {}
@@ -308,8 +316,9 @@ def tile_list_two_phase_weave_kernel(
                 return PACK - 1
             return i % PACK
 
-        wo_q = {1: packed_tile("wo_q1", 1)}
+        wo_q = [packed_tile("wo_q%d" % a, 1) for a in range(2)]
         wo_grouped = {}
+        wo_raw = []
         wo_last = [packed_tile("wo_last%d" % c, 1) for c in range(PACK - 1)] + [wo_q[1]]
         page_q = {LAST: packed_tile("page_q_last", 2)}
         z_q = {(a, c): packed_tile("z_q%d%d" % (a, c), 2) for a in range(2) for c in range(PACK)}
@@ -319,13 +328,14 @@ def tile_list_two_phase_weave_kernel(
                 out=codes_of(wo_q[a]), scales=scales_of(wo_q[a]), in_=wo_grouped[a].rearrange("p n j -> p (n j)")
             )
 
+        def round_wo(a, grouped):
+            wo_grouped[a] = grouped[:]
+            round_rows(wo_raw[0][:, a], grouped[:], 1.0)
+
         def prepare_wo():
-            raw = ring.tile([P, 2, PACK, N], F32, name="wo_raw", tag="rows_2k", bufs=3)
-            nc.sync.dma_start(raw[:], wo.rearrange("(a p j) n -> p a j n", a=2, j=PACK))
-            both = ring.tile([P, 2, N, PACK], BF16, name="wo_grouped", tag="late", bufs=1, align_bytes=64)
-            for a in (1, 0):
-                wo_grouped[a] = both[:, a]
-                round_rows(raw[:, a], wo_grouped[a], 1.0)
+            wo_raw.append(ring.tile([P, 2, PACK, N], F32, name="wo_raw", tag="rows_2k", bufs=4))
+            nc.sync.dma_start(wo_raw[0][:], wo.rearrange("(a p j) n -> p a j n", a=2, j=PACK))
+            round_wo(1, ring.tile([P, N, PACK], BF16, name="wo_grouped1", tag="late", bufs=1, align_bytes=64))
             quantize_wo(1)
             for c in range(PACK - 1):
                 for q in range(PACK):
@@ -366,7 +376,10 @@ def tile_list_two_phase_weave_kernel(
             acc = next_bank()
             if i not in refs:
                 refs[i] = load_ref(i)
-            z_t[i, h, b] = z_t_tile()
+            if i == LAST - 1 and h == 1:
+                z_t[i, h, b] = placed.tile([P, BANK], BF16, name="z_t_late%d" % b, offset=LATE + b * 4 * BANK)
+            else:
+                z_t[i, h, b] = z_t_tile()
             turn_onto(acc, refs[i], h, b, True)
             turn_onto(acc, neg_pages[i], h, b, False)
             round_z(acc, z_t[i, h, b], False)
@@ -391,22 +404,22 @@ def tile_list_two_phase_weave_kernel(
                 nc.sync.dma_start(quadrant(z_q[i // PACK, c], place(i, c)), quadrant(page_q[i], c))
 
         def side_work(r):
-            ahead, dep = r + 2, r - 1
+            liq, dep, vap = r + 1, r - 1, r + 2
+            liquid = [(liquid_open, liq, 0), (liquid_close, liq, 0), (liquid_open, liq, 1), (liquid_close, liq, 1)]
+            if liq not in TURNED_PAGES:
+                liquid += [(liquid_gap, liq, 0), (liquid_base, liq, 0), (liquid_gap, liq, 1), (liquid_base, liq, 1)]
+            liquid += [(liquid_join, liq, 0)]
             steps = [
-                (liquid_open, ahead, 0), (vapour_join, r + 1, 1), (depart, dep, 0, 0),
-                (liquid_close, ahead, 0), (depart, dep, 0, 1), (depart, dep, 1, 0),
-                (liquid_open, ahead, 1), (depart, dep, 1, 1), (liquid_gap, ahead, 0), (regroup, dep, 0),
-                (liquid_close, ahead, 1), (liquid_base, ahead, 0), (regroup, dep, 1),
-                (vapour_product, ahead, 0), (liquid_join, r + 1, 0 if r + 1 == LAST else 1), (liquid_gap, ahead, 1),
-                (liquid_join, ahead, 0), (vapour_gap, ahead, 0),
-                (vapour_product, ahead, 1), (liquid_base, ahead, 1), (vapour_base, ahead, 0),
-                (vapour_gap, ahead, 1), (vapour_base, ahead, 1), (vapour_join, ahead, 0),
+                None, (vapour_join, liq, 1), None, None, None, None,
+                (depart, dep, 0, 0), None, (depart, dep, 0, 1), None, (depart, dep, 1, 0),
+                (vapour_product, vap, 0), (depart, dep, 1, 1), None, (regroup, dep, 0),
+                (vapour_product, vap, 1), None, (regroup, dep, 1), (vapour_gap, vap, 0), (liquid_join, liq, 1),
+                (vapour_base, vap, 0), (vapour_gap, vap, 1), (vapour_base, vap, 1), (vapour_join, vap, 0),
             ]
-            for k, step in enumerate(steps):
-                first = 0 if step[0] in (depart, regroup) else HEAD_PAGES
-                if step == (vapour_join, 1, 1):
-                    first = 1
-                if first <= step[1] < PAGES and not (r + 2 == LAST and step == (liquid_join, LAST, 0)):
+            for step in steps:
+                if step is None:
+                    step = liquid.pop(0) if liquid else None
+                if step is not None and step[1] < PAGES:
                     step[0](*step[1:])
 
         def scatter(i, lst, values, weights, j0, j1):
@@ -414,39 +427,41 @@ def tile_list_two_phase_weave_kernel(
                 neg_pages[i][:].indirect(lst[:, j0 // 16 : j1 // 16]), values, weights[:, j0:j1], ALU.mult
             )
 
-        def project(acc, a, h, pair, nh):
-            for k in range(2):
-                c = 2 * pair + k
-                wo_cols = wo_last[c] if a == 1 else wo_q[0]
+        def project(acc, a, h, c):
+            wo_cols = wo_last[c] if a == 1 else wo_q[0]
+            for nh in range(N // P):
                 nc.tensor.matmul_mx(
-                    acc[:, k * COLS : (k + 1) * COLS],
+                    acc[:, nh * COLS : (nh + 1) * COLS],
                     lhsT=codes_of(wo_cols, nh * P, (nh + 1) * P), lhsT_scale=scales_of(wo_cols, nh * P, (nh + 1) * P),
                     rhs=codes_of(half_of(z_q[a, c], h)), rhs_scale=scales_of(half_of(z_q[a, c], h)),
-                    start=(a == 0 and k == 0), stop=(a == 1 and k == 1),
+                    start=(a == 0 and nh == 0), stop=(a == 1 and nh == 1),
                 )
 
-        def store(acc, h, pair, nh, copy):
-            result = ring.tile([P, BANK], F32, name="result", tag=("parts_a", "parts_b")[nh], bufs=4)
-            copy(result[:], acc[:])
-            m0 = h * HALF + pair * BANK
-            nc.sync.dma_start(out[nh * P : (nh + 1) * P, m0 : m0 + BANK], result[:])
+        def store(acc, h, c):
+            result = ring.tile([P, 2, COLS], F32, name="result", tag=("parts_a", "parts_b")[c % 2], bufs=4)
+            nc.scalar.copy(result[:].rearrange("p nh m -> p (nh m)"), acc[:])
+            m0 = h * HALF + c * COLS
+            nc.sync.dma_start(out[:, m0 : m0 + COLS].rearrange("(nh p) m -> p nh m", p=P), result[:])
 
         head = [
             (liquid_open, 0, 0), (liquid_close, 0, 0), (liquid_open, 0, 1), (liquid_open, 1, 0),
             (liquid_close, 0, 1), (liquid_close, 1, 0), (liquid_join, 0, 0), (liquid_open, 1, 1),
             (liquid_join, 0, 1), (liquid_close, 1, 1), (liquid_gap, 1, 0), (vapour_product, 0, 0),
             (liquid_base, 1, 0), (liquid_gap, 1, 1), (vapour_product, 0, 1), (liquid_base, 1, 1),
-            (liquid_join, 1, 0), (vapour_gap, 0, 0), (liquid_join, 1, 1), (vapour_base, 0, 0),
-            (vapour_product, 1, 0), (vapour_gap, 0, 1), (vapour_base, 0, 1), (vapour_join, 0, 0),
-            (vapour_product, 1, 1), (vapour_gap, 1, 0), (vapour_join, 0, 1), (vapour_base, 1, 0),
-            (vapour_gap, 1, 1), (vapour_base, 1, 1), (vapour_join, 1, 0),
+            (liquid_join, 1, 0), (vapour_gap, 0, 0), (liquid_join, 1, 1), (quantize_w1, 1), (vapour_base, 0, 0),
         ]
+        for i in (1, 2):
+            head += [
+                (vapour_product, i, 0), (vapour_gap, i - 1, 1), (vapour_base, i - 1, 1), (vapour_join, i - 1, 0),
+                (vapour_product, i, 1), (vapour_gap, i, 0), (vapour_join, i - 1, 1), (vapour_base, i, 0),
+            ]
+        head += [(vapour_gap, 2, 1), (vapour_base, 2, 1), (vapour_join, 2, 0)]
+        w3_rest = load_w3(W_COLS, H, "w3_rest")
         for step in head:
             step[0](*step[1:])
         for i in range(HEAD_PAGES):
             neg_pages.append(page_bytes(F32, "neg_page", i))
             scatter(i, idx3, neg_h1[i][:], wg1_sb, 0, S)
-        w3_rest = load_w3(W_COLS, H, "w3_rest")
 
         for i in range(PAGES):
             if i >= HEAD_PAGES:
@@ -456,44 +471,43 @@ def tile_list_two_phase_weave_kernel(
                 quantize_page(i - 2)
                 cut = LAST_CUT if i == LAST else S
                 scatter(i, idx3, neg_h1[i][:, :cut], wg1_sb, 0, cut)
-            if i + 1 < H // W_COLS:
+            if 1 < i + 1 < H // W_COLS:
                 quantize_w1(i + 1)
-            side_work(i)
+            if i >= 1:
+                side_work(i)
             if i + 1 == LAST:
                 prepare_wo()
 
-        liquid_join(LAST, 1)
         quantize_page(LAST - 1)
-        spot = grouped_offset(LAST - 1, 1)
-        wo_q[0] = placed.tile([P, PACKED], U32, name="wo_q0", offset=spot, align_bytes=64)
+        round_wo(0, placed.tile([P, N, PACK], BF16, name="wo_grouped0", offset=LATE, align_bytes=64))
         quantize_wo(0)
-        scatter(LAST, idx3, neg_h1[LAST][:, LAST_CUT:], wg1_sb, LAST_CUT, S)
+        neg_h1_end = placed.tile([P, S - LAST_CUT], F32, name="neg_h1_end", offset=LATE + 4 * BANK)
+        nc.scalar.activation(neg_h1_end[:], held[0][:, LAST_CUT - BANK :], COPY, scale=-1.0)
+        scatter(LAST, idx3, neg_h1_end[:], wg1_sb, LAST_CUT, S)
 
-        tiles = [(pair, nh) for pair in range(2) for nh in range(N // P)]
         refs[LAST] = load_ref(LAST)
-        first = [next_number() for k in range(PACK)]
-        second = [next_number() for k in range(PACK)]
+        first = list(range(TURN, HELD_BANK)) + [next_number() for k in range(2)]
+        second = [next_number() for k in range(PACK - 1)] + [HELD_BANK]
         sums = {(h, b): bank(first[2 * h + b]) for h in range(2) for b in range(2)}
         for (h, b), acc in sums.items():
             turn_onto(acc, refs[LAST], h, b, True)
         results = {}
-        for k, (pair, nh) in enumerate(tiles):
-            results[0, k] = bank(second[k])
-            project(results[0, k], 0, 0, pair, nh)
+        for c in range(PACK):
+            results[0, c] = bank(second[c])
+            project(results[0, c], 0, 0, c)
         for h in range(2):
             blocks_t = [z_t_tile() for b in range(2)]
             for b in range(2):
                 turn_onto(sums[h, b], neg_pages[LAST], h, b, False)
                 round_z(sums[h, b], blocks_t[b], b == 1)
-            grouped = ring.tile([P, HALF], BF16, name="z_grouped_last", tag="liquid", bufs=6, align_bytes=64)
-            turn_back(blocks_t, bank(first[h]), grouped)
+            grouped = ring.tile([P, HALF], BF16, name="z_grouped_last", tag="liquid", bufs=4, align_bytes=64)
+            turn_back(blocks_t, bank(first[2 * h + 1]), grouped)
             if h == 1:
-                for k, (pair, nh) in enumerate(tiles):
-                    results[1, k] = bank(first[(k + 2) % PACK])
-                    project(results[1, k], 0, 1, pair, nh)
+                for c in range(PACK):
+                    results[1, c] = bank(first[(0, 2, 1, 3)[c]])
+                    project(results[1, c], 0, 1, c)
             quantize_z(LAST, h, grouped)
             for c in range(PACK):
                 nc.vector.tensor_copy(quadrant(half_of(z_q[1, c], h), c), quadrant(half_of(page_q[LAST], h), c))
-            for k, (pair, nh) in enumerate(tiles):
-                project(results[h, k], 1, h, pair, nh)
-                store(results[h, k], h, pair, nh, nc.vector.tensor_copy if h == 1 and k != 1 else nc.scalar.copy)
+                project(results[h, c], 1, h, c)
+                store(results[h, c], h, c)

@@ -30,7 +30,7 @@ COLS = 256
 PACKED = COLS + COLS // PACK
 HEAD_PAGES = 2
 W_COLS = HEAD_PAGES * P
-TURNED_PAGES = (0, 2, 3, 4)
+TURNED_PAGES = (0, 1, 2, 3)
 TURN = 5
 LAST_CUT = 640
 HELD_BANK = BANKS - 1
@@ -105,7 +105,7 @@ def tile_list_two_phase_weave_kernel(
             if g == 0:
                 grouped = keep.tile([P, W_COLS, PACK], BF16, name="w1_first", tag="first", align_bytes=64)
             else:
-                grouped = ring.tile([P, W_COLS, PACK], BF16, name="w1_grouped", bufs=1, align_bytes=64)
+                grouped = ring.tile([P, W_COLS, PACK], BF16, name="w1_grouped", bufs=2, align_bytes=64)
             round_rows(raw[:], grouped[:], -1.0)
             nc.vector.quantize_mx(
                 out=w1_w[g][:].bitcast(FP8X4), scales=w1_s[g][:], in_=grouped[:].rearrange("p c j -> p (c j)")
@@ -142,14 +142,16 @@ def tile_list_two_phase_weave_kernel(
         v_s = gather(tab_s, idx, U8, "v_s")
         v_w = gather(tab_w, idx, U32, "v_w")
         quantize_w1(0)
-        idx2 = load_list(offs2, "idx2")
-        tab2_s = load_scales(tab2_scales, "tab2_s", nc.vector, nc.sync)
         w2_w = keep.tile([P, 2 * H], U8, name="w2_w", align_bytes=64)
         nc.sync.dma_start(w2_w[:].bitcast(I32), w2_words[0].bitcast(I32))
         w2_s = load_scales(w2_scales, "w2_s", nc.vector, nc.sync)
-        tab2_w = [load_words(page_bytes(U32, "tab2_w%d" % a, 1 - a), tab2_words[a]) for a in range(2)]
-        v2_s = gather(tab2_s, idx2, U8, "v2_s", "first")
-        v2_w = [gather(tab2_w[a], idx2, U32, "v2_w%d" % a) for a in range(2)]
+        idx2 = load_list(offs2, "idx2")
+        tab2_w0 = load_words(page_bytes(U32, "tab2_w0", 1), tab2_words[0])
+        tab2_s = load_scales(tab2_scales, "tab2_s", nc.vector, nc.sync)
+        tab2_w1 = load_words(page_bytes(U32, "tab2_w1", 0), tab2_words[1])
+        v2_w = [gather(tab2_w0, idx2, U32, "v2_w0", "first")]
+        v2_s = gather(tab2_s, idx2, U8, "v2_s")
+        v2_w.append(gather(tab2_w1, idx2, U32, "v2_w1"))
         idx3 = load_list(offs3, "idx3")
         wg1_sb = load_weights(wg1, "wg1_sb")
         ident = keep.tile([P, P], F32, name="ident")
@@ -437,18 +439,18 @@ def tile_list_two_phase_weave_kernel(
                     start=(a == 0 and nh == 0), stop=(a == 1 and nh == 1),
                 )
 
-        def store(acc, h, c):
+        def store(acc, h, c, copy):
             result = ring.tile([P, 2, COLS], F32, name="result", tag=("parts_a", "parts_b")[c % 2], bufs=4)
-            nc.scalar.copy(result[:].rearrange("p nh m -> p (nh m)"), acc[:])
+            copy(result[:].rearrange("p nh m -> p (nh m)"), acc[:])
             m0 = h * HALF + c * COLS
             nc.sync.dma_start(out[:, m0 : m0 + COLS].rearrange("(nh p) m -> p nh m", p=P), result[:])
 
         head = [
-            (liquid_open, 0, 0), (liquid_close, 0, 0), (liquid_open, 0, 1), (liquid_open, 1, 0),
-            (liquid_close, 0, 1), (liquid_close, 1, 0), (liquid_join, 0, 0), (liquid_open, 1, 1),
-            (liquid_join, 0, 1), (liquid_close, 1, 1), (liquid_gap, 1, 0), (vapour_product, 0, 0),
-            (liquid_base, 1, 0), (liquid_gap, 1, 1), (vapour_product, 0, 1), (liquid_base, 1, 1),
-            (liquid_join, 1, 0), (vapour_gap, 0, 0), (liquid_join, 1, 1), (quantize_w1, 1), (vapour_base, 0, 0),
+            (liquid_open, 0, 0), (liquid_close, 0, 0), (liquid_open, 0, 1), (liquid_close, 0, 1),
+            (liquid_join, 0, 0), (liquid_open, 1, 0), (liquid_join, 0, 1),
+            (liquid_close, 1, 0), (liquid_open, 1, 1), (liquid_close, 1, 1),
+            (liquid_join, 1, 0), (vapour_product, 0, 0), (liquid_join, 1, 1), (vapour_product, 0, 1),
+            (quantize_w1, 1), (vapour_gap, 0, 0), (vapour_base, 0, 0),
         ]
         for i in (1, 2):
             head += [
@@ -506,8 +508,15 @@ def tile_list_two_phase_weave_kernel(
                 for c in range(PACK):
                     results[1, c] = bank(first[(0, 2, 1, 3)[c]])
                     project(results[1, c], 0, 1, c)
+            own = half_of(z_q[1, 0], h)
+            for b in range(2):
+                nc.vector.quantize_mx(
+                    out=codes_of(own, b * P, (b + 1) * P)[:QUAD], scales=scales_of(own, b * P, (b + 1) * P)[:QUAD],
+                    in_=grouped[:QUAD, b * BANK : (b + 1) * BANK],
+                )
             quantize_z(LAST, h, grouped)
             for c in range(PACK):
-                nc.vector.tensor_copy(quadrant(half_of(z_q[1, c], h), c), quadrant(half_of(page_q[LAST], h), c))
+                if c > 0:
+                    nc.vector.tensor_copy(quadrant(half_of(z_q[1, c], h), c), quadrant(half_of(page_q[LAST], h), c))
                 project(results[h, c], 1, h, c)
-                store(results[h, c], h, c)
+                store(results[h, c], h, c, nc.scalar.copy)

@@ -35,6 +35,7 @@ TURN = 5
 LAST_CUT = 640
 HELD_BANK = BANKS - 1
 LATE = 4 * 2 * HALF
+V2_WORDS = LATE + 8 * BANK
 
 
 def tile_list_two_phase_weave_kernel(
@@ -72,9 +73,12 @@ def tile_list_two_phase_weave_kernel(
         def page_bytes(dtype, name, k):
             return ring.tile([P, T2], dtype, name=name, tag="page%d" % (k % 3), bufs=1, align_bytes=64)
 
-        def load_scales(src, name, clear_engine, queue):
+        def load_scales(src, name, clear_engine, queue, offset=None):
             passes, width = src.shape[0], src.shape[2]
-            t = keep.tile([P, width], U8, name=name, align_bytes=64)
+            if offset is None:
+                t = keep.tile([P, width], U8, name=name, align_bytes=64)
+            else:
+                t = placed.tile([P, width], U8, name=name, offset=offset, align_bytes=64)
             clear_engine.memset(t[:].bitcast(I32), 0)
             for q in range(PACK):
                 queue.dma_start(
@@ -85,8 +89,11 @@ def tile_list_two_phase_weave_kernel(
         def quadrant(t, q):
             return t[QUAD * q : QUAD * (q + 1), :].bitcast(I32)
 
-        def gather(window, lst, dtype, name, tag=None):
-            t = keep.tile([P, S], dtype, name=name, tag=tag or name, align_bytes=64)
+        def gather(window, lst, dtype, name, tag=None, offset=None):
+            if offset is None:
+                t = keep.tile([P, S], dtype, name=name, tag=tag or name, align_bytes=64)
+            else:
+                t = placed.tile([P, S], dtype, name=name, offset=offset, align_bytes=64)
             nc.vector.tensor_copy(t[:], window[:].indirect(lst[:]))
             return t
 
@@ -139,6 +146,7 @@ def tile_list_two_phase_weave_kernel(
             rows = tab_scales[:, 4 * q : 4 * q + 4, :].bitcast(I32)
             nc.sync.dma_start(quadrant(tab_s, q), rows.broadcast_to([QUAD // 4, 4, T // 4]))
         tab_w = load_words(page_bytes(U32, "tab_w", 2), tab_words[0])
+        tab2_s = load_scales(tab2_scales, "tab2_s", nc.vector, nc.gpsimd, V2_WORDS + 4 * S - T // 2)
         v_s = gather(tab_s, idx, U8, "v_s")
         v_w = gather(tab_w, idx, U32, "v_w")
         quantize_w1(0)
@@ -146,12 +154,9 @@ def tile_list_two_phase_weave_kernel(
         nc.sync.dma_start(w2_w[:].bitcast(I32), w2_words[0].bitcast(I32))
         w2_s = load_scales(w2_scales, "w2_s", nc.vector, nc.sync)
         idx2 = load_list(offs2, "idx2")
-        tab2_w0 = load_words(page_bytes(U32, "tab2_w0", 1), tab2_words[0])
-        tab2_s = load_scales(tab2_scales, "tab2_s", nc.vector, nc.sync)
-        tab2_w1 = load_words(page_bytes(U32, "tab2_w1", 0), tab2_words[1])
-        v2_w = [gather(tab2_w0, idx2, U32, "v2_w0", "first")]
-        v2_s = gather(tab2_s, idx2, U8, "v2_s")
-        v2_w.append(gather(tab2_w1, idx2, U32, "v2_w1"))
+        tab2_w = [load_words(page_bytes(U32, "tab2_w%d" % a, 1 - a), tab2_words[a]) for a in range(2)]
+        v2_s = gather(tab2_s, idx2, U8, "v2_s", "first")
+        v2_w = [gather(tab2_w[a], idx2, U32, "v2_w%d" % a, offset=V2_WORDS + 4 * S * a) for a in range(2)]
         idx3 = load_list(offs3, "idx3")
         wg1_sb = load_weights(wg1, "wg1_sb")
         ident = keep.tile([P, P], F32, name="ident")

@@ -35,7 +35,7 @@ TURN = 5
 LAST_CUT = 640
 HELD_BANK = BANKS - 1
 LATE = 4 * 2 * HALF
-V2_WORDS = LATE + 8 * BANK
+V2_WORDS = LATE + 4 * BANK + 8 * PACKED
 
 
 def tile_list_two_phase_weave_kernel(
@@ -89,9 +89,9 @@ def tile_list_two_phase_weave_kernel(
         def quadrant(t, q):
             return t[QUAD * q : QUAD * (q + 1), :].bitcast(I32)
 
-        def gather(window, lst, dtype, name, tag=None, offset=None):
+        def gather(window, lst, dtype, name, offset=None):
             if offset is None:
-                t = keep.tile([P, S], dtype, name=name, tag=tag or name, align_bytes=64)
+                t = keep.tile([P, S], dtype, name=name, align_bytes=64)
             else:
                 t = placed.tile([P, S], dtype, name=name, offset=offset, align_bytes=64)
             nc.vector.tensor_copy(t[:], window[:].indirect(lst[:]))
@@ -109,10 +109,7 @@ def tile_list_two_phase_weave_kernel(
         def quantize_w1(g):
             raw = ring.tile([P, PACK, W_COLS], F32, name="w1_raw", bufs=1)
             nc.sync.dma_start(raw[:], w1[:, g * W_COLS : (g + 1) * W_COLS].rearrange("(p j) c -> p j c", j=PACK))
-            if g == 0:
-                grouped = keep.tile([P, W_COLS, PACK], BF16, name="w1_first", tag="first", align_bytes=64)
-            else:
-                grouped = ring.tile([P, W_COLS, PACK], BF16, name="w1_grouped", bufs=2, align_bytes=64)
+            grouped = ring.tile([P, W_COLS, PACK], BF16, name="w1_grouped", align_bytes=64)
             round_rows(raw[:], grouped[:], -1.0)
             nc.vector.quantize_mx(
                 out=w1_w[g][:].bitcast(FP8X4), scales=w1_s[g][:], in_=grouped[:].rearrange("p c j -> p (c j)")
@@ -154,8 +151,8 @@ def tile_list_two_phase_weave_kernel(
         nc.sync.dma_start(w2_w[:].bitcast(I32), w2_words[0].bitcast(I32))
         w2_s = load_scales(w2_scales, "w2_s", nc.vector, nc.sync)
         idx2 = load_list(offs2, "idx2")
-        tab2_w = [load_words(page_bytes(U32, "tab2_w%d" % a, 1 - a), tab2_words[a]) for a in range(2)]
-        v2_s = gather(tab2_s, idx2, U8, "v2_s", "first")
+        tab2_w = [load_words(page_bytes(U32, "tab2_w%d" % a, a), tab2_words[a]) for a in range(2)]
+        v2_s = gather(tab2_s, idx2, U8, "v2_s")
         v2_w = [gather(tab2_w[a], idx2, U32, "v2_w%d" % a, offset=V2_WORDS + 4 * S * a) for a in range(2)]
         idx3 = load_list(offs3, "idx3")
         wg1_sb = load_weights(wg1, "wg1_sb")
@@ -369,14 +366,15 @@ def tile_list_two_phase_weave_kernel(
             else:
                 nc.scalar.activation(dst, src, COPY, scale=-1.0)
 
-        def turn_back(blocks_t, acc, grouped):
-            for slot in range(PACK):
-                b, u = divmod(slot, 2)
-                words = blocks_t[b][:].bitcast(F32)
-                nc.tensor.transpose(acc[:, slot * P : (slot + 1) * P], words[:, u * P : (u + 1) * P], ident[:])
-            nc.scalar.copy(
-                grouped[:].bitcast(F32).rearrange("p (b n u) -> p b n u", b=2, u=2),
-                acc[:].rearrange("p (b u n) -> p b n u", b=2, u=2),
+        def turn_back(blocks_t, acc, grouped, copy):
+            for b, block_t in enumerate(blocks_t):
+                words = block_t[:].bitcast(F32)
+                for u in range(2):
+                    slot = 2 * b + u
+                    nc.tensor.transpose(acc[:, slot * P : (slot + 1) * P], words[:, u * P : (u + 1) * P], ident[:])
+            copy(
+                grouped.bitcast(F32).rearrange("p (b n u) -> p b n u", n=P, u=2),
+                acc[:, : len(blocks_t) * COLS].rearrange("p (b u n) -> p b n u", n=P, u=2),
             )
 
         def depart(i, h, b):
@@ -397,18 +395,24 @@ def tile_list_two_phase_weave_kernel(
         def regroup(i, h):
             spot = grouped_offset(i, h)
             z_grouped[i, h] = placed.tile([P, HALF], BF16, name="z_grouped%d" % spot, offset=spot, align_bytes=64)
-            turn_back([z_t[i, h, b] for b in range(2)], next_bank(), z_grouped[i, h])
+            turn_back([z_t[i, h, b] for b in range(2)], next_bank(), z_grouped[i, h][:], nc.scalar.copy)
 
         def quantize_z(i, h, grouped):
             packed = half_of(page_q[i], h)
             nc.vector.quantize_mx(out=codes_of(packed), scales=scales_of(packed), in_=grouped[:])
 
         def quantize_page(i):
-            page_q[i] = ring.tile([P, 2 * PACKED], U32, name="page_q", bufs=2, align_bytes=64)
+            if i == LAST - 1:
+                page_q[i] = placed.tile([P, 2 * PACKED], U32, name="page_q_late", offset=LATE + 4 * BANK, align_bytes=64)
+            else:
+                page_q[i] = ring.tile([P, 2 * PACKED], U32, name="page_q", bufs=2, align_bytes=64)
             for h in range(2):
                 quantize_z(i, h, z_grouped[i, h])
-            for c in range(PACK):
-                nc.sync.dma_start(quadrant(z_q[i // PACK, c], place(i, c)), quadrant(page_q[i], c))
+            for cols in ([slice(0, PACKED), slice(PACKED, 2 * PACKED)] if i == LAST - 1 else [slice(0, 2 * PACKED)]):
+                for c in range(PACK):
+                    nc.sync.dma_start(
+                        quadrant(z_q[i // PACK, c][:, cols], place(i, c)), quadrant(page_q[i][:, cols], c)
+                    )
 
         def side_work(r):
             liq, dep, vap = r + 1, r - 1, r + 2
@@ -485,12 +489,12 @@ def tile_list_two_phase_weave_kernel(
             if i + 1 == LAST:
                 prepare_wo()
 
-        quantize_page(LAST - 1)
         round_wo(0, placed.tile([P, N, PACK], BF16, name="wo_grouped0", offset=LATE, align_bytes=64))
         quantize_wo(0)
         neg_h1_end = placed.tile([P, S - LAST_CUT], F32, name="neg_h1_end", offset=LATE + 4 * BANK)
         nc.scalar.activation(neg_h1_end[:], held[0][:, LAST_CUT - BANK :], COPY, scale=-1.0)
         scatter(LAST, idx3, neg_h1_end[:], wg1_sb, LAST_CUT, S)
+        quantize_page(LAST - 1)
 
         refs[LAST] = load_ref(LAST)
         first = list(range(TURN, HELD_BANK)) + [next_number() for k in range(2)]
@@ -502,16 +506,21 @@ def tile_list_two_phase_weave_kernel(
         for c in range(PACK):
             results[0, c] = bank(second[c])
             project(results[0, c], 0, 0, c)
+        for (h, b), acc in sums.items():
+            z_t[LAST, h, b] = z_t_tile()
+            turn_onto(acc, neg_pages[LAST], h, b, False)
+            round_z(acc, z_t[LAST, h, b], b == 1)
         for h in range(2):
-            blocks_t = [z_t_tile() for b in range(2)]
-            for b in range(2):
-                turn_onto(sums[h, b], neg_pages[LAST], h, b, False)
-                round_z(sums[h, b], blocks_t[b], b == 1)
+            blocks_t = [z_t[LAST, h, b] for b in range(2)]
             grouped = ring.tile([P, HALF], BF16, name="z_grouped_last", tag="liquid", bufs=4, align_bytes=64)
-            turn_back(blocks_t, bank(first[2 * h + 1]), grouped)
+            if h == 0:
+                for b, copy in enumerate((nc.scalar.copy, nc.vector.tensor_copy)):
+                    turn_back(blocks_t[b : b + 1], bank(first[b]), grouped[:, b * BANK : (b + 1) * BANK], copy)
+            else:
+                turn_back(blocks_t, bank(first[3]), grouped[:], nc.scalar.copy)
             if h == 1:
                 for c in range(PACK):
-                    results[1, c] = bank(first[(0, 2, 1, 3)[c]])
+                    results[1, c] = bank(first[(2, 0, 1, 3)[c]])
                     project(results[1, c], 0, 1, c)
             own = half_of(z_q[1, 0], h)
             for b in range(2):

@@ -30,12 +30,13 @@ COLS = 256
 PACKED = COLS + COLS // PACK
 HEAD_PAGES = 2
 W_COLS = HEAD_PAGES * P
-TURNED_PAGES = (0, 1, 2, 3)
+TURNED_PAGES = range(4)
 TURN = 5
-LAST_CUT = 640
 HELD_BANK = BANKS - 1
-LATE = 4 * 2 * HALF
-V2_WORDS = LATE + 4 * BANK + 8 * PACKED
+LAST_CUT = 640
+LATE_A = 4 * 2 * HALF
+LATE_B = LATE_A + 2 * N * PACK
+V2_WORDS = LATE_B + 4 * 2 * PACKED
 
 
 def tile_list_two_phase_weave_kernel(
@@ -73,27 +74,26 @@ def tile_list_two_phase_weave_kernel(
         def page_bytes(dtype, name, k):
             return ring.tile([P, T2], dtype, name=name, tag="page%d" % (k % 3), bufs=1, align_bytes=64)
 
-        def load_scales(src, name, clear_engine, queue, offset=None):
-            passes, width = src.shape[0], src.shape[2]
+        def sbuf_tile(shape, dtype, name, offset):
             if offset is None:
-                t = keep.tile([P, width], U8, name=name, align_bytes=64)
-            else:
-                t = placed.tile([P, width], U8, name=name, offset=offset, align_bytes=64)
-            clear_engine.memset(t[:].bitcast(I32), 0)
+                return keep.tile(shape, dtype, name=name, align_bytes=64)
+            return placed.tile(shape, dtype, name=name, offset=offset, align_bytes=64)
+
+        def quadrant(t, q):
+            return t[QUAD * q : QUAD * (q + 1), :].bitcast(I32)
+
+        def load_scales(src, name, queue, offset=None):
+            passes, width = src.shape[0], src.shape[2]
+            t = sbuf_tile([P, width], U8, name, offset)
+            nc.vector.memset(t[:].bitcast(I32), 0)
             for q in range(PACK):
                 queue.dma_start(
                     t[QUAD * q : QUAD * q + 4 * passes, :].bitcast(I32), src[:, 4 * q : 4 * q + 4, :].bitcast(I32)
                 )
             return t
 
-        def quadrant(t, q):
-            return t[QUAD * q : QUAD * (q + 1), :].bitcast(I32)
-
         def gather(window, lst, dtype, name, offset=None):
-            if offset is None:
-                t = keep.tile([P, S], dtype, name=name, align_bytes=64)
-            else:
-                t = placed.tile([P, S], dtype, name=name, offset=offset, align_bytes=64)
+            t = sbuf_tile([P, S], dtype, name, offset)
             nc.vector.tensor_copy(t[:], window[:].indirect(lst[:]))
             return t
 
@@ -138,18 +138,18 @@ def tile_list_two_phase_weave_kernel(
             return [load_words(tiles[a], w3_words[a, :, c0:c1, :]) for a in range(2)]
 
         idx = load_list(offs, "idx")
-        tab_s = keep.tile([P, T], U8, name="tab_s", tag="tab_s", align_bytes=64)
+        tab_s = keep.tile([P, T], U8, name="tab_s", align_bytes=64)
         for q in range(PACK):
             rows = tab_scales[:, 4 * q : 4 * q + 4, :].bitcast(I32)
             nc.sync.dma_start(quadrant(tab_s, q), rows.broadcast_to([QUAD // 4, 4, T // 4]))
         tab_w = load_words(page_bytes(U32, "tab_w", 2), tab_words[0])
-        tab2_s = load_scales(tab2_scales, "tab2_s", nc.vector, nc.gpsimd, V2_WORDS + 4 * S - T // 2)
+        tab2_s = load_scales(tab2_scales, "tab2_s", nc.gpsimd, V2_WORDS + 4 * S - T // 2)
         v_s = gather(tab_s, idx, U8, "v_s")
         v_w = gather(tab_w, idx, U32, "v_w")
         quantize_w1(0)
         w2_w = keep.tile([P, 2 * H], U8, name="w2_w", align_bytes=64)
         nc.sync.dma_start(w2_w[:].bitcast(I32), w2_words[0].bitcast(I32))
-        w2_s = load_scales(w2_scales, "w2_s", nc.vector, nc.sync)
+        w2_s = load_scales(w2_scales, "w2_s", nc.sync)
         idx2 = load_list(offs2, "idx2")
         tab2_w = [load_words(page_bytes(U32, "tab2_w%d" % a, a), tab2_words[a]) for a in range(2)]
         v2_s = gather(tab2_s, idx2, U8, "v2_s")
@@ -159,7 +159,7 @@ def tile_list_two_phase_weave_kernel(
         ident = keep.tile([P, P], F32, name="ident")
         make_identity(nc, ident[:])
         w3_head = load_w3(0, W_COLS, "w3_head")
-        w3_s = load_scales(w3_scales, "w3_s", nc.vector, nc.sync)
+        w3_s = load_scales(w3_scales, "w3_s", nc.sync)
         caps = {0: load_cap(0)}
         idx4 = load_list(offs4, "idx4")
         wg2_sb = load_weights(wg2, "wg2_sb")
@@ -172,7 +172,8 @@ def tile_list_two_phase_weave_kernel(
         def turn_sum(acc, sources):
             for k, src in enumerate(sources):
                 for b in range(PACK):
-                    turn(acc, b, src[:, b * P : (b + 1) * P], k == 0 and b == 0, k == len(sources) - 1 and b == PACK - 1)
+                    closes = k == len(sources) - 1 and b == PACK - 1
+                    turn(acc, b, src[:, b * P : (b + 1) * P], k == 0 and b == 0, closes)
 
         def gap_part(terms, sign):
             acc = next_bank()
@@ -248,12 +249,10 @@ def tile_list_two_phase_weave_kernel(
                 nc.scalar.copy(neg_a[i, s][:], acc[:])
 
         def liquid_gap(i, s):
-            if i not in TURNED_PAGES:
-                liquid_parts[i, s].append(gap_part([b_sb[i, s], neg_a[i, s]], 1.0))
+            liquid_parts[i, s].append(gap_part([b_sb[i, s], neg_a[i, s]], 1.0))
 
         def liquid_base(i, s):
-            if i not in TURNED_PAGES:
-                liquid_parts[i, s].append(base_part(neg_a[i, s], -1.0))
+            liquid_parts[i, s].append(base_part(neg_a[i, s], -1.0))
 
         def liquid_join(i, s):
             if s == 0:
@@ -382,7 +381,7 @@ def tile_list_two_phase_weave_kernel(
             if i not in refs:
                 refs[i] = load_ref(i)
             if i == LAST - 1 and h == 1:
-                z_t[i, h, b] = placed.tile([P, BANK], BF16, name="z_t_late%d" % b, offset=LATE + b * 4 * BANK)
+                z_t[i, h, b] = placed.tile([P, BANK], BF16, name="z_t_late%d" % b, offset=(LATE_A, LATE_B)[b])
             else:
                 z_t[i, h, b] = z_t_tile()
             turn_onto(acc, refs[i], h, b, True)
@@ -403,12 +402,14 @@ def tile_list_two_phase_weave_kernel(
 
         def quantize_page(i):
             if i == LAST - 1:
-                page_q[i] = placed.tile([P, 2 * PACKED], U32, name="page_q_late", offset=LATE + 4 * BANK, align_bytes=64)
+                page_q[i] = placed.tile([P, 2 * PACKED], U32, name="page_q_late", offset=LATE_B, align_bytes=64)
+                moves = [slice(0, PACKED), slice(PACKED, 2 * PACKED)]
             else:
-                page_q[i] = ring.tile([P, 2 * PACKED], U32, name="page_q", bufs=2, align_bytes=64)
+                page_q[i] = ring.tile([P, 2 * PACKED], U32, name="page_q", align_bytes=64)
+                moves = [slice(0, 2 * PACKED)]
             for h in range(2):
                 quantize_z(i, h, z_grouped[i, h])
-            for cols in ([slice(0, PACKED), slice(PACKED, 2 * PACKED)] if i == LAST - 1 else [slice(0, 2 * PACKED)]):
+            for cols in moves:
                 for c in range(PACK):
                     nc.sync.dma_start(
                         quadrant(z_q[i // PACK, c][:, cols], place(i, c)), quadrant(page_q[i][:, cols], c)
@@ -448,11 +449,13 @@ def tile_list_two_phase_weave_kernel(
                     start=(a == 0 and nh == 0), stop=(a == 1 and nh == 1),
                 )
 
-        def store(acc, h, c, copy):
+        def store(acc, h, c):
             result = ring.tile([P, 2, COLS], F32, name="result", tag=("parts_a", "parts_b")[c % 2], bufs=4)
-            copy(result[:].rearrange("p nh m -> p (nh m)"), acc[:])
             m0 = h * HALF + c * COLS
-            nc.sync.dma_start(out[:, m0 : m0 + COLS].rearrange("(nh p) m -> p nh m", p=P), result[:])
+            rows = out[:, m0 : m0 + COLS].rearrange("(nh p) m -> p nh m", p=P)
+            for nh0, nh1 in ([(0, 1), (1, 2)] if (h, c) in ((0, 0), (1, PACK - 1)) else [(0, 2)]):
+                nc.scalar.copy(result[:, nh0:nh1].rearrange("p nh m -> p (nh m)"), acc[:, nh0 * COLS : nh1 * COLS])
+                nc.sync.dma_start(rows[:, nh0:nh1], result[:, nh0:nh1])
 
         head = [
             (liquid_open, 0, 0), (liquid_close, 0, 0), (liquid_open, 0, 1), (liquid_close, 0, 1),
@@ -482,29 +485,29 @@ def tile_list_two_phase_weave_kernel(
                 quantize_page(i - 2)
                 cut = LAST_CUT if i == LAST else S
                 scatter(i, idx3, neg_h1[i][:, :cut], wg1_sb, 0, cut)
-            if 1 < i + 1 < H // W_COLS:
+            if 1 <= i < H // W_COLS - 1:
                 quantize_w1(i + 1)
+            if i == LAST - 1:
+                prepare_wo()
             if i >= 1:
                 side_work(i)
-            if i + 1 == LAST:
-                prepare_wo()
 
-        round_wo(0, placed.tile([P, N, PACK], BF16, name="wo_grouped0", offset=LATE, align_bytes=64))
+        round_wo(0, placed.tile([P, N, PACK], BF16, name="wo_grouped0", offset=LATE_A, align_bytes=64))
         quantize_wo(0)
-        neg_h1_end = placed.tile([P, S - LAST_CUT], F32, name="neg_h1_end", offset=LATE + 4 * BANK)
+        neg_h1_end = placed.tile([P, S - LAST_CUT], F32, name="neg_h1_end", offset=LATE_B)
         nc.scalar.activation(neg_h1_end[:], held[0][:, LAST_CUT - BANK :], COPY, scale=-1.0)
         scatter(LAST, idx3, neg_h1_end[:], wg1_sb, LAST_CUT, S)
         quantize_page(LAST - 1)
 
         refs[LAST] = load_ref(LAST)
-        first = list(range(TURN, HELD_BANK)) + [next_number() for k in range(2)]
-        second = [next_number() for k in range(PACK - 1)] + [HELD_BANK]
-        sums = {(h, b): bank(first[2 * h + b]) for h in range(2) for b in range(2)}
+        sum_banks = list(range(TURN, HELD_BANK)) + [next_number() for k in range(2)]
+        result_banks = [next_number() for k in range(PACK - 1)] + [HELD_BANK]
+        sums = {(h, b): bank(sum_banks[2 * h + b]) for h in range(2) for b in range(2)}
         for (h, b), acc in sums.items():
             turn_onto(acc, refs[LAST], h, b, True)
         results = {}
         for c in range(PACK):
-            results[0, c] = bank(second[c])
+            results[0, c] = bank(result_banks[c])
             project(results[0, c], 0, 0, c)
         for (h, b), acc in sums.items():
             z_t[LAST, h, b] = z_t_tile()
@@ -515,12 +518,11 @@ def tile_list_two_phase_weave_kernel(
             grouped = ring.tile([P, HALF], BF16, name="z_grouped_last", tag="liquid", bufs=4, align_bytes=64)
             if h == 0:
                 for b, copy in enumerate((nc.scalar.copy, nc.vector.tensor_copy)):
-                    turn_back(blocks_t[b : b + 1], bank(first[b]), grouped[:, b * BANK : (b + 1) * BANK], copy)
+                    turn_back(blocks_t[b : b + 1], bank(sum_banks[b]), grouped[:, b * BANK : (b + 1) * BANK], copy)
             else:
-                turn_back(blocks_t, bank(first[3]), grouped[:], nc.scalar.copy)
-            if h == 1:
-                for c in range(PACK):
-                    results[1, c] = bank(first[(2, 0, 1, 3)[c]])
+                turn_back(blocks_t, bank(sum_banks[3]), grouped[:], nc.scalar.copy)
+                for c, k in enumerate((2, 0, 1, 3)):
+                    results[1, c] = bank(sum_banks[k])
                     project(results[1, c], 0, 1, c)
             own = half_of(z_q[1, 0], h)
             for b in range(2):
@@ -533,4 +535,4 @@ def tile_list_two_phase_weave_kernel(
                 if c > 0:
                     nc.vector.tensor_copy(quadrant(half_of(z_q[1, c], h), c), quadrant(half_of(page_q[LAST], h), c))
                 project(results[h, c], 1, h, c)
-                store(results[h, c], h, c, nc.scalar.copy)
+                store(results[h, c], h, c)

@@ -37,6 +37,7 @@ LAST_CUT = 640
 LATE_A = 4 * 2 * HALF
 LATE_B = LATE_A + 2 * N * PACK
 V2_WORDS = LATE_B + 4 * 2 * PACKED
+WG1 = V2_WORDS + 2 * 4 * S
 
 
 def tile_list_two_phase_weave_kernel(
@@ -115,8 +116,8 @@ def tile_list_two_phase_weave_kernel(
                 out=w1_w[g][:].bitcast(FP8X4), scales=w1_s[g][:], in_=grouped[:].rearrange("p c j -> p (c j)")
             )
 
-        def load_weights(src, name):
-            t = keep.tile([P, S], F32, name=name)
+        def load_weights(src, name, offset=None):
+            t = sbuf_tile([P, S], F32, name, offset)
             nc.sync.dma_start(t[:], src)
             return t
 
@@ -155,7 +156,7 @@ def tile_list_two_phase_weave_kernel(
         v2_s = gather(tab2_s, idx2, U8, "v2_s")
         v2_w = [gather(tab2_w[a], idx2, U32, "v2_w%d" % a, offset=V2_WORDS + 4 * S * a) for a in range(2)]
         idx3 = load_list(offs3, "idx3")
-        wg1_sb = load_weights(wg1, "wg1_sb")
+        wg1_sb = load_weights(wg1, "wg1_sb", WG1)
         ident = keep.tile([P, P], F32, name="ident")
         make_identity(nc, ident[:])
         w3_head = load_w3(0, W_COLS, "w3_head")
@@ -324,7 +325,10 @@ def tile_list_two_phase_weave_kernel(
         wo_raw = []
         wo_last = [packed_tile("wo_last%d" % c, 1) for c in range(PACK - 1)] + [wo_q[1]]
         page_q = {LAST: packed_tile("page_q_last", 2)}
-        z_q = {(a, c): packed_tile("z_q%d%d" % (a, c), 2) for a in range(2) for c in range(PACK)}
+        z_q = {(a, c): packed_tile("z_q%d%d" % (a, c), a + 1) for a in range(2) for c in range(PACK)}
+        operand = {(a, h, c): half_of(z_q[a, c], h) for a in range(2) for h in range(a + 1) for c in range(PACK)}
+        joint_t = keep.tile([P, 2, PACK, BANK], BF16, name="joint_t")
+        joint_grouped = {}
 
         def quantize_wo(a):
             nc.vector.quantize_mx(
@@ -367,7 +371,7 @@ def tile_list_two_phase_weave_kernel(
 
         def turn_back(blocks_t, acc, grouped, copy):
             for b, block_t in enumerate(blocks_t):
-                words = block_t[:].bitcast(F32)
+                words = block_t.bitcast(F32)
                 for u in range(2):
                     slot = 2 * b + u
                     nc.tensor.transpose(acc[:, slot * P : (slot + 1) * P], words[:, u * P : (u + 1) * P], ident[:])
@@ -380,6 +384,14 @@ def tile_list_two_phase_weave_kernel(
             acc = next_bank()
             if i not in refs:
                 refs[i] = load_ref(i)
+            if i < PACK and h == 1:
+                turn_onto(acc, refs[i], h, b, True)
+                turn_onto(acc, neg_pages[i], h, b, False)
+                nc.scalar.activation(
+                    joint_t[:, b].rearrange("m c (u i q e) -> m i u c q e", u=2, i=PACK, e=2)[:, i],
+                    acc[:].rearrange("m (c q u e) -> m u c q e", c=PACK, u=2, e=2), COPY, scale=-1.0,
+                )
+                return
             if i == LAST - 1 and h == 1:
                 z_t[i, h, b] = placed.tile([P, BANK], BF16, name="z_t_late%d" % b, offset=(LATE_A, LATE_B)[b])
             else:
@@ -391,10 +403,21 @@ def tile_list_two_phase_weave_kernel(
         def grouped_offset(i, h):
             return (2 * ((LAST - i) % 2) + h) * 2 * HALF
 
+        def regroup_joint(c):
+            spot = V2_WORDS + c * 2 * HALF
+            joint_grouped[c] = placed.tile([P, HALF], BF16, name="joint_grouped%d" % c, offset=spot, align_bytes=64)
+            turn_back([joint_t[:, b, c] for b in range(2)], next_bank(), joint_grouped[c][:], nc.scalar.copy)
+
+        def quantize_joint(c):
+            late = operand[0, 1, c]
+            nc.vector.quantize_mx(out=codes_of(late), scales=scales_of(late), in_=joint_grouped[c][:])
+
         def regroup(i, h):
+            if i < PACK and h == 1:
+                return
             spot = grouped_offset(i, h)
             z_grouped[i, h] = placed.tile([P, HALF], BF16, name="z_grouped%d" % spot, offset=spot, align_bytes=64)
-            turn_back([z_t[i, h, b] for b in range(2)], next_bank(), z_grouped[i, h][:], nc.scalar.copy)
+            turn_back([z_t[i, h, b][:] for b in range(2)], next_bank(), z_grouped[i, h][:], nc.scalar.copy)
 
         def quantize_z(i, h, grouped):
             packed = half_of(page_q[i], h)
@@ -406,8 +429,8 @@ def tile_list_two_phase_weave_kernel(
                 moves = [slice(0, PACKED), slice(PACKED, 2 * PACKED)]
             else:
                 page_q[i] = ring.tile([P, 2 * PACKED], U32, name="page_q", align_bytes=64)
-                moves = [slice(0, 2 * PACKED)]
-            for h in range(2):
+                moves = [slice(0, (i // PACK + 1) * PACKED)]
+            for h in range(i // PACK + 1):
                 quantize_z(i, h, z_grouped[i, h])
             for cols in moves:
                 for c in range(PACK):
@@ -421,6 +444,8 @@ def tile_list_two_phase_weave_kernel(
             if liq not in TURNED_PAGES:
                 liquid += [(liquid_gap, liq, 0), (liquid_base, liq, 0), (liquid_gap, liq, 1), (liquid_base, liq, 1)]
             liquid += [(liquid_join, liq, 0)]
+            if r == LAST:
+                liquid = [(regroup_joint, c) for c in range(PACK)]
             steps = [
                 None, (vapour_join, liq, 1), None, None, None, None,
                 (depart, dep, 0, 0), None, (depart, dep, 0, 1), None, (depart, dep, 1, 0),
@@ -445,23 +470,24 @@ def tile_list_two_phase_weave_kernel(
                 nc.tensor.matmul_mx(
                     acc[:, nh * COLS : (nh + 1) * COLS],
                     lhsT=codes_of(wo_cols, nh * P, (nh + 1) * P), lhsT_scale=scales_of(wo_cols, nh * P, (nh + 1) * P),
-                    rhs=codes_of(half_of(z_q[a, c], h)), rhs_scale=scales_of(half_of(z_q[a, c], h)),
+                    rhs=codes_of(operand[a, h, c]), rhs_scale=scales_of(operand[a, h, c]),
                     start=(a == 0 and nh == 0), stop=(a == 1 and nh == 1),
                 )
 
         def store(acc, h, c):
             result = ring.tile([P, 2, COLS], F32, name="result", tag=("parts_a", "parts_b")[c % 2], bufs=4)
+            copy = nc.vector.tensor_copy if h == 1 and c >= 2 else nc.scalar.copy
             m0 = h * HALF + c * COLS
             rows = out[:, m0 : m0 + COLS].rearrange("(nh p) m -> p nh m", p=P)
             for nh0, nh1 in ([(0, 1), (1, 2)] if (h, c) in ((0, 0), (1, PACK - 1)) else [(0, 2)]):
-                nc.scalar.copy(result[:, nh0:nh1].rearrange("p nh m -> p (nh m)"), acc[:, nh0 * COLS : nh1 * COLS])
+                copy(result[:, nh0:nh1].rearrange("p nh m -> p (nh m)"), acc[:, nh0 * COLS : nh1 * COLS])
                 nc.sync.dma_start(rows[:, nh0:nh1], result[:, nh0:nh1])
 
         head = [
-            (liquid_open, 0, 0), (liquid_close, 0, 0), (liquid_open, 0, 1), (liquid_close, 0, 1),
-            (liquid_join, 0, 0), (liquid_open, 1, 0), (liquid_join, 0, 1),
-            (liquid_close, 1, 0), (liquid_open, 1, 1), (liquid_close, 1, 1),
-            (liquid_join, 1, 0), (vapour_product, 0, 0), (liquid_join, 1, 1), (vapour_product, 0, 1),
+            (liquid_open, 0, 0), (liquid_close, 0, 0), (liquid_open, 1, 0), (liquid_join, 0, 0),
+            (liquid_close, 1, 0), (liquid_open, 0, 1), (liquid_join, 1, 0),
+            (liquid_close, 0, 1), (liquid_open, 1, 1), (liquid_join, 0, 1), (liquid_close, 1, 1),
+            (vapour_product, 0, 0), (liquid_join, 1, 1), (vapour_product, 0, 1),
             (quantize_w1, 1), (vapour_gap, 0, 0), (vapour_base, 0, 0),
         ]
         for i in (1, 2):
@@ -475,7 +501,9 @@ def tile_list_two_phase_weave_kernel(
             step[0](*step[1:])
         for i in range(HEAD_PAGES):
             neg_pages.append(page_bytes(F32, "neg_page", i))
-            scatter(i, idx3, neg_h1[i][:], wg1_sb, 0, S)
+        for s in range(2):
+            for i in range(HEAD_PAGES):
+                scatter(i, idx3, neg_h1[i][:, s * BANK : (s + 1) * BANK], wg1_sb, s * BANK, (s + 1) * BANK)
 
         for i in range(PAGES):
             if i >= HEAD_PAGES:
@@ -513,26 +541,37 @@ def tile_list_two_phase_weave_kernel(
             z_t[LAST, h, b] = z_t_tile()
             turn_onto(acc, neg_pages[LAST], h, b, False)
             round_z(acc, z_t[LAST, h, b], b == 1)
+        grouped = [
+            placed.tile([P, HALF], BF16, name="z_grouped_last%d" % h, offset=(1 - h) * 2 * HALF, align_bytes=64)
+            for h in range(2)
+        ]
+        for (h, b), acc in sums.items():
+            block = grouped[h][:, b * BANK : (b + 1) * BANK]
+            turn_back([z_t[LAST, h, b][:]], bank(sum_banks[2 * h + b]), block, nc.scalar.copy)
+
+        late_first = placed.tile([P, 2 * PACKED], U32, name="z_q_late_first", offset=WG1, align_bytes=64)
+        late_rest = placed.tile([P, 2 * PACKED], U32, name="z_q_late_rest", offset=2 * HALF, align_bytes=64)
+        for c in range(PACK):
+            operand[0, 1, c] = half_of((late_first, late_rest)[c // 2], c % 2)
+        for c in range(2):
+            quantize_joint(c)
         for h in range(2):
-            blocks_t = [z_t[LAST, h, b] for b in range(2)]
-            grouped = ring.tile([P, HALF], BF16, name="z_grouped_last", tag="liquid", bufs=4, align_bytes=64)
-            if h == 0:
-                for b, copy in enumerate((nc.scalar.copy, nc.vector.tensor_copy)):
-                    turn_back(blocks_t[b : b + 1], bank(sum_banks[b]), grouped[:, b * BANK : (b + 1) * BANK], copy)
-            else:
-                turn_back(blocks_t, bank(sum_banks[3]), grouped[:], nc.scalar.copy)
-                for c, k in enumerate((2, 0, 1, 3)):
-                    results[1, c] = bank(sum_banks[k])
+            if h == 1:
+                for c in range(PACK):
+                    if c >= 2:
+                        quantize_joint(c)
+                    results[1, c] = bank(sum_banks[c])
                     project(results[1, c], 0, 1, c)
             own = half_of(z_q[1, 0], h)
             for b in range(2):
                 nc.vector.quantize_mx(
                     out=codes_of(own, b * P, (b + 1) * P)[:QUAD], scales=scales_of(own, b * P, (b + 1) * P)[:QUAD],
-                    in_=grouped[:QUAD, b * BANK : (b + 1) * BANK],
+                    in_=grouped[h][:QUAD, b * BANK : (b + 1) * BANK],
                 )
-            quantize_z(LAST, h, grouped)
+            quantize_z(LAST, h, grouped[h])
             for c in range(PACK):
                 if c > 0:
                     nc.vector.tensor_copy(quadrant(half_of(z_q[1, c], h), c), quadrant(half_of(page_q[LAST], h), c))
                 project(results[h, c], 1, h, c)
+            for c in range(PACK):
                 store(results[h, c], h, c)

@@ -83,10 +83,9 @@ def tile_list_two_phase_weave_kernel(
         def quadrant(t, q):
             return t[QUAD * q : QUAD * (q + 1), :].bitcast(I32)
 
-        def load_scales(src, name, queue, offset=None):
+        def load_scales(src, name, queue):
             passes, width = src.shape[0], src.shape[2]
-            t = sbuf_tile([P, width], U8, name, offset)
-            nc.vector.memset(t[:].bitcast(I32), 0)
+            t = keep.tile([P, width], U8, name=name, align_bytes=64)
             for q in range(PACK):
                 queue.dma_start(
                     t[QUAD * q : QUAD * q + 4 * passes, :].bitcast(I32), src[:, 4 * q : 4 * q + 4, :].bitcast(I32)
@@ -110,7 +109,10 @@ def tile_list_two_phase_weave_kernel(
         def quantize_w1(g):
             raw = ring.tile([P, PACK, W_COLS], F32, name="w1_raw", bufs=1)
             nc.sync.dma_start(raw[:], w1[:, g * W_COLS : (g + 1) * W_COLS].rearrange("(p j) c -> p j c", j=PACK))
-            grouped = ring.tile([P, W_COLS, PACK], BF16, name="w1_grouped", align_bytes=64)
+            if g == 0:
+                grouped = placed.tile([P, W_COLS, PACK], BF16, name="w1_first", offset=V2_WORDS, align_bytes=64)
+            else:
+                grouped = ring.tile([P, W_COLS, PACK], BF16, name="w1_grouped", align_bytes=64)
             round_rows(raw[:], grouped[:], -1.0)
             nc.vector.quantize_mx(
                 out=w1_w[g][:].bitcast(FP8X4), scales=w1_s[g][:], in_=grouped[:].rearrange("p c j -> p (c j)")
@@ -138,22 +140,39 @@ def tile_list_two_phase_weave_kernel(
             tiles = [keep.tile([P, c1 - c0], U32, name="%s%d" % (name, a), align_bytes=64) for a in range(2)]
             return [load_words(tiles[a], w3_words[a, :, c0:c1, :]) for a in range(2)]
 
+        def load_scale_rows(src, name, offset=None):
+            rows = src.rearrange("a q t -> (a q) t").bitcast(I32)
+            t = sbuf_tile([P, T], U8, name, offset)
+            nc.sync.dma_start(t[:].bitcast(I32), rows.unsqueeze(1).broadcast_to([rows.shape[0], P // rows.shape[0], T // 4]))
+            return t
+
+        def spread_scale_rows(gathered, passes, name, queue):
+            t = keep.tile([P, S], U8, name=name, align_bytes=64)
+            step = P // (16 * passes)
+            for a in range(passes):
+                for q in range(PACK):
+                    first = (16 * a + 4 * q) * step
+                    queue.dma_start(
+                        t[QUAD * q + 4 * a : QUAD * q + 4 * (a + 1), :].bitcast(I32),
+                        gathered[first : first + 4 * step : step, :].bitcast(I32),
+                    )
+            return t
+
         idx = load_list(offs, "idx")
-        tab_s = keep.tile([P, T], U8, name="tab_s", align_bytes=64)
-        for q in range(PACK):
-            rows = tab_scales[:, 4 * q : 4 * q + 4, :].bitcast(I32)
-            nc.sync.dma_start(quadrant(tab_s, q), rows.broadcast_to([QUAD // 4, 4, T // 4]))
+        tab_s = load_scale_rows(tab_scales, "tab_s")
+        idx2 = load_list(offs2, "idx2")
+        tab2_s = load_scale_rows(tab2_scales, "tab2_s", V2_WORDS + 4 * S - T // 2)
         tab_w = load_words(page_bytes(U32, "tab_w", 2), tab_words[0])
-        tab2_s = load_scales(tab2_scales, "tab2_s", nc.gpsimd, V2_WORDS + 4 * S - T // 2)
-        v_s = gather(tab_s, idx, U8, "v_s")
+        v_s_rows = gather(tab_s, idx, U8, "v_s_rows")
+        v2_s_rows = gather(tab2_s, idx2, U8, "v2_s_rows")
         v_w = gather(tab_w, idx, U32, "v_w")
         quantize_w1(0)
+        tab2_w = [load_words(page_bytes(U32, "tab2_w0", 0), tab2_words[0])]
         w2_w = keep.tile([P, 2 * H], U8, name="w2_w", align_bytes=64)
         nc.sync.dma_start(w2_w[:].bitcast(I32), w2_words[0].bitcast(I32))
-        w2_s = load_scales(w2_scales, "w2_s", nc.sync)
-        idx2 = load_list(offs2, "idx2")
-        tab2_w = [load_words(page_bytes(U32, "tab2_w%d" % a, a), tab2_words[a]) for a in range(2)]
-        v2_s = gather(tab2_s, idx2, U8, "v2_s")
+        w2_s = load_scales(w2_scales, "w2_s", nc.scalar)
+        v_s = spread_scale_rows(v_s_rows, 1, "v_s", nc.scalar)
+        tab2_w.append(load_words(page_bytes(U32, "tab2_w1", 1), tab2_words[1]))
         v2_w = [gather(tab2_w[a], idx2, U32, "v2_w%d" % a, offset=V2_WORDS + 4 * S * a) for a in range(2)]
         idx3 = load_list(offs3, "idx3")
         wg1_sb = load_weights(wg1, "wg1_sb", WG1)
@@ -161,6 +180,7 @@ def tile_list_two_phase_weave_kernel(
         make_identity(nc, ident[:])
         w3_head = load_w3(0, W_COLS, "w3_head")
         w3_s = load_scales(w3_scales, "w3_s", nc.sync)
+        v2_s = spread_scale_rows(v2_s_rows, 2, "v2_s", nc.sync)
         caps = {0: load_cap(0)}
         idx4 = load_list(offs4, "idx4")
         wg2_sb = load_weights(wg2, "wg2_sb")
@@ -231,7 +251,7 @@ def tile_list_two_phase_weave_kernel(
                 acc = cells_times(s, [w1_cols(i), w2_cols(i)])
                 lead_t = liquid_tile("lead_t")
                 nc.scalar.activation(lead_t[:], acc[:], RELU)
-                liquid_parts[i, s] = [lead_t]
+                liquid_parts.setdefault((i, s), []).append(lead_t)
             else:
                 acc = times_cells(s, *w2_cols(i))
                 b_sb[i, s] = liquid_tile("b_sb")
@@ -243,7 +263,7 @@ def tile_list_two_phase_weave_kernel(
                 acc = cells_times(s, [w1_cols(i)])
                 a_t = liquid_tile("a_t")
                 nc.scalar.activation(a_t[:], acc[:], COPY, scale=-1.0)
-                liquid_parts[i, s].append(a_t)
+                liquid_parts.setdefault((i, s), []).append(a_t)
             else:
                 acc = times_cells(s, *w1_cols(i))
                 neg_a[i, s] = ring.tile([P, BANK], F32, name="neg_a", tag="sums", bufs=4)
@@ -484,8 +504,8 @@ def tile_list_two_phase_weave_kernel(
                 nc.sync.dma_start(rows[:, nh0:nh1], result[:, nh0:nh1])
 
         head = [
-            (liquid_open, 0, 0), (liquid_close, 0, 0), (liquid_open, 1, 0), (liquid_join, 0, 0),
-            (liquid_close, 1, 0), (liquid_open, 0, 1), (liquid_join, 1, 0),
+            (liquid_open, 0, 0), (liquid_close, 0, 0), (liquid_close, 1, 0), (liquid_join, 0, 0),
+            (liquid_open, 1, 0), (liquid_open, 0, 1), (liquid_join, 1, 0),
             (liquid_close, 0, 1), (liquid_open, 1, 1), (liquid_join, 0, 1), (liquid_close, 1, 1),
             (vapour_product, 0, 0), (liquid_join, 1, 1), (vapour_product, 0, 1),
             (quantize_w1, 1), (vapour_gap, 0, 0), (vapour_base, 0, 0),

@@ -470,7 +470,7 @@ def tile_list_two_phase_weave_kernel(
                 None, (vapour_join, liq, 1), None, None, None, None,
                 (depart, dep, 0, 0), None, (depart, dep, 0, 1), None, (depart, dep, 1, 0),
                 (vapour_product, vap, 0), (depart, dep, 1, 1), None, (regroup, dep, 0),
-                (vapour_product, vap, 1), None, (regroup, dep, 1), (vapour_gap, vap, 0), (liquid_join, liq, 1),
+                None, (regroup, dep, 1), (liquid_join, liq, 1), (vapour_product, vap, 1), (vapour_gap, vap, 0),
                 (vapour_base, vap, 0), (vapour_gap, vap, 1), (vapour_base, vap, 1), (vapour_join, vap, 0),
             ]
             for step in steps:
@@ -507,15 +507,17 @@ def tile_list_two_phase_weave_kernel(
             (liquid_open, 0, 0), (liquid_close, 0, 0), (liquid_close, 1, 0), (liquid_join, 0, 0),
             (liquid_open, 1, 0), (liquid_open, 0, 1), (liquid_join, 1, 0),
             (liquid_close, 0, 1), (liquid_open, 1, 1), (liquid_join, 0, 1), (liquid_close, 1, 1),
-            (vapour_product, 0, 0), (liquid_join, 1, 1), (vapour_product, 0, 1),
-            (quantize_w1, 1), (vapour_gap, 0, 0), (vapour_base, 0, 0),
+            (vapour_product, 0, 0), (liquid_join, 1, 1),
         ]
-        for i in (1, 2):
+        for i in range(3):
             head += [
-                (vapour_product, i, 0), (vapour_gap, i - 1, 1), (vapour_base, i - 1, 1), (vapour_join, i - 1, 0),
-                (vapour_product, i, 1), (vapour_gap, i, 0), (vapour_join, i - 1, 1), (vapour_base, i, 0),
+                (vapour_product, i, 1), (vapour_gap, i, 0), (vapour_base, i, 0), (vapour_gap, i, 1),
+                (vapour_base, i, 1), (vapour_join, i, 0),
             ]
-        head += [(vapour_gap, 2, 1), (vapour_base, 2, 1), (vapour_join, 2, 0)]
+            if i < 2:
+                head += [(vapour_product, i + 1, 0), (vapour_join, i, 1)]
+            if i == 0:
+                head += [(quantize_w1, 1)]
         w3_rest = load_w3(W_COLS, H, "w3_rest")
         for step in head:
             step[0](*step[1:])
@@ -533,12 +535,12 @@ def tile_list_two_phase_weave_kernel(
                 quantize_page(i - 2)
                 cut = LAST_CUT if i == LAST else S
                 scatter(i, idx3, neg_h1[i][:, :cut], wg1_sb, 0, cut)
+            if i >= 1:
+                side_work(i)
             if 1 <= i < H // W_COLS - 1:
                 quantize_w1(i + 1)
             if i == LAST - 1:
                 prepare_wo()
-            if i >= 1:
-                side_work(i)
 
         round_wo(0, placed.tile([P, N, PACK], BF16, name="wo_grouped0", offset=LATE_A, align_bytes=64))
         quantize_wo(0)

@@ -36,7 +36,8 @@ HELD_BANK = BANKS - 1
 LAST_CUT = 640
 LATE_A = 4 * 2 * HALF
 LATE_B = LATE_A + 2 * N * PACK
-V2_WORDS = LATE_B + 4 * 2 * PACKED
+V2_ROWS = LATE_B + 4 * 2 * PACKED
+V2_WORDS = V2_ROWS + S
 WG1 = V2_WORDS + 2 * 4 * S
 
 
@@ -110,7 +111,7 @@ def tile_list_two_phase_weave_kernel(
             raw = ring.tile([P, PACK, W_COLS], F32, name="w1_raw", bufs=1)
             nc.sync.dma_start(raw[:], w1[:, g * W_COLS : (g + 1) * W_COLS].rearrange("(p j) c -> p j c", j=PACK))
             if g == 0:
-                grouped = placed.tile([P, W_COLS, PACK], BF16, name="w1_first", offset=V2_WORDS, align_bytes=64)
+                grouped = placed.tile([P, W_COLS, PACK], BF16, name="w1_first", offset=V2_ROWS, align_bytes=64)
             else:
                 grouped = ring.tile([P, W_COLS, PACK], BF16, name="w1_grouped", align_bytes=64)
             round_rows(raw[:], grouped[:], -1.0)
@@ -140,39 +141,24 @@ def tile_list_two_phase_weave_kernel(
             tiles = [keep.tile([P, c1 - c0], U32, name="%s%d" % (name, a), align_bytes=64) for a in range(2)]
             return [load_words(tiles[a], w3_words[a, :, c0:c1, :]) for a in range(2)]
 
-        def load_scale_rows(src, name, offset=None):
-            rows = src.rearrange("a q t -> (a q) t").bitcast(I32)
-            t = sbuf_tile([P, T], U8, name, offset)
-            nc.sync.dma_start(t[:].bitcast(I32), rows.unsqueeze(1).broadcast_to([rows.shape[0], P // rows.shape[0], T // 4]))
-            return t
-
-        def spread_scale_rows(gathered, passes, name, queue):
-            t = keep.tile([P, S], U8, name=name, align_bytes=64)
-            step = P // (16 * passes)
-            for a in range(passes):
-                for q in range(PACK):
-                    first = (16 * a + 4 * q) * step
-                    queue.dma_start(
-                        t[QUAD * q + 4 * a : QUAD * q + 4 * (a + 1), :].bitcast(I32),
-                        gathered[first : first + 4 * step : step, :].bitcast(I32),
-                    )
-            return t
-
         idx = load_list(offs, "idx")
-        tab_s = load_scale_rows(tab_scales, "tab_s")
-        idx2 = load_list(offs2, "idx2")
-        tab2_s = load_scale_rows(tab2_scales, "tab2_s", V2_WORDS + 4 * S - T // 2)
+        tab_s = keep.tile([P, T], U8, name="tab_s", align_bytes=64)
+        for q in range(PACK):
+            rows = tab_scales[:, 4 * q : 4 * q + 4, :].bitcast(I32)
+            (nc.sync, nc.scalar)[q // 2].dma_start(quadrant(tab_s, q), rows.broadcast_to([QUAD // 4, 4, T // 4]))
         tab_w = load_words(page_bytes(U32, "tab_w", 2), tab_words[0])
-        v_s_rows = gather(tab_s, idx, U8, "v_s_rows")
-        v2_s_rows = gather(tab2_s, idx2, U8, "v2_s_rows")
+        v_s = gather(tab_s, idx, U8, "v_s")
         v_w = gather(tab_w, idx, U32, "v_w")
         quantize_w1(0)
-        tab2_w = [load_words(page_bytes(U32, "tab2_w0", 0), tab2_words[0])]
+        idx2 = load_list(offs2, "idx2")
+        tab2_s = placed.tile([P, T], U8, name="tab2_s", offset=V2_WORDS + 4 * S - T // 2, align_bytes=64)
+        rows = tab2_scales.rearrange("a q t -> (a q) t").bitcast(I32).unsqueeze(1)
+        nc.sync.dma_start(tab2_s[:].bitcast(I32), rows.broadcast_to([QUAD, PACK, T // 4]))
         w2_w = keep.tile([P, 2 * H], U8, name="w2_w", align_bytes=64)
         nc.sync.dma_start(w2_w[:].bitcast(I32), w2_words[0].bitcast(I32))
         w2_s = load_scales(w2_scales, "w2_s", nc.scalar)
-        v_s = spread_scale_rows(v_s_rows, 1, "v_s", nc.scalar)
-        tab2_w.append(load_words(page_bytes(U32, "tab2_w1", 1), tab2_words[1]))
+        v2_s_rows = gather(tab2_s, idx2, U8, "v2_s_rows", V2_ROWS)
+        tab2_w = [load_words(page_bytes(U32, "tab2_w%d" % a, a), tab2_words[a]) for a in range(2)]
         v2_w = [gather(tab2_w[a], idx2, U32, "v2_w%d" % a, offset=V2_WORDS + 4 * S * a) for a in range(2)]
         idx3 = load_list(offs3, "idx3")
         wg1_sb = load_weights(wg1, "wg1_sb", WG1)
@@ -180,7 +166,14 @@ def tile_list_two_phase_weave_kernel(
         make_identity(nc, ident[:])
         w3_head = load_w3(0, W_COLS, "w3_head")
         w3_s = load_scales(w3_scales, "w3_s", nc.sync)
-        v2_s = spread_scale_rows(v2_s_rows, 2, "v2_s", nc.sync)
+        v2_s = keep.tile([P, S], U8, name="v2_s", align_bytes=64)
+        for a in range(2):
+            for q in range(PACK):
+                first = 64 * a + 16 * q
+                nc.sync.dma_start(
+                    v2_s[QUAD * q + 4 * a : QUAD * q + 4 * (a + 1), :].bitcast(I32),
+                    v2_s_rows[first : first + 16 : 4, :].bitcast(I32),
+                )
         caps = {0: load_cap(0)}
         idx4 = load_list(offs4, "idx4")
         wg2_sb = load_weights(wg2, "wg2_sb")
@@ -504,7 +497,7 @@ def tile_list_two_phase_weave_kernel(
                 nc.sync.dma_start(rows[:, nh0:nh1], result[:, nh0:nh1])
 
         head = [
-            (liquid_open, 0, 0), (liquid_close, 0, 0), (liquid_close, 1, 0), (liquid_join, 0, 0),
+            (liquid_close, 0, 0), (liquid_open, 0, 0), (liquid_close, 1, 0), (liquid_join, 0, 0),
             (liquid_open, 1, 0), (liquid_open, 0, 1), (liquid_join, 1, 0),
             (liquid_close, 0, 1), (liquid_open, 1, 1), (liquid_join, 0, 1), (liquid_close, 1, 1),
             (vapour_product, 0, 0), (liquid_join, 1, 1),

@@ -28,17 +28,32 @@ LAST = PAGES - 1
 HALF = T2 // 2
 COLS = 256
 PACKED = COLS + COLS // PACK
-HEAD_PAGES = 2
-W_COLS = HEAD_PAGES * P
+W_COLS = 2 * P
 TURNED_PAGES = range(4)
 TURN = 5
 HELD_BANK = BANKS - 1
 LAST_CUT = 640
-LATE_A = 4 * 2 * HALF
-LATE_B = LATE_A + 2 * N * PACK
-V2_ROWS = LATE_B + 4 * 2 * PACKED
+UNIT = 2 * QUAD
+STAGE_UNITS = 38
+
+REF = 0
+V2_ROWS = REF + 3 * 4 * T2
 V2_WORDS = V2_ROWS + S
-WG1 = V2_WORDS + 2 * 4 * S
+W3 = V2_WORDS + 2 * 4 * S
+LATE = W3 + 2 * 4 * H
+V_WORDS = LATE + 4 * S
+W1_WORDS = V_WORDS + 4 * S
+W2_WORDS = W1_WORDS + 4 * H
+W1_SCALES = W2_WORDS + 2 * H
+RAW = W1_SCALES + H
+STAGE = RAW + 4 * 2 * PACK * N
+
+
+def weave(*chains):
+    steps = []
+    for k in range(max(len(chain) for chain in chains)):
+        steps += [chain[k] for chain in chains if k < len(chain)]
+    return steps
 
 
 def tile_list_two_phase_weave_kernel(
@@ -64,6 +79,15 @@ def tile_list_two_phase_weave_kernel(
         def next_bank():
             return bank(next_number())
 
+        def at(offset, shape, dtype, name):
+            return placed.tile(shape, dtype, name=name, offset=offset, align_bytes=64)
+
+        def kept(shape, dtype, name):
+            return keep.tile(shape, dtype, name=name, align_bytes=64)
+
+        def quadrant(t, q):
+            return t[QUAD * q : QUAD * (q + 1), :].bitcast(I32)
+
         def load_list(src, name):
             t = keep.tile([P, S // 16], U16, name=name)
             nc.sync.dma_start(t[:], src)
@@ -76,97 +100,90 @@ def tile_list_two_phase_weave_kernel(
         def page_bytes(dtype, name, k):
             return ring.tile([P, T2], dtype, name=name, tag="page%d" % (k % 3), bufs=1, align_bytes=64)
 
-        def sbuf_tile(shape, dtype, name, offset):
-            if offset is None:
-                return keep.tile(shape, dtype, name=name, align_bytes=64)
-            return placed.tile(shape, dtype, name=name, offset=offset, align_bytes=64)
-
-        def quadrant(t, q):
-            return t[QUAD * q : QUAD * (q + 1), :].bitcast(I32)
-
         def load_scales(src, name, queue):
             passes, width = src.shape[0], src.shape[2]
-            t = keep.tile([P, width], U8, name=name, align_bytes=64)
+            t = kept([P, width], U8, name)
             for q in range(PACK):
                 queue.dma_start(
                     t[QUAD * q : QUAD * q + 4 * passes, :].bitcast(I32), src[:, 4 * q : 4 * q + 4, :].bitcast(I32)
                 )
             return t
 
-        def gather(window, lst, dtype, name, offset=None):
-            t = sbuf_tile([P, S], dtype, name, offset)
+        def gather(t, window, lst):
             nc.vector.tensor_copy(t[:], window[:].indirect(lst[:]))
             return t
 
-        def round_rows(raw, grouped, sign):
+        def round_rows(raw, grouped):
             nc.scalar.activation(
                 grouped.rearrange("p (c i) j -> p c j i", i=4), raw.rearrange("p j (c i) -> p c j i", i=4),
-                COPY, scale=sign,
+                COPY, scale=-1.0,
             )
 
-        w1_w = [keep.tile([P, W_COLS], U32, name="w1_w%d" % g, align_bytes=64) for g in range(H // W_COLS)]
-        w1_s = [keep.tile([P, W_COLS], U8, name="w1_s%d" % g, align_bytes=64) for g in range(H // W_COLS)]
+        w1_w = [at(W1_WORDS + 4 * W_COLS * g, [P, W_COLS], U32, "w1_w%d" % g) for g in range(H // W_COLS)]
+        w1_s = [at(W1_SCALES + W_COLS * g, [P, W_COLS], U8, "w1_s%d" % g) for g in range(H // W_COLS)]
+        w1_raw = {}
+
+        def load_w1(g):
+            w1_raw[g] = at(RAW, [P, PACK, W_COLS], F32, "w1_raw%d" % g)
+            nc.sync.dma_start(
+                w1_raw[g][:], w1[:, g * W_COLS : (g + 1) * W_COLS].rearrange("(p j) c -> p j c", j=PACK)
+            )
 
         def quantize_w1(g):
-            raw = ring.tile([P, PACK, W_COLS], F32, name="w1_raw", bufs=1)
-            nc.sync.dma_start(raw[:], w1[:, g * W_COLS : (g + 1) * W_COLS].rearrange("(p j) c -> p j c", j=PACK))
-            if g == 0:
-                grouped = placed.tile([P, W_COLS, PACK], BF16, name="w1_first", offset=V2_ROWS, align_bytes=64)
-            else:
-                grouped = ring.tile([P, W_COLS, PACK], BF16, name="w1_grouped", align_bytes=64)
-            round_rows(raw[:], grouped[:], -1.0)
+            if g not in w1_raw:
+                load_w1(g)
+            spot = V2_ROWS if g == 0 else RAW + 4 * PACK * W_COLS + 2 * PACK * W_COLS * (g % 2)
+            grouped = at(spot, [P, W_COLS, PACK], BF16, "w1_grouped%d" % g)
+            round_rows(w1_raw[g][:], grouped[:])
             nc.vector.quantize_mx(
                 out=w1_w[g][:].bitcast(FP8X4), scales=w1_s[g][:], in_=grouped[:].rearrange("p c j -> p (c j)")
             )
 
-        def load_weights(src, name, offset=None):
-            t = sbuf_tile([P, S], F32, name, offset)
-            nc.sync.dma_start(t[:], src)
-            return t
-
         def load_cap(i):
-            if i == LAST:
-                t = ring.tile([P, S], F32, name="cap_last", tag="late", bufs=1, align_bytes=64)
-            else:
-                t = ring.tile([P, S], F32, name="cap_rows", bufs=3)
+            t = ring.tile([P, S], F32, name="cap_rows", bufs=3)
             nc.sync.dma_start(t[:], cap[i * P : (i + 1) * P, :])
             return t
 
+        def ref_spot(i):
+            return REF + 4 * T2 * (i % 3)
+
         def load_ref(i):
-            t = ring.tile([P, T2], F32, name="ref_rows", tag="rows_2k", bufs=4)
+            t = at(ref_spot(i), [P, T2], F32, "ref_rows%d" % i)
             nc.sync.dma_start(t[:], ref[i * P : (i + 1) * P, :])
             return t
 
-        def load_w3(c0, c1, name):
-            tiles = [keep.tile([P, c1 - c0], U32, name="%s%d" % (name, a), align_bytes=64) for a in range(2)]
+        def load_w3(c0, c1):
+            tiles = [at(W3 + 8 * c0 + 4 * (c1 - c0) * a, [P, c1 - c0], U32, "w3_%d_%d" % (c0, a)) for a in range(2)]
             return [load_words(tiles[a], w3_words[a, :, c0:c1, :]) for a in range(2)]
 
         idx = load_list(offs, "idx")
-        tab_s = keep.tile([P, T], U8, name="tab_s", align_bytes=64)
+        tab_s = kept([P, T], U8, "tab_s")
         for q in range(PACK):
             rows = tab_scales[:, 4 * q : 4 * q + 4, :].bitcast(I32)
             (nc.sync, nc.scalar)[q // 2].dma_start(quadrant(tab_s, q), rows.broadcast_to([QUAD // 4, 4, T // 4]))
         tab_w = load_words(page_bytes(U32, "tab_w", 2), tab_words[0])
-        v_s = gather(tab_s, idx, U8, "v_s")
-        v_w = gather(tab_w, idx, U32, "v_w")
+        v_s = gather(kept([P, S], U8, "v_s"), tab_s, idx)
+        v_w = gather(at(V_WORDS, [P, S], U32, "v_w"), tab_w, idx)
         quantize_w1(0)
         idx2 = load_list(offs2, "idx2")
-        tab2_s = placed.tile([P, T], U8, name="tab2_s", offset=V2_WORDS + 4 * S - T // 2, align_bytes=64)
+        tab2_s = at(V2_WORDS + 4 * S - T // 2, [P, T], U8, "tab2_s")
         rows = tab2_scales.rearrange("a q t -> (a q) t").bitcast(I32).unsqueeze(1)
         nc.sync.dma_start(tab2_s[:].bitcast(I32), rows.broadcast_to([QUAD, PACK, T // 4]))
-        w2_w = keep.tile([P, 2 * H], U8, name="w2_w", align_bytes=64)
+        w2_w = at(W2_WORDS, [P, 2 * H], U8, "w2_w")
         nc.sync.dma_start(w2_w[:].bitcast(I32), w2_words[0].bitcast(I32))
         w2_s = load_scales(w2_scales, "w2_s", nc.scalar)
-        v2_s_rows = gather(tab2_s, idx2, U8, "v2_s_rows", V2_ROWS)
+        v2_s_rows = gather(at(V2_ROWS, [P, S], U8, "v2_s_rows"), tab2_s, idx2)
         tab2_w = [load_words(page_bytes(U32, "tab2_w%d" % a, a), tab2_words[a]) for a in range(2)]
-        v2_w = [gather(tab2_w[a], idx2, U32, "v2_w%d" % a, offset=V2_WORDS + 4 * S * a) for a in range(2)]
+        v2_w = [gather(at(V2_WORDS + 4 * S * a, [P, S], U32, "v2_w%d" % a), tab2_w[a], idx2) for a in range(2)]
         idx3 = load_list(offs3, "idx3")
-        wg1_sb = load_weights(wg1, "wg1_sb", WG1)
+        wg1_sb = at(LATE, [P, S], F32, "wg1_sb")
+        nc.sync.dma_start(wg1_sb[:], wg1)
         ident = keep.tile([P, P], F32, name="ident")
         make_identity(nc, ident[:])
-        w3_head = load_w3(0, W_COLS, "w3_head")
+        load_w1(1)
+        w3_head = load_w3(0, W_COLS)
         w3_s = load_scales(w3_scales, "w3_s", nc.sync)
-        v2_s = keep.tile([P, S], U8, name="v2_s", align_bytes=64)
+        v2_s = kept([P, S], U8, "v2_s")
         for a in range(2):
             for q in range(PACK):
                 first = 64 * a + 16 * q
@@ -176,7 +193,9 @@ def tile_list_two_phase_weave_kernel(
                 )
         caps = {0: load_cap(0)}
         idx4 = load_list(offs4, "idx4")
-        wg2_sb = load_weights(wg2, "wg2_sb")
+        wg2_sb = kept([P, S], F32, "wg2_sb")
+        nc.sync.dma_start(wg2_sb[:], wg2)
+        w3_rest = load_w3(W_COLS, H)
 
         def turn(acc, slot, src, start, stop):
             nc.tensor.matmul(
@@ -202,6 +221,15 @@ def tile_list_two_phase_weave_kernel(
             base_t = ring.tile([P, BANK], F32, name="base_t", tag="parts_b", bufs=4)
             nc.scalar.activation(base_t[:], acc[:], COPY, scale=sign)
             return base_t
+
+        neg_pages = {}
+
+        def scatter(i, lst, values, weights, j0, j1):
+            if i not in neg_pages:
+                neg_pages[i] = page_bytes(F32, "neg_page", i)
+            nc.vector.tensor_tensor(
+                neg_pages[i][:].indirect(lst[:, j0 // 16 : j1 // 16]), values, weights[:, j0:j1], ALU.mult
+            )
 
         neg_h1 = {}
         liquid_parts = {}
@@ -278,6 +306,16 @@ def tile_list_two_phase_weave_kernel(
             nc.scalar.activation(neg_h1[i][:, s * BANK : s * BANK + width], both[:, :width], COPY, scale=-1.0)
             if very_last:
                 held.append(both)
+            if i >= 2 and s == 1:
+                cut = BANK + width
+                scatter(i, idx3, neg_h1[i][:, :cut], wg1_sb, 0, cut)
+
+        def liquid(i):
+            names = [liquid_open, liquid_close]
+            steps = [(f, i, s) for s in range(2) for f in names]
+            if i not in TURNED_PAGES:
+                steps += [(f, i, s) for s in range(2) for f in (liquid_gap, liquid_base)]
+            return steps + [(liquid_join, i, s) for s in range(2)]
 
         neg_h2 = {}
         neg_sum = {}
@@ -285,13 +323,11 @@ def tile_list_two_phase_weave_kernel(
 
         def vapour_product(i, s):
             cells = slice(s * BANK, (s + 1) * BANK)
-            if s == 0:
-                neg_h2[i] = ring.tile([P, S], F32, name="neg_h2", bufs=3)
-                if i not in caps:
-                    caps[i] = load_cap(i)
+            if i not in caps:
+                caps[i] = load_cap(i)
             acc = next_bank()
             for a in range(2):
-                if i < HEAD_PAGES:
+                if i * P < W_COLS:
                     w3_cols = w3_head[a][:, i * P : (i + 1) * P]
                 else:
                     w3_cols = w3_rest[a][:, i * P - W_COLS : (i + 1) * P - W_COLS]
@@ -310,21 +346,30 @@ def tile_list_two_phase_weave_kernel(
             vapour_parts[i, s].append(base_part(neg_sum[i, s], 1.0))
 
         def vapour_join(i, s):
+            if s == 0:
+                neg_h2[i] = ring.tile([P, S], F32, name="neg_h2", bufs=3)
             both = next_bank()
             turn_sum(both, vapour_parts[i, s])
             nc.scalar.copy(neg_h2[i][:, s * BANK : (s + 1) * BANK], both[:])
+            if s == 1:
+                scatter(i, idx4, neg_h2[i][:], wg2_sb, 0, S)
 
-        def packed_tile(name, halves):
-            return keep.tile([P, halves * PACKED], U32, name=name, align_bytes=64)
+        def vapour(i):
+            steps = [(vapour_product, i, s) for s in range(2)]
+            steps += [(f, i, s) for s in range(2) for f in (vapour_gap, vapour_base)]
+            return steps + [(vapour_join, i, s) for s in range(2)]
 
-        def half_of(t, h):
-            return t[:, h * PACKED : (h + 1) * PACKED]
+        def part_of(t, k):
+            return t[:, k * PACKED : (k + 1) * PACKED]
 
         def codes_of(t, c0=0, c1=COLS):
             return t[:, c0:c1].bitcast(FP8X4)
 
         def scales_of(t, c0=0, c1=COLS):
             return t[:, COLS:].bitcast(U8)[:, c0:c1]
+
+        def quantize(packed, grouped):
+            nc.vector.quantize_mx(out=codes_of(packed), scales=scales_of(packed), in_=grouped)
 
         def place(i, c):
             if i == LAST:
@@ -333,149 +378,67 @@ def tile_list_two_phase_weave_kernel(
                 return PACK - 1
             return i % PACK
 
-        wo_q = [packed_tile("wo_q%d" % a, 1) for a in range(2)]
-        wo_grouped = {}
+        wo_q = [kept([P, PACKED], U32, "wo_q%d" % a) for a in range(2)]
+        wo_last = [kept([P, PACKED], U32, "wo_last%d" % c) for c in range(PACK - 1)] + [wo_q[1]]
         wo_raw = []
-        wo_last = [packed_tile("wo_last%d" % c, 1) for c in range(PACK - 1)] + [wo_q[1]]
-        page_q = {LAST: packed_tile("page_q_last", 2)}
-        z_q = {(a, c): packed_tile("z_q%d%d" % (a, c), a + 1) for a in range(2) for c in range(PACK)}
-        operand = {(a, h, c): half_of(z_q[a, c], h) for a in range(2) for h in range(a + 1) for c in range(PACK)}
-        joint_t = keep.tile([P, 2, PACK, BANK], BF16, name="joint_t")
-        joint_grouped = {}
+
+        def load_wo():
+            wo_raw.append(at(RAW, [P, 2, PACK, N], F32, "wo_raw"))
+            nc.sync.dma_start(wo_raw[0][:], wo.rearrange("(a p j) n -> p a j n", a=2, j=PACK))
 
         def quantize_wo(a):
-            nc.vector.quantize_mx(
-                out=codes_of(wo_q[a]), scales=scales_of(wo_q[a]), in_=wo_grouped[a].rearrange("p n j -> p (n j)")
-            )
+            grouped = at(ref_spot(LAST - 1 - a), [P, N, PACK], BF16, "wo_grouped%d" % a)
+            round_rows(wo_raw[0][:, a], grouped[:])
+            quantize(wo_q[a][:], grouped[:].rearrange("p n j -> p (n j)"))
+            if a == 1:
+                for c in range(PACK - 1):
+                    for q in range(PACK):
+                        nc.sync.dma_start(quadrant(wo_last[c], place(PACK + q, c)), quadrant(wo_q[1], q))
 
-        def round_wo(a, grouped):
-            wo_grouped[a] = grouped[:]
-            round_rows(wo_raw[0][:, a], grouped[:], 1.0)
-
-        def prepare_wo():
-            wo_raw.append(ring.tile([P, 2, PACK, N], F32, name="wo_raw", tag="rows_2k", bufs=4))
-            nc.sync.dma_start(wo_raw[0][:], wo.rearrange("(a p j) n -> p a j n", a=2, j=PACK))
-            round_wo(1, ring.tile([P, N, PACK], BF16, name="wo_grouped1", tag="late", bufs=1, align_bytes=64))
-            quantize_wo(1)
-            for c in range(PACK - 1):
-                for q in range(PACK):
-                    nc.sync.dma_start(quadrant(wo_last[c], place(PACK + q, c)), quadrant(wo_q[1], q))
-
-        neg_pages = []
         refs = {}
-        z_t = {}
-        z_grouped = {}
+        stage_spot = {(h, d): STAGE + 2 * STAGE_UNITS * UNIT * (2 * h + d) for h in range(2) for d in range(2)}
+        stage = {key: at(spot, [P, STAGE_UNITS, UNIT], BF16, "stage%d%d" % key) for key, spot in stage_spot.items()}
+        grouped_z = {}
+        operand = {(0, 0, c): kept([P, PACKED], U32, "z_q00%d" % c)[:] for c in range(PACK)}
 
-        def turn_onto(acc, src, h, b, opens):
-            for c in range(PACK):
-                m0 = h * HALF + c * COLS + b * P
-                turn(acc, c, src[:, m0 : m0 + P], opens and c == 0, not opens and c == PACK - 1)
-
-        def z_t_tile():
-            return ring.tile([P, BANK], BF16, name="z_t", bufs=8)
-
-        def round_z(acc, dst, on_vector):
-            dst = dst[:].rearrange("m (u cq e) -> m u cq e", u=2, e=2)
-            src = acc[:].rearrange("m (cq u e) -> m u cq e", u=2, e=2)
-            if on_vector:
-                nc.vector.tensor_scalar_mul(dst, src, -1.0)
-            else:
-                nc.scalar.activation(dst, src, COPY, scale=-1.0)
-
-        def turn_back(blocks_t, acc, grouped, copy):
-            for b, block_t in enumerate(blocks_t):
-                words = block_t.bitcast(F32)
-                for u in range(2):
-                    slot = 2 * b + u
-                    nc.tensor.transpose(acc[:, slot * P : (slot + 1) * P], words[:, u * P : (u + 1) * P], ident[:])
-            copy(
-                grouped.bitcast(F32).rearrange("p (b n u) -> p b n u", n=P, u=2),
-                acc[:, : len(blocks_t) * COLS].rearrange("p (b u n) -> p b n u", n=P, u=2),
-            )
-
-        def depart(i, h, b):
+        def depart(i, h, d):
             acc = next_bank()
             if i not in refs:
                 refs[i] = load_ref(i)
-            if i < PACK and h == 1:
-                turn_onto(acc, refs[i], h, b, True)
-                turn_onto(acc, neg_pages[i], h, b, False)
-                nc.scalar.activation(
-                    joint_t[:, b].rearrange("m c (u i q e) -> m i u c q e", u=2, i=PACK, e=2)[:, i],
-                    acc[:].rearrange("m (c q u e) -> m u c q e", c=PACK, u=2, e=2), COPY, scale=-1.0,
-                )
-                return
-            if i == LAST - 1 and h == 1:
-                z_t[i, h, b] = placed.tile([P, BANK], BF16, name="z_t_late%d" % b, offset=(LATE_A, LATE_B)[b])
-            else:
-                z_t[i, h, b] = z_t_tile()
-            turn_onto(acc, refs[i], h, b, True)
-            turn_onto(acc, neg_pages[i], h, b, False)
-            round_z(acc, z_t[i, h, b], False)
-
-        def grouped_offset(i, h):
-            return (2 * ((LAST - i) % 2) + h) * 2 * HALF
-
-        def regroup_joint(c):
-            spot = V2_WORDS + c * 2 * HALF
-            joint_grouped[c] = placed.tile([P, HALF], BF16, name="joint_grouped%d" % c, offset=spot, align_bytes=64)
-            turn_back([joint_t[:, b, c] for b in range(2)], next_bank(), joint_grouped[c][:], nc.scalar.copy)
-
-        def quantize_joint(c):
-            late = operand[0, 1, c]
-            nc.vector.quantize_mx(out=codes_of(late), scales=scales_of(late), in_=joint_grouped[c][:])
-
-        def regroup(i, h):
-            if i < PACK and h == 1:
-                return
-            spot = grouped_offset(i, h)
-            z_grouped[i, h] = placed.tile([P, HALF], BF16, name="z_grouped%d" % spot, offset=spot, align_bytes=64)
-            turn_back([z_t[i, h, b][:] for b in range(2)], next_bank(), z_grouped[i, h][:], nc.scalar.copy)
-
-        def quantize_z(i, h, grouped):
-            packed = half_of(page_q[i], h)
-            nc.vector.quantize_mx(out=codes_of(packed), scales=scales_of(packed), in_=grouped[:])
-
-        def quantize_page(i):
-            if i == LAST - 1:
-                page_q[i] = placed.tile([P, 2 * PACKED], U32, name="page_q_late", offset=LATE_B, align_bytes=64)
-                moves = [slice(0, PACKED), slice(PACKED, 2 * PACKED)]
-            else:
-                page_q[i] = ring.tile([P, 2 * PACKED], U32, name="page_q", align_bytes=64)
-                moves = [slice(0, (i // PACK + 1) * PACKED)]
-            for h in range(i // PACK + 1):
-                quantize_z(i, h, z_grouped[i, h])
-            for cols in moves:
-                for c in range(PACK):
-                    nc.sync.dma_start(
-                        quadrant(z_q[i // PACK, c][:, cols], place(i, c)), quadrant(page_q[i][:, cols], c)
-                    )
-
-        def side_work(r):
-            liq, dep, vap = r + 1, r - 1, r + 2
-            liquid = [(liquid_open, liq, 0), (liquid_close, liq, 0), (liquid_open, liq, 1), (liquid_close, liq, 1)]
-            if liq not in TURNED_PAGES:
-                liquid += [(liquid_gap, liq, 0), (liquid_base, liq, 0), (liquid_gap, liq, 1), (liquid_base, liq, 1)]
-            liquid += [(liquid_join, liq, 0)]
-            if r == LAST:
-                liquid = [(regroup_joint, c) for c in range(PACK)]
-            steps = [
-                None, (vapour_join, liq, 1), None, None, None, None,
-                (depart, dep, 0, 0), None, (depart, dep, 0, 1), None, (depart, dep, 1, 0),
-                (vapour_product, vap, 0), (depart, dep, 1, 1), None, (regroup, dep, 0),
-                None, (regroup, dep, 1), (liquid_join, liq, 1), (vapour_product, vap, 1), (vapour_gap, vap, 0),
-                (vapour_base, vap, 0), (vapour_gap, vap, 1), (vapour_base, vap, 1), (vapour_join, vap, 0),
-            ]
-            for step in steps:
-                if step is None:
-                    step = liquid.pop(0) if liquid else None
-                if step is not None and step[1] < PAGES:
-                    step[0](*step[1:])
-
-        def scatter(i, lst, values, weights, j0, j1):
-            nc.vector.tensor_tensor(
-                neg_pages[i][:].indirect(lst[:, j0 // 16 : j1 // 16]), values, weights[:, j0:j1], ALU.mult
+            m0 = h * HALF + d * BANK
+            turn_sum(acc, [refs[i][:, m0 : m0 + BANK], neg_pages[i][:, m0 : m0 + BANK]])
+            first, second = place(i, 2 * d), place(i, 2 * d + 1)
+            step = 16 + second - first
+            dst = stage[h, d][:, first : first + 2 * step, :].rearrange("m (c y) w -> m c y w", c=2)[:, :, 0:13:4, :]
+            nc.scalar.copy(
+                dst.rearrange("m c (b u) (q e) -> m c b u q e", u=2, e=2),
+                acc[:].rearrange("m (c b q u e) -> m c b u q e", c=2, b=2, u=2, e=2),
             )
+
+        def departs(i):
+            return [(depart, i, h, d) for h in range(2) for d in range(2)]
+
+        def turn_back(planes, acc, grouped):
+            for slot, words in enumerate(planes):
+                nc.tensor.transpose(acc[:, slot * P : (slot + 1) * P], words, ident[:])
+            nc.scalar.copy(
+                grouped.bitcast(F32).rearrange("p (b n u) -> p b n u", n=P, u=2),
+                acc[:, : len(planes) * P].rearrange("p (b u n) -> p b n u", n=P, u=2),
+            )
+
+        def regroup(a, h, c):
+            if a == 0:
+                grouped_z[a, h, c] = kept([P, HALF], BF16, "grouped0%d%d" % (h, c))
+            else:
+                grouped_z[a, h, c] = at(V2_WORDS + 2 * HALF * (PACK * h + c), [P, HALF], BF16, "grouped1%d%d" % (h, c))
+            words = stage[h, c // 2][:].rearrange("m x w -> m (x w)").bitcast(F32)
+            w0 = (c % 2) * BANK
+            turn_back([words[:, w0 + k * P : w0 + (k + 1) * P] for k in range(PACK)], next_bank(), grouped_z[a, h, c][:])
+            if (a, h) == (0, 0):
+                quantize(operand[a, h, c], grouped_z[a, h, c][:])
+
+        def regroups(a):
+            return [(regroup, a, h, c) for h in range(2) for c in range(PACK)]
 
         def project(acc, a, h, c):
             wo_cols = wo_last[c] if a == 1 else wo_q[0]
@@ -496,53 +459,40 @@ def tile_list_two_phase_weave_kernel(
                 copy(result[:, nh0:nh1].rearrange("p nh m -> p (nh m)"), acc[:, nh0 * COLS : nh1 * COLS])
                 nc.sync.dma_start(rows[:, nh0:nh1], result[:, nh0:nh1])
 
-        head = [
+        def run(steps):
+            for step in steps:
+                step[0](*step[1:])
+
+        run([
             (liquid_close, 0, 0), (liquid_open, 0, 0), (liquid_close, 1, 0), (liquid_join, 0, 0),
             (liquid_open, 1, 0), (liquid_open, 0, 1), (liquid_join, 1, 0),
             (liquid_close, 0, 1), (liquid_open, 1, 1), (liquid_join, 0, 1), (liquid_close, 1, 1),
-            (vapour_product, 0, 0), (liquid_join, 1, 1),
-        ]
-        for i in range(3):
-            head += [
-                (vapour_product, i, 1), (vapour_gap, i, 0), (vapour_base, i, 0), (vapour_gap, i, 1),
-                (vapour_base, i, 1), (vapour_join, i, 0),
-            ]
-            if i < 2:
-                head += [(vapour_product, i + 1, 0), (vapour_join, i, 1)]
-            if i == 0:
-                head += [(quantize_w1, 1)]
-        w3_rest = load_w3(W_COLS, H, "w3_rest")
-        for step in head:
-            step[0](*step[1:])
-        for i in range(HEAD_PAGES):
-            neg_pages.append(page_bytes(F32, "neg_page", i))
+            (vapour_product, 0, 0), (liquid_join, 1, 1), (quantize_w1, 1),
+        ])
         for s in range(2):
-            for i in range(HEAD_PAGES):
+            for i in range(2):
                 scatter(i, idx3, neg_h1[i][:, s * BANK : (s + 1) * BANK], wg1_sb, s * BANK, (s + 1) * BANK)
-
-        for i in range(PAGES):
-            if i >= HEAD_PAGES:
-                neg_pages.append(page_bytes(F32, "neg_page", i))
-            scatter(i, idx4, neg_h2[i][:], wg2_sb, 0, S)
-            if i >= HEAD_PAGES:
-                quantize_page(i - 2)
-                cut = LAST_CUT if i == LAST else S
-                scatter(i, idx3, neg_h1[i][:, :cut], wg1_sb, 0, cut)
-            if i >= 1:
-                side_work(i)
-            if 1 <= i < H // W_COLS - 1:
-                quantize_w1(i + 1)
-            if i == LAST - 1:
-                prepare_wo()
-
-        round_wo(0, placed.tile([P, N, PACK], BF16, name="wo_grouped0", offset=LATE_A, align_bytes=64))
-        quantize_wo(0)
-        neg_h1_end = placed.tile([P, S - LAST_CUT], F32, name="neg_h1_end", offset=LATE_B)
+        run(vapour(0)[1:])
+        run(weave(liquid(2), vapour(1)[:-1]) + [(quantize_w1, 2)] + vapour(1)[-1:])
+        run(liquid(3))
+        for i in range(3):
+            extra = [(quantize_w1, 3), (load_wo,)] if i == 0 else []
+            run(weave(departs(i) + extra + liquid(i + 4), vapour(i + 2)))
+        run(weave(departs(3) + regroups(0), vapour(5) + vapour(6)))
+        run(weave(departs(4) + liquid(LAST)[:-2], vapour(LAST)))
+        run(departs(5) + [(quantize_wo, 1)] + liquid(LAST)[-2:])
+        run(departs(6) + [(quantize_wo, 0)] + regroups(1))
+        neg_h1_end = at(stage_spot[1, 1], [P, S - LAST_CUT], F32, "neg_h1_end")
         nc.scalar.activation(neg_h1_end[:], held[0][:, LAST_CUT - BANK :], COPY, scale=-1.0)
         scatter(LAST, idx3, neg_h1_end[:], wg1_sb, LAST_CUT, S)
-        quantize_page(LAST - 1)
 
         refs[LAST] = load_ref(LAST)
+
+        def turn_onto(acc, src, h, b, opens):
+            for c in range(PACK):
+                m0 = h * HALF + c * COLS + b * P
+                turn(acc, c, src[:, m0 : m0 + P], opens and c == 0, not opens and c == PACK - 1)
+
         sum_banks = list(range(TURN, HELD_BANK)) + [next_number() for k in range(2)]
         result_banks = [next_number() for k in range(PACK - 1)] + [HELD_BANK]
         sums = {(h, b): bank(sum_banks[2 * h + b]) for h in range(2) for b in range(2)}
@@ -552,41 +502,62 @@ def tile_list_two_phase_weave_kernel(
         for c in range(PACK):
             results[0, c] = bank(result_banks[c])
             project(results[0, c], 0, 0, c)
-        for (h, b), acc in sums.items():
-            z_t[LAST, h, b] = z_t_tile()
-            turn_onto(acc, neg_pages[LAST], h, b, False)
-            round_z(acc, z_t[LAST, h, b], b == 1)
-        grouped = [
-            placed.tile([P, HALF], BF16, name="z_grouped_last%d" % h, offset=(1 - h) * 2 * HALF, align_bytes=64)
-            for h in range(2)
-        ]
-        for (h, b), acc in sums.items():
-            block = grouped[h][:, b * BANK : (b + 1) * BANK]
-            turn_back([z_t[LAST, h, b][:]], bank(sum_banks[2 * h + b]), block, nc.scalar.copy)
-
-        late_first = placed.tile([P, 2 * PACKED], U32, name="z_q_late_first", offset=WG1, align_bytes=64)
-        late_rest = placed.tile([P, 2 * PACKED], U32, name="z_q_late_rest", offset=2 * HALF, align_bytes=64)
+        spare = STAGE
+        last_grouped = [kept([P, HALF], BF16, "last_grouped%d" % h) for h in range(2)]
+        late = at(LATE, [P, 2 * PACK * PACKED], U32, "z_q_late")
         for c in range(PACK):
-            operand[0, 1, c] = half_of((late_first, late_rest)[c // 2], c % 2)
-        for c in range(2):
-            quantize_joint(c)
-        for h in range(2):
-            if h == 1:
-                for c in range(PACK):
-                    if c >= 2:
-                        quantize_joint(c)
-                    results[1, c] = bank(sum_banks[c])
-                    project(results[1, c], 0, 1, c)
-            own = half_of(z_q[1, 0], h)
+            operand[1, 0, c] = part_of(late, c)
+            operand[c % 2, 1, c // 2] = part_of(late, PACK + c)
+        last_q = kept([P, 2 * PACKED], U32, "last_q")
+
+        def regroup_last(h):
+            last_t = []
             for b in range(2):
-                nc.vector.quantize_mx(
-                    out=codes_of(own, b * P, (b + 1) * P)[:QUAD], scales=scales_of(own, b * P, (b + 1) * P)[:QUAD],
-                    in_=grouped[h][:QUAD, b * BANK : (b + 1) * BANK],
+                last_t.append(at(spare + 2 * BANK * (3 - 2 * h - b), [P, BANK], BF16, "last_t%d%d" % (h, b)))
+                turn_onto(sums[h, b], neg_pages[LAST], h, b, False)
+                nc.scalar.copy(
+                    last_t[b][:].rearrange("m (u cq e) -> m u cq e", u=2, e=2),
+                    sums[h, b][:].rearrange("m (cq u e) -> m u cq e", u=2, e=2),
                 )
-            quantize_z(LAST, h, grouped[h])
-            for c in range(PACK):
-                if c > 0:
-                    nc.vector.tensor_copy(quadrant(half_of(z_q[1, c], h), c), quadrant(half_of(page_q[LAST], h), c))
-                project(results[h, c], 1, h, c)
-            for c in range(PACK):
-                store(results[h, c], h, c)
+            for b in range(2):
+                words = last_t[b][:].bitcast(F32)
+                turn_back(
+                    [words[:, u * P : (u + 1) * P] for u in range(2)], bank(sum_banks[2 * h + b]),
+                    last_grouped[h][:, b * BANK : (b + 1) * BANK],
+                )
+
+        def quantize_z(a, h, c):
+            quantize(operand[a, h, c], grouped_z[a, h, c][:])
+
+        def add_last(h, c):
+            if c == 0:
+                own = operand[1, h, 0]
+                for b in range(2):
+                    nc.vector.quantize_mx(
+                        out=codes_of(own, b * P, (b + 1) * P)[:QUAD], scales=scales_of(own, b * P, (b + 1) * P)[:QUAD],
+                        in_=last_grouped[h][:QUAD, b * BANK : (b + 1) * BANK],
+                    )
+            else:
+                if c == 1:
+                    quantize(part_of(last_q, h), last_grouped[h][:])
+                nc.vector.tensor_copy(quadrant(operand[1, h, c], c), quadrant(part_of(last_q, h), c))
+
+        regroup_last(0)
+        later = at(spare + 2 * BANK * 3, [P, PACK * PACKED], U32, "z_q_later")
+        for c in range(PACK):
+            operand[c % 2, 1, 2 + c // 2] = part_of(later, c)
+        for c in range(PACK):
+            quantize_z(1, 0, c)
+            add_last(0, c)
+            project(results[0, c], 1, 0, c)
+            store(results[0, c], 0, c)
+            if c == 0:
+                regroup_last(1)
+        for c in range(PACK):
+            quantize_z(0, 1, c)
+            quantize_z(1, 1, c)
+            results[1, c] = bank(sum_banks[c])
+            project(results[1, c], 0, 1, c)
+            add_last(1, c)
+            project(results[1, c], 1, 1, c)
+            store(results[1, c], 1, c)

@@ -31,8 +31,7 @@ PACKED = COLS + COLS // PACK
 W_COLS = 2 * P
 TURNED_PAGES = range(4)
 TURN = 5
-HELD_BANK = BANKS - 1
-LAST_CUT = 640
+LAST_CUT = 768
 UNIT = 2 * QUAD
 STAGE_UNITS = 38
 
@@ -46,7 +45,8 @@ W1_WORDS = V_WORDS + 4 * S
 W2_WORDS = W1_WORDS + 4 * H
 W1_SCALES = W2_WORDS + 2 * H
 RAW = W1_SCALES + H
-STAGE = RAW + 4 * 2 * PACK * N
+WO_GROUPED = RAW + 4 * 2 * PACK * N
+STAGE = WO_GROUPED + 2 * 2 * PACK * N
 
 
 def weave(*chains):
@@ -71,10 +71,11 @@ def tile_list_two_phase_weave_kernel(
             return psum.tile([P, BANK], F32, name="bank%d" % k)
 
         taken = []
+        turn_of = [TURN]
 
         def next_number():
             taken.append(0)
-            return len(taken) % TURN
+            return len(taken) % turn_of[0]
 
         def next_bank():
             return bank(next_number())
@@ -215,10 +216,11 @@ def tile_list_two_phase_weave_kernel(
             nc.scalar.activation(gap_t[:], acc[:], RELU, scale=sign)
             return gap_t
 
-        def base_part(term, sign):
+        def base_part(term, sign, base_t=None):
             acc = next_bank()
             turn_sum(acc, [term])
-            base_t = ring.tile([P, BANK], F32, name="base_t", tag="parts_b", bufs=4)
+            if base_t is None:
+                base_t = ring.tile([P, BANK], F32, name="base_t", tag="parts_b", bufs=4)
             nc.scalar.activation(base_t[:], acc[:], COPY, scale=sign)
             return base_t
 
@@ -235,7 +237,6 @@ def tile_list_two_phase_weave_kernel(
         liquid_parts = {}
         b_sb = {}
         neg_a = {}
-        held = []
 
         def w1_cols(i):
             g, c0 = divmod(i * P, W_COLS)
@@ -298,16 +299,12 @@ def tile_list_two_phase_weave_kernel(
 
         def liquid_join(i, s):
             if s == 0:
-                neg_h1[i] = ring.tile([P, S], F32, name="neg_h1", bufs=2)
-            very_last = i == LAST and s == 1
-            both = bank(HELD_BANK) if very_last else next_bank()
+                neg_h1[i] = ring.tile([P, S], F32, name="neg_h1", tag="neg_h1_%d" % (i % 2), bufs=1)
+            both = next_bank()
             turn_sum(both, liquid_parts[i, s])
-            width = LAST_CUT - BANK if very_last else BANK
-            nc.scalar.activation(neg_h1[i][:, s * BANK : s * BANK + width], both[:, :width], COPY, scale=-1.0)
-            if very_last:
-                held.append(both)
+            nc.scalar.activation(neg_h1[i][:, s * BANK : (s + 1) * BANK], both[:], COPY, scale=-1.0)
             if i >= 2 and s == 1:
-                cut = BANK + width
+                cut = LAST_CUT if i == LAST else S
                 scatter(i, idx3, neg_h1[i][:, :cut], wg1_sb, 0, cut)
 
         def liquid(i):
@@ -343,11 +340,12 @@ def tile_list_two_phase_weave_kernel(
             vapour_parts[i, s] = [gap_part([caps[i][:, s * BANK : (s + 1) * BANK], neg_sum[i, s]], -1.0)]
 
         def vapour_base(i, s):
-            vapour_parts[i, s].append(base_part(neg_sum[i, s], 1.0))
+            own = at(WO_GROUPED, [P, BANK], F32, "base_last") if (i, s) == (LAST, 1) else None
+            vapour_parts[i, s].append(base_part(neg_sum[i, s], 1.0, own))
 
         def vapour_join(i, s):
             if s == 0:
-                neg_h2[i] = ring.tile([P, S], F32, name="neg_h2", bufs=3)
+                neg_h2[i] = ring.tile([P, S], F32, name="neg_h2", tag="neg_h2_%d" % (i % 3), bufs=1)
             both = next_bank()
             turn_sum(both, vapour_parts[i, s])
             nc.scalar.copy(neg_h2[i][:, s * BANK : (s + 1) * BANK], both[:])
@@ -387,7 +385,7 @@ def tile_list_two_phase_weave_kernel(
             nc.sync.dma_start(wo_raw[0][:], wo.rearrange("(a p j) n -> p a j n", a=2, j=PACK))
 
         def quantize_wo(a):
-            grouped = at(ref_spot(LAST - 1 - a), [P, N, PACK], BF16, "wo_grouped%d" % a)
+            grouped = at(WO_GROUPED + 2 * PACK * N * (1 - a), [P, N, PACK], BF16, "wo_grouped%d" % a)
             round_rows(wo_raw[0][:, a], grouped[:])
             quantize(wo_q[a][:], grouped[:].rearrange("p n j -> p (n j)"))
             if a == 1:
@@ -399,7 +397,7 @@ def tile_list_two_phase_weave_kernel(
         stage_spot = {(h, d): STAGE + 2 * STAGE_UNITS * UNIT * (2 * h + d) for h in range(2) for d in range(2)}
         stage = {key: at(spot, [P, STAGE_UNITS, UNIT], BF16, "stage%d%d" % key) for key, spot in stage_spot.items()}
         grouped_z = {}
-        operand = {(0, 0, c): kept([P, PACKED], U32, "z_q00%d" % c)[:] for c in range(PACK)}
+        operand = {}
 
         def depart(i, h, d):
             acc = next_bank()
@@ -434,8 +432,9 @@ def tile_list_two_phase_weave_kernel(
             words = stage[h, c // 2][:].rearrange("m x w -> m (x w)").bitcast(F32)
             w0 = (c % 2) * BANK
             turn_back([words[:, w0 + k * P : w0 + (k + 1) * P] for k in range(PACK)], next_bank(), grouped_z[a, h, c][:])
-            if (a, h) == (0, 0):
-                quantize(operand[a, h, c], grouped_z[a, h, c][:])
+
+        def quantize_z(a, h, c):
+            quantize(operand[a, h, c], grouped_z[a, h, c][:])
 
         def regroups(a):
             return [(regroup, a, h, c) for h in range(2) for c in range(PACK)]
@@ -467,24 +466,39 @@ def tile_list_two_phase_weave_kernel(
             (liquid_close, 0, 0), (liquid_open, 0, 0), (liquid_close, 1, 0), (liquid_join, 0, 0),
             (liquid_open, 1, 0), (liquid_open, 0, 1), (liquid_join, 1, 0),
             (liquid_close, 0, 1), (liquid_open, 1, 1), (liquid_join, 0, 1), (liquid_close, 1, 1),
-            (vapour_product, 0, 0), (liquid_join, 1, 1), (quantize_w1, 1),
+            (quantize_w1, 1), (vapour_product, 0, 0), (vapour_product, 0, 1), (liquid_join, 1, 1),
         ])
         for s in range(2):
             for i in range(2):
                 scatter(i, idx3, neg_h1[i][:, s * BANK : (s + 1) * BANK], wg1_sb, s * BANK, (s + 1) * BANK)
-        run(vapour(0)[1:])
-        run(weave(liquid(2), vapour(1)[:-1]) + [(quantize_w1, 2)] + vapour(1)[-1:])
-        run(liquid(3))
+
+        def products(stream):
+            return [step for step in stream if step[0] in (vapour_product, liquid_open, liquid_close)]
+
+        def parts(stream):
+            return [step for step in stream if step[0] in (vapour_gap, vapour_base, liquid_gap, liquid_base)]
+
+        def joins(stream):
+            return stream[-2:]
+
+        def slot(stream, before, beside):
+            if beside and beside[0][0] is depart:
+                run(products(stream) + joins(before)[:1] + weave(beside, parts(stream)) + joins(before)[1:])
+            else:
+                run(products(stream) + joins(before) + weave(beside, parts(stream)))
+
+        run(parts(vapour(0)))
+        slot(vapour(1), vapour(0), [])
+        run(products(liquid(2)) + joins(vapour(1))[:1] + [(quantize_w1, 2)] + joins(liquid(2)))
+        run(products(liquid(3)) + joins(vapour(1))[1:])
         for i in range(3):
-            extra = [(quantize_w1, 3), (load_wo,)] if i == 0 else []
-            run(weave(departs(i) + extra + liquid(i + 4), vapour(i + 2)))
-        run(weave(departs(3) + regroups(0), vapour(5) + vapour(6)))
-        run(weave(departs(4) + liquid(LAST)[:-2], vapour(LAST)))
-        run(departs(5) + [(quantize_wo, 1)] + liquid(LAST)[-2:])
-        run(departs(6) + [(quantize_wo, 0)] + regroups(1))
-        neg_h1_end = at(stage_spot[1, 1], [P, S - LAST_CUT], F32, "neg_h1_end")
-        nc.scalar.activation(neg_h1_end[:], held[0][:, LAST_CUT - BANK :], COPY, scale=-1.0)
-        scatter(LAST, idx3, neg_h1_end[:], wg1_sb, LAST_CUT, S)
+            slot(vapour(i + 2), liquid(i + 3), [(quantize_w1, 3), (load_wo,)] if i == 0 else [])
+            slot(liquid(i + 4), vapour(i + 2), departs(i))
+        slot(vapour(5), liquid(6), [(quantize_wo, 0)])
+        slot(vapour(6), vapour(5), departs(3))
+        slot(vapour(7), vapour(6), regroups(0))
+        slot(liquid(7), vapour(7), departs(4))
+        quantize_wo(1)
 
         refs[LAST] = load_ref(LAST)
 
@@ -493,11 +507,24 @@ def tile_list_two_phase_weave_kernel(
                 m0 = h * HALF + c * COLS + b * P
                 turn(acc, c, src[:, m0 : m0 + P], opens and c == 0, not opens and c == PACK - 1)
 
-        sum_banks = list(range(TURN, HELD_BANK)) + [next_number() for k in range(2)]
-        result_banks = [next_number() for k in range(PACK - 1)] + [HELD_BANK]
+        turn_of[0] = PACK
+        sum_banks = [BANKS - 1 - k for k in range(PACK)]
         sums = {(h, b): bank(sum_banks[2 * h + b]) for h in range(2) for b in range(2)}
         for (h, b), acc in sums.items():
             turn_onto(acc, refs[LAST], h, b, True)
+
+        run(joins(liquid(7)))
+        run(departs(5) + departs(6)[:3] + regroups(1)[:1] + departs(6)[3:])
+        early = at(ref_spot(LAST - 1), [P, PACK * PACKED], U32, "z_q_early")
+        for c in range(PACK):
+            operand[0, 0, c] = part_of(early, c)
+            quantize_z(0, 0, c)
+        run(regroups(1)[1:])
+        neg_h1_end = at(stage_spot[1, 1], [P, S - LAST_CUT], F32, "neg_h1_end")
+        nc.scalar.copy(neg_h1_end[:], neg_h1[LAST][:, LAST_CUT:])
+        scatter(LAST, idx3, neg_h1_end[:], wg1_sb, LAST_CUT, S)
+
+        result_banks = [next_number() for k in range(PACK)]
         results = {}
         for c in range(PACK):
             results[0, c] = bank(result_banks[c])
@@ -525,9 +552,6 @@ def tile_list_two_phase_weave_kernel(
                     [words[:, u * P : (u + 1) * P] for u in range(2)], bank(sum_banks[2 * h + b]),
                     last_grouped[h][:, b * BANK : (b + 1) * BANK],
                 )
-
-        def quantize_z(a, h, c):
-            quantize(operand[a, h, c], grouped_z[a, h, c][:])
 
         def add_last(h, c):
             if c == 0:

@@ -28,31 +28,31 @@ LAST = PAGES - 1
 HALF = T2 // 2
 COLS = 256
 PACKED = COLS + COLS // PACK
-W_COLS = 2 * P
+HEAD_PAGES = 2
+W_COLS = HEAD_PAGES * P
 TURNED_PAGES = range(4)
 TURN = 5
-LAST_CUT = 768
 UNIT = 2 * QUAD
-STAGE_UNITS = 38
+RANGE_UNITS = 16
+STAGE_UNITS = 2 * RANGE_UNITS + 6
 
-REF = 0
-V2_ROWS = REF + 3 * 4 * T2
-V2_WORDS = V2_ROWS + S
+V2_WORDS = 0
 W3 = V2_WORDS + 2 * 4 * S
-LATE = W3 + 2 * 4 * H
-V_WORDS = LATE + 4 * S
+REF = W3 + 2 * 4 * H
+V_WORDS = REF + 3 * 4 * T2
+LATE = V_WORDS - 4 * T2 + 4 * P
 W1_WORDS = V_WORDS + 4 * S
 W2_WORDS = W1_WORDS + 4 * H
 W1_SCALES = W2_WORDS + 2 * H
 RAW = W1_SCALES + H
 WO_GROUPED = RAW + 4 * 2 * PACK * N
-STAGE = WO_GROUPED + 2 * 2 * PACK * N
+STAGE = WO_GROUPED + 2 * PACK * N
 
 
-def weave(*chains):
+def weave(first, second):
     steps = []
-    for k in range(max(len(chain) for chain in chains)):
-        steps += [chain[k] for chain in chains if k < len(chain)]
+    for k in range(max(len(first), len(second))):
+        steps += [chain[k] for chain in (first, second) if k < len(chain)]
     return steps
 
 
@@ -71,11 +71,11 @@ def tile_list_two_phase_weave_kernel(
             return psum.tile([P, BANK], F32, name="bank%d" % k)
 
         taken = []
-        turn_of = [TURN]
+        turn_of = [list(range(TURN))]
 
         def next_number():
             taken.append(0)
-            return len(taken) % turn_of[0]
+            return turn_of[0][len(taken) % len(turn_of[0])]
 
         def next_bank():
             return bank(next_number())
@@ -125,7 +125,7 @@ def tile_list_two_phase_weave_kernel(
         w1_raw = {}
 
         def load_w1(g):
-            w1_raw[g] = at(RAW, [P, PACK, W_COLS], F32, "w1_raw%d" % g)
+            w1_raw[g] = at(RAW if g else STAGE, [P, PACK, W_COLS], F32, "w1_raw%d" % g)
             nc.sync.dma_start(
                 w1_raw[g][:], w1[:, g * W_COLS : (g + 1) * W_COLS].rearrange("(p j) c -> p j c", j=PACK)
             )
@@ -133,7 +133,7 @@ def tile_list_two_phase_weave_kernel(
         def quantize_w1(g):
             if g not in w1_raw:
                 load_w1(g)
-            spot = V2_ROWS if g == 0 else RAW + 4 * PACK * W_COLS + 2 * PACK * W_COLS * (g % 2)
+            spot = RAW + 4 * PACK * W_COLS + 2 * PACK * W_COLS * (g % 2)
             grouped = at(spot, [P, W_COLS, PACK], BF16, "w1_grouped%d" % g)
             round_rows(w1_raw[g][:], grouped[:])
             nc.vector.quantize_mx(
@@ -146,7 +146,7 @@ def tile_list_two_phase_weave_kernel(
             return t
 
         def ref_spot(i):
-            return REF + 4 * T2 * (i % 3)
+            return REF + 4 * T2 * ((i + 1) % 3)
 
         def load_ref(i):
             t = at(ref_spot(i), [P, T2], F32, "ref_rows%d" % i)
@@ -167,17 +167,17 @@ def tile_list_two_phase_weave_kernel(
         v_w = gather(at(V_WORDS, [P, S], U32, "v_w"), tab_w, idx)
         quantize_w1(0)
         idx2 = load_list(offs2, "idx2")
-        tab2_s = at(V2_WORDS + 4 * S - T // 2, [P, T], U8, "tab2_s")
-        rows = tab2_scales.rearrange("a q t -> (a q) t").bitcast(I32).unsqueeze(1)
-        nc.sync.dma_start(tab2_s[:].bitcast(I32), rows.broadcast_to([QUAD, PACK, T // 4]))
         w2_w = at(W2_WORDS, [P, 2 * H], U8, "w2_w")
         nc.sync.dma_start(w2_w[:].bitcast(I32), w2_words[0].bitcast(I32))
         w2_s = load_scales(w2_scales, "w2_s", nc.scalar)
-        v2_s_rows = gather(at(V2_ROWS, [P, S], U8, "v2_s_rows"), tab2_s, idx2)
+        tab2_s = kept([P, T], U8, "tab2_s")
+        rows = tab2_scales.rearrange("a q t -> (a q) t").bitcast(I32).unsqueeze(1)
+        nc.sync.dma_start(tab2_s[:].bitcast(I32), rows.broadcast_to([QUAD, PACK, T // 4]))
+        v2_s_rows = gather(at(STAGE, [P, S], U8, "v2_s_rows"), tab2_s, idx2)
         tab2_w = [load_words(page_bytes(U32, "tab2_w%d" % a, a), tab2_words[a]) for a in range(2)]
         v2_w = [gather(at(V2_WORDS + 4 * S * a, [P, S], U32, "v2_w%d" % a), tab2_w[a], idx2) for a in range(2)]
         idx3 = load_list(offs3, "idx3")
-        wg1_sb = at(LATE, [P, S], F32, "wg1_sb")
+        wg1_sb = kept([P, S], F32, "wg1_sb")
         nc.sync.dma_start(wg1_sb[:], wg1)
         ident = keep.tile([P, P], F32, name="ident")
         make_identity(nc, ident[:])
@@ -198,9 +198,9 @@ def tile_list_two_phase_weave_kernel(
         nc.sync.dma_start(wg2_sb[:], wg2)
         w3_rest = load_w3(W_COLS, H)
 
-        def turn(acc, slot, src, start, stop):
+        def turn(acc, slot, src, start, stop, by=ident):
             nc.tensor.matmul(
-                acc[:, slot * P : (slot + 1) * P], lhsT=src, rhs=ident[:], is_transpose=True, start=start, stop=stop
+                acc[:, slot * P : (slot + 1) * P], lhsT=src, rhs=by[:], is_transpose=True, start=start, stop=stop
             )
 
         def turn_sum(acc, sources):
@@ -303,13 +303,11 @@ def tile_list_two_phase_weave_kernel(
             both = next_bank()
             turn_sum(both, liquid_parts[i, s])
             nc.scalar.activation(neg_h1[i][:, s * BANK : (s + 1) * BANK], both[:], COPY, scale=-1.0)
-            if i >= 2 and s == 1:
-                cut = LAST_CUT if i == LAST else S
-                scatter(i, idx3, neg_h1[i][:, :cut], wg1_sb, 0, cut)
+            if i >= HEAD_PAGES and s == 1:
+                scatter(i, idx3, neg_h1[i][:], wg1_sb, 0, S)
 
         def liquid(i):
-            names = [liquid_open, liquid_close]
-            steps = [(f, i, s) for s in range(2) for f in names]
+            steps = [(f, i, s) for s in range(2) for f in (liquid_open, liquid_close)]
             if i not in TURNED_PAGES:
                 steps += [(f, i, s) for s in range(2) for f in (liquid_gap, liquid_base)]
             return steps + [(liquid_join, i, s) for s in range(2)]
@@ -324,7 +322,7 @@ def tile_list_two_phase_weave_kernel(
                 caps[i] = load_cap(i)
             acc = next_bank()
             for a in range(2):
-                if i * P < W_COLS:
+                if i < HEAD_PAGES:
                     w3_cols = w3_head[a][:, i * P : (i + 1) * P]
                 else:
                     w3_cols = w3_rest[a][:, i * P - W_COLS : (i + 1) * P - W_COLS]
@@ -376,7 +374,7 @@ def tile_list_two_phase_weave_kernel(
                 return PACK - 1
             return i % PACK
 
-        wo_q = [kept([P, PACKED], U32, "wo_q%d" % a) for a in range(2)]
+        wo_q = {1: kept([P, PACKED], U32, "wo_q1")}
         wo_last = [kept([P, PACKED], U32, "wo_last%d" % c) for c in range(PACK - 1)] + [wo_q[1]]
         wo_raw = []
 
@@ -384,30 +382,55 @@ def tile_list_two_phase_weave_kernel(
             wo_raw.append(at(RAW, [P, 2, PACK, N], F32, "wo_raw"))
             nc.sync.dma_start(wo_raw[0][:], wo.rearrange("(a p j) n -> p a j n", a=2, j=PACK))
 
+        wo_grouped = {}
+
+        def round_wo(a):
+            wo_grouped[a] = at((ref_spot(LAST - 2), WO_GROUPED)[a], [P, N, PACK], BF16, "wo_grouped%d" % a)
+            round_rows(wo_raw[0][:, a], wo_grouped[a][:])
+
         def quantize_wo(a):
-            grouped = at(WO_GROUPED + 2 * PACK * N * (1 - a), [P, N, PACK], BF16, "wo_grouped%d" % a)
-            round_rows(wo_raw[0][:, a], grouped[:])
-            quantize(wo_q[a][:], grouped[:].rearrange("p n j -> p (n j)"))
+            quantize(wo_q[a][:, :], wo_grouped[a][:].rearrange("p n j -> p (n j)"))
             if a == 1:
                 for c in range(PACK - 1):
                     for q in range(PACK):
                         nc.sync.dma_start(quadrant(wo_last[c], place(PACK + q, c)), quadrant(wo_q[1], q))
 
         refs = {}
-        stage_spot = {(h, d): STAGE + 2 * STAGE_UNITS * UNIT * (2 * h + d) for h in range(2) for d in range(2)}
-        stage = {key: at(spot, [P, STAGE_UNITS, UNIT], BF16, "stage%d%d" % key) for key, spot in stage_spot.items()}
+        stage = {
+            (a, h, d): at(
+                STAGE + 2 * STAGE_UNITS * UNIT * (PACK * a + 2 * h + d), [P, STAGE_UNITS, UNIT], BF16,
+                "stage%d%d%d" % (a, h, d),
+            )
+            for a in range(2) for h in range(2) for d in range(2)
+        }
+        for h in range(2):
+            for c in range(PACK):
+                first = RANGE_UNITS * (c % 2) + place(LAST, c)
+                nc.gpsimd.memset(stage[1, h, c // 2][:, first : first + 3 * PACK + 1 : PACK, :], 0.0)
         grouped_z = {}
         operand = {}
+        opened = {}
 
-        def depart(i, h, d):
-            acc = next_bank()
+        def turn_blocks(acc, src, h, d, opens):
+            for k in range(PACK):
+                m0 = h * HALF + d * BANK + k * P
+                turn(acc, k, src[:, m0 : m0 + P], opens and k == 0, not opens and k == PACK - 1)
+
+        def open_depart(i, h, d):
+            opened[i, h, d] = next_bank()
             if i not in refs:
                 refs[i] = load_ref(i)
-            m0 = h * HALF + d * BANK
-            turn_sum(acc, [refs[i][:, m0 : m0 + BANK], neg_pages[i][:, m0 : m0 + BANK]])
+            turn_blocks(opened[i, h, d], refs[i], h, d, True)
+
+        def depart(i, h, d):
+            if (i, h, d) not in opened:
+                open_depart(i, h, d)
+            acc = opened[i, h, d]
+            turn_blocks(acc, neg_pages[i], h, d, False)
             first, second = place(i, 2 * d), place(i, 2 * d + 1)
-            step = 16 + second - first
-            dst = stage[h, d][:, first : first + 2 * step, :].rearrange("m (c y) w -> m c y w", c=2)[:, :, 0:13:4, :]
+            step = RANGE_UNITS + second - first
+            both = stage[i // PACK, h, d][:, first : first + 2 * step, :].rearrange("m (c y) w -> m c y w", c=2)
+            dst = both[:, :, 0 : 3 * PACK + 1 : PACK, :]
             nc.scalar.copy(
                 dst.rearrange("m c (b u) (q e) -> m c b u q e", u=2, e=2),
                 acc[:].rearrange("m (c b q u e) -> m c b u q e", c=2, b=2, u=2, e=2),
@@ -428,10 +451,12 @@ def tile_list_two_phase_weave_kernel(
             if a == 0:
                 grouped_z[a, h, c] = kept([P, HALF], BF16, "grouped0%d%d" % (h, c))
             else:
-                grouped_z[a, h, c] = at(V2_WORDS + 2 * HALF * (PACK * h + c), [P, HALF], BF16, "grouped1%d%d" % (h, c))
-            words = stage[h, c // 2][:].rearrange("m x w -> m (x w)").bitcast(F32)
+                spot = V2_WORDS + 2 * HALF * (PACK * h + c)
+                grouped_z[a, h, c] = at(spot, [P, HALF], BF16, "grouped1%d%d" % (h, c))
+            words = stage[a, h, c // 2][:].rearrange("m x w -> m (x w)").bitcast(F32)
             w0 = (c % 2) * BANK
-            turn_back([words[:, w0 + k * P : w0 + (k + 1) * P] for k in range(PACK)], next_bank(), grouped_z[a, h, c][:])
+            planes = [words[:, w0 + k * P : w0 + (k + 1) * P] for k in range(PACK)]
+            turn_back(planes, next_bank(), grouped_z[a, h, c][:])
 
         def quantize_z(a, h, c):
             quantize(operand[a, h, c], grouped_z[a, h, c][:])
@@ -441,22 +466,27 @@ def tile_list_two_phase_weave_kernel(
 
         def project(acc, a, h, c):
             wo_cols = wo_last[c] if a == 1 else wo_q[0]
+            apart = acc[0] is not acc[1]
             for nh in range(N // P):
                 nc.tensor.matmul_mx(
-                    acc[:, nh * COLS : (nh + 1) * COLS],
+                    acc[nh][:, nh * COLS : (nh + 1) * COLS],
                     lhsT=codes_of(wo_cols, nh * P, (nh + 1) * P), lhsT_scale=scales_of(wo_cols, nh * P, (nh + 1) * P),
                     rhs=codes_of(operand[a, h, c]), rhs_scale=scales_of(operand[a, h, c]),
-                    start=(a == 0 and nh == 0), stop=(a == 1 and nh == 1),
+                    start=(a == 0 and (apart or nh == 0)), stop=(a == 1 and (apart or nh == 1)),
                 )
 
-        def store(acc, h, c):
-            result = ring.tile([P, 2, COLS], F32, name="result", tag=("parts_a", "parts_b")[c % 2], bufs=4)
-            copy = nc.vector.tensor_copy if h == 1 and c >= 2 else nc.scalar.copy
+        staged = {}
+
+        def store(acc, h, c, nh0, nh1):
+            if (h, c) not in staged:
+                staged[h, c] = ring.tile([P, 2, COLS], F32, name="result", tag=("parts_a", "parts_b")[c % 2], bufs=4)
+            result = staged[h, c]
+            on_vector = (h, c, nh0) in ((1, PACK - 2, 0), (1, PACK - 1, 1))
+            copy = nc.vector.tensor_copy if on_vector else nc.scalar.copy
             m0 = h * HALF + c * COLS
             rows = out[:, m0 : m0 + COLS].rearrange("(nh p) m -> p nh m", p=P)
-            for nh0, nh1 in ([(0, 1), (1, 2)] if (h, c) in ((0, 0), (1, PACK - 1)) else [(0, 2)]):
-                copy(result[:, nh0:nh1].rearrange("p nh m -> p (nh m)"), acc[:, nh0 * COLS : nh1 * COLS])
-                nc.sync.dma_start(rows[:, nh0:nh1], result[:, nh0:nh1])
+            copy(result[:, nh0:nh1].rearrange("p nh m -> p (nh m)"), acc[nh0][:, nh0 * COLS : nh1 * COLS])
+            nc.sync.dma_start(rows[:, nh0:nh1], result[:, nh0:nh1])
 
         def run(steps):
             for step in steps:
@@ -469,7 +499,7 @@ def tile_list_two_phase_weave_kernel(
             (quantize_w1, 1), (vapour_product, 0, 0), (vapour_product, 0, 1), (liquid_join, 1, 1),
         ])
         for s in range(2):
-            for i in range(2):
+            for i in range(HEAD_PAGES):
                 scatter(i, idx3, neg_h1[i][:, s * BANK : (s + 1) * BANK], wg1_sb, s * BANK, (s + 1) * BANK)
 
         def products(stream):
@@ -489,59 +519,55 @@ def tile_list_two_phase_weave_kernel(
 
         run(parts(vapour(0)))
         slot(vapour(1), vapour(0), [])
-        run(products(liquid(2)) + joins(vapour(1))[:1] + [(quantize_w1, 2)] + joins(liquid(2)))
+        run(products(liquid(2)) + joins(vapour(1))[:1] + joins(liquid(2)) + [(quantize_w1, 2)])
         run(products(liquid(3)) + joins(vapour(1))[1:])
         for i in range(3):
             slot(vapour(i + 2), liquid(i + 3), [(quantize_w1, 3), (load_wo,)] if i == 0 else [])
             slot(liquid(i + 4), vapour(i + 2), departs(i))
-        slot(vapour(5), liquid(6), [(quantize_wo, 0)])
+        slot(vapour(5), liquid(6), [])
         slot(vapour(6), vapour(5), departs(3))
-        slot(vapour(7), vapour(6), regroups(0))
-        slot(liquid(7), vapour(7), departs(4))
-        quantize_wo(1)
+        slot(vapour(LAST), vapour(6), [])
 
+        last_slot = products(liquid(LAST)) + joins(vapour(LAST))[:1] + weave(departs(4), parts(liquid(LAST)))
+        run(last_slot[:-1])
+        lower, upper = list(range(PACK)), list(range(PACK, BANKS))
+        turn_of[0] = upper
+        run(last_slot[-1:] + joins(vapour(LAST))[1:] + [(round_wo, 1), (quantize_wo, 1)])
         refs[LAST] = load_ref(LAST)
+        run(joins(liquid(LAST)))
+        run([(open_depart,) + step[1:] for step in departs(6)])
+        turn_of[0] = lower
+        run(regroups(0)[:PACK] + weave(departs(5), regroups(0)[PACK:]) + [(round_wo, 0)])
+        run(departs(6)[:3] + regroups(1)[:1] + departs(6)[3:] + regroups(1)[1:PACK])
+        result_banks = [next_number() for k in range(PACK)]
+        turn_of[0] = upper
+        run(regroups(1)[PACK:])
 
-        def turn_onto(acc, src, h, b, opens):
+        def turn_onto(acc, src, h, b, opens, by):
             for c in range(PACK):
                 m0 = h * HALF + c * COLS + b * P
-                turn(acc, c, src[:, m0 : m0 + P], opens and c == 0, not opens and c == PACK - 1)
+                turn(acc, c, src[:, m0 : m0 + P], opens and c == 0, not opens and c == PACK - 1, by)
 
-        turn_of[0] = PACK
-        sum_banks = [BANKS - 1 - k for k in range(PACK)]
+        sum_banks = upper
         sums = {(h, b): bank(sum_banks[2 * h + b]) for h in range(2) for b in range(2)}
         for (h, b), acc in sums.items():
-            turn_onto(acc, refs[LAST], h, b, True)
+            turn_onto(acc, refs[LAST], h, b, True, ident)
+        ident_last = at(ref_spot(LAST), [P, P], F32, "ident_last")
+        nc.scalar.copy(ident_last[:], ident[:])
 
-        run(joins(liquid(7)))
-        run(departs(5) + departs(6)[:3] + regroups(1)[:1] + departs(6)[3:])
-        early = at(ref_spot(LAST - 1), [P, PACK * PACKED], U32, "z_q_early")
-        for c in range(PACK):
-            operand[0, 0, c] = part_of(early, c)
-            quantize_z(0, 0, c)
-        run(regroups(1)[1:])
-        neg_h1_end = at(stage_spot[1, 1], [P, S - LAST_CUT], F32, "neg_h1_end")
-        nc.scalar.copy(neg_h1_end[:], neg_h1[LAST][:, LAST_CUT:])
-        scatter(LAST, idx3, neg_h1_end[:], wg1_sb, LAST_CUT, S)
-
-        result_banks = [next_number() for k in range(PACK)]
         results = {}
-        for c in range(PACK):
-            results[0, c] = bank(result_banks[c])
-            project(results[0, c], 0, 0, c)
-        spare = STAGE
         last_grouped = [kept([P, HALF], BF16, "last_grouped%d" % h) for h in range(2)]
-        late = at(LATE, [P, 2 * PACK * PACKED], U32, "z_q_late")
-        for c in range(PACK):
-            operand[1, 0, c] = part_of(late, c)
-            operand[c % 2, 1, c // 2] = part_of(late, PACK + c)
-        last_q = kept([P, 2 * PACKED], U32, "last_q")
+        free = [(a, 0, c) for c in range(PACK) for a in range(2)] + [(a, 1, c) for c in range(2) for a in range(2)]
+        late = at(LATE, [P, (len(free) + 1) * PACKED], U32, "z_q_late")
+        wo_q[0] = part_of(late, 0)
+        for k, key in enumerate(free):
+            operand[key] = part_of(late, k + 1)
 
         def regroup_last(h):
             last_t = []
             for b in range(2):
-                last_t.append(at(spare + 2 * BANK * (3 - 2 * h - b), [P, BANK], BF16, "last_t%d%d" % (h, b)))
-                turn_onto(sums[h, b], neg_pages[LAST], h, b, False)
+                last_t.append(at(STAGE + 2 * BANK * (3 - 2 * h - b), [P, BANK], BF16, "last_t%d%d" % (h, b)))
+                turn_onto(sums[h, b], neg_pages[LAST], h, b, False, ident_last)
                 nc.scalar.copy(
                     last_t[b][:].rearrange("m (u cq e) -> m u cq e", u=2, e=2),
                     sums[h, b][:].rearrange("m (cq u e) -> m u cq e", u=2, e=2),
@@ -553,35 +579,47 @@ def tile_list_two_phase_weave_kernel(
                     last_grouped[h][:, b * BANK : (b + 1) * BANK],
                 )
 
-        def add_last(h, c):
+        def quantize_rows(h, c, grouped, rows):
+            own = operand[1, h, c]
+            for b in range(2):
+                nc.vector.quantize_mx(
+                    out=codes_of(own, b * P, (b + 1) * P)[:rows], scales=scales_of(own, b * P, (b + 1) * P)[:rows],
+                    in_=grouped[:rows, b * BANK : (b + 1) * BANK],
+                )
+
+        def close_range(h, c):
             if c == 0:
-                own = operand[1, h, 0]
-                for b in range(2):
-                    nc.vector.quantize_mx(
-                        out=codes_of(own, b * P, (b + 1) * P)[:QUAD], scales=scales_of(own, b * P, (b + 1) * P)[:QUAD],
-                        in_=last_grouped[h][:QUAD, b * BANK : (b + 1) * BANK],
-                    )
+                quantize_rows(h, 0, last_grouped[h], QUAD)
+            elif c == PACK - 1:
+                quantize_rows(h, c, grouped_z[1, h, c], P - QUAD)
             else:
                 if c == 1:
-                    quantize(part_of(last_q, h), last_grouped[h][:])
-                nc.vector.tensor_copy(quadrant(operand[1, h, c], c), quadrant(part_of(last_q, h), c))
+                    quantize(operand[1, h, PACK - 1], last_grouped[h][:])
+                nc.vector.tensor_copy(quadrant(operand[1, h, c], c), quadrant(operand[1, h, PACK - 1], c))
+            project(results[h, c], 1, h, c)
+            if (h, c) == (0, 0):
+                store(results[h, c], h, c, 0, 1)
+                regroup_last(1)
+                store(results[h, c], h, c, 1, 2)
+            elif (h, c) == (1, PACK - 1):
+                store(results[h, c], h, c, 0, 1)
+                store(results[h, c], h, c, 1, 2)
+            else:
+                store(results[h, c], h, c, 0, 2)
 
         regroup_last(0)
-        later = at(spare + 2 * BANK * 3, [P, PACK * PACKED], U32, "z_q_later")
-        for c in range(PACK):
-            operand[c % 2, 1, 2 + c // 2] = part_of(later, c)
-        for c in range(PACK):
-            quantize_z(1, 0, c)
-            add_last(0, c)
-            project(results[0, c], 1, 0, c)
-            store(results[0, c], 0, c)
-            if c == 0:
-                regroup_last(1)
-        for c in range(PACK):
-            quantize_z(0, 1, c)
-            quantize_z(1, 1, c)
-            results[1, c] = bank(sum_banks[c])
-            project(results[1, c], 0, 1, c)
-            add_last(1, c)
-            project(results[1, c], 1, 1, c)
-            store(results[1, c], 1, c)
+        quantize_wo(0)
+        held = [(a, 1, c) for c in range(2, PACK) for a in range(2)]
+        later = at(STAGE + 2 * BANK * 3, [P, len(held) * PACKED], U32, "z_q_later")
+        for k, key in enumerate(held):
+            operand[key] = part_of(later, k)
+        for h in range(2):
+            for c in range(PACK):
+                quantize_z(0, h, c)
+                if c < PACK - 1:
+                    quantize_z(1, h, c)
+                results[h, c] = [bank((result_banks, sum_banks)[h][c])] * 2
+                if (h, c) == (1, PACK - 1):
+                    results[h, c][1] = bank(result_banks[0])
+                project(results[h, c], 0, h, c)
+                close_range(h, c)

@@ -153,6 +153,11 @@ def tile_list_two_phase_weave_kernel(
             nc.sync.dma_start(t[:], ref[i * P : (i + 1) * P, :])
             return t
 
+        def load_w2(c0, c1):
+            t = at(W2_WORDS + 2 * c0, [P, 2 * (c1 - c0)], U8, "w2_%d" % c0)
+            nc.sync.dma_start(t[:].bitcast(I32), w2_words[0, :, 2 * c0 : 2 * c1].bitcast(I32))
+            return t
+
         def load_w3(c0, c1):
             tiles = [at(W3 + 8 * c0 + 4 * (c1 - c0) * a, [P, c1 - c0], U32, "w3_%d_%d" % (c0, a)) for a in range(2)]
             return [load_words(tiles[a], w3_words[a, :, c0:c1, :]) for a in range(2)]
@@ -167,8 +172,7 @@ def tile_list_two_phase_weave_kernel(
         v_w = gather(at(V_WORDS, [P, S], U32, "v_w"), tab_w, idx)
         quantize_w1(0)
         idx2 = load_list(offs2, "idx2")
-        w2_w = at(W2_WORDS, [P, 2 * H], U8, "w2_w")
-        nc.sync.dma_start(w2_w[:].bitcast(I32), w2_words[0].bitcast(I32))
+        w2_head = load_w2(0, W_COLS)
         w2_s = load_scales(w2_scales, "w2_s", nc.scalar)
         tab2_s = kept([P, T], U8, "tab2_s")
         rows = tab2_scales.rearrange("a q t -> (a q) t").bitcast(I32).unsqueeze(1)
@@ -196,6 +200,7 @@ def tile_list_two_phase_weave_kernel(
         idx4 = load_list(offs4, "idx4")
         wg2_sb = kept([P, S], F32, "wg2_sb")
         nc.sync.dma_start(wg2_sb[:], wg2)
+        w2_rest = load_w2(W_COLS, H)
         w3_rest = load_w3(W_COLS, H)
 
         def turn(acc, slot, src, start, stop, by=ident):
@@ -243,7 +248,8 @@ def tile_list_two_phase_weave_kernel(
             return w1_w[g][:, c0 : c0 + P].bitcast(FP8X4), w1_s[g][:, c0 : c0 + P]
 
         def w2_cols(i):
-            return w2_w[:, 2 * i * P : 2 * (i + 1) * P].bitcast(FP4X4), w2_s[:, i * P : (i + 1) * P]
+            words, c0 = (w2_head, i * P) if i < HEAD_PAGES else (w2_rest, i * P - W_COLS)
+            return words[:, 2 * c0 : 2 * (c0 + P)].bitcast(FP4X4), w2_s[:, i * P : (i + 1) * P]
 
         def liquid_tile(name):
             return ring.tile([P, BANK], F32, name=name, tag="liquid", bufs=4, align_bytes=64)

from contextlib import ExitStack

import concourse.mybir as mybir
from concourse.masks import make_identity

K, K2, T, S, H, N, T2 = 512, 1024, 2048, 1024, 1024, 256, 2048
FLOPS = 2 * (2 * K * H * S + K2 * H * S + H * N * T2)

F32 = mybir.dt.float32
BF16 = mybir.dt.bfloat16
I32 = mybir.dt.int32
U32 = mybir.dt.uint32
U16 = mybir.dt.uint16
U8 = mybir.dt.uint8
FP8X4 = mybir.dt.float8_e4m3fn_x4
FP4X4 = mybir.dt.float4_e2m1fn_x4
ALU = mybir.AluOpType
COPY = mybir.ActivationFunctionType.Copy
RELU = mybir.ActivationFunctionType.Relu

P = 128
PACK = 4
QUAD = P // PACK
BANK = 512
BANKS = 8
PAGES = H // P
LAST = PAGES - 1
HALF = T2 // 2
COLS = 256
PACKED = COLS + COLS // PACK
HEAD_PAGES = 2
W_COLS = HEAD_PAGES * P
TURNED_PAGES = range(4)
TURN = 5
UNIT = 2 * QUAD
RANGE_UNITS = 16
STAGE_UNITS = 2 * RANGE_UNITS + 6

V2_WORDS = 0
W3 = V2_WORDS + 2 * 4 * S
REF = W3 + 2 * 4 * H
V_WORDS = REF + 3 * 4 * T2
LATE = V_WORDS - 4 * T2 + 4 * P
W1_WORDS = V_WORDS + 4 * S
W2_WORDS = W1_WORDS + 4 * H
W1_SCALES = W2_WORDS + 2 * H
RAW = W1_SCALES + H
WO_GROUPED = RAW + 4 * 2 * PACK * N
STAGE = WO_GROUPED + 2 * PACK * N


def weave(first, second):
    steps = []
    for k in range(max(len(first), len(second))):
        steps += [chain[k] for chain in (first, second) if k < len(chain)]
    return steps


def tile_list_two_phase_weave_kernel(
    tc, tab_words, tab_scales, tab2_words, tab2_scales, w1, w2_words, w2_scales, w3_words, w3_scales,
    wo, cap, ref, wg1, wg2, offs, offs2, offs3, offs4, out,
):
    nc = tc.nc
    with ExitStack() as ctx:
        keep = ctx.enter_context(tc.tile_pool(name="keep", bufs=1))
        ring = ctx.enter_context(tc.tile_pool(name="ring", bufs=2))
        placed = ctx.enter_context(tc.tile_pool(name="placed", bufs=1))
        psum = ctx.enter_context(tc.psum_pool(name="psum", bufs=1))

        def bank(k):
            return psum.tile([P, BANK], F32, name="bank%d" % k)

        taken = []
        turn_of = [list(range(TURN))]

        def next_number():
            taken.append(0)
            return turn_of[0][len(taken) % len(turn_of[0])]

        def next_bank():
            return bank(next_number())

        def at(offset, shape, dtype, name):
            return placed.tile(shape, dtype, name=name, offset=offset, align_bytes=64)

        def kept(shape, dtype, name):
            return keep.tile(shape, dtype, name=name, align_bytes=64)

        def quadrant(t, q):
            return t[QUAD * q : QUAD * (q + 1), :].bitcast(I32)

        def load_list(src, name):
            t = keep.tile([P, S // 16], U16, name=name)
            nc.sync.dma_start(t[:], src)
            return t

        def load_words(t, src):
            nc.sync.dma_start(t[:].bitcast(I32), src.rearrange("p n t -> p (n t)").bitcast(I32))
            return t

        def page_bytes(dtype, name, k):
            return ring.tile([P, T2], dtype, name=name, tag="page%d" % (k % 3), bufs=1, align_bytes=64)

        def load_scales(src, name, queue):
            passes, width = src.shape[0], src.shape[2]
            t = kept([P, width], U8, name)
            for q in range(PACK):
                queue.dma_start(
                    t[QUAD * q : QUAD * q + 4 * passes, :].bitcast(I32), src[:, 4 * q : 4 * q + 4, :].bitcast(I32)
                )
            return t

        def gather(t, window, lst):
            nc.vector.tensor_copy(t[:], window[:].indirect(lst[:]))
            return t

        def round_rows(raw, grouped):
            nc.scalar.activation(
                grouped.rearrange("p (c i) j -> p c j i", i=4), raw.rearrange("p j (c i) -> p c j i", i=4),
                COPY, scale=-1.0,
            )

        w1_w = [at(W1_WORDS + 4 * W_COLS * g, [P, W_COLS], U32, "w1_w%d" % g) for g in range(H // W_COLS)]
        w1_s = [at(W1_SCALES + W_COLS * g, [P, W_COLS], U8, "w1_s%d" % g) for g in range(H // W_COLS)]
        w1_raw = {}

        def load_w1(g):
            w1_raw[g] = at(RAW if g else STAGE, [P, PACK, W_COLS], F32, "w1_raw%d" % g)
            nc.sync.dma_start(
                w1_raw[g][:], w1[:, g * W_COLS : (g + 1) * W_COLS].rearrange("(p j) c -> p j c", j=PACK)
            )

        def quantize_w1(g):
            if g not in w1_raw:
                load_w1(g)
            spot = RAW + 4 * PACK * W_COLS + 2 * PACK * W_COLS * (g % 2)
            grouped = at(spot, [P, W_COLS, PACK], BF16, "w1_grouped%d" % g)
            round_rows(w1_raw[g][:], grouped[:])
            nc.vector.quantize_mx(
                out=w1_w[g][:].bitcast(FP8X4), scales=w1_s[g][:], in_=grouped[:].rearrange("p c j -> p (c j)")
            )

        def load_cap(i):
            t = ring.tile([P, S], F32, name="cap_rows", bufs=3)
            nc.sync.dma_start(t[:], cap[i * P : (i + 1) * P, :])
            return t

        def ref_spot(i):
            return REF + 4 * T2 * ((i + 1) % 3)

        def load_ref(i):
            t = at(ref_spot(i), [P, T2], F32, "ref_rows%d" % i)
            nc.sync.dma_start(t[:], ref[i * P : (i + 1) * P, :])
            return t

        def load_w2(c0, c1):
            t = at(W2_WORDS + 2 * c0, [P, 2 * (c1 - c0)], U8, "w2_%d" % c0)
            nc.sync.dma_start(t[:].bitcast(I32), w2_words[0, :, 2 * c0 : 2 * c1].bitcast(I32))
            return t

        def load_w3(c0, c1):
            tiles = [at(W3 + 8 * c0 + 4 * (c1 - c0) * a, [P, c1 - c0], U32, "w3_%d_%d" % (c0, a)) for a in range(2)]
            return [load_words(tiles[a], w3_words[a, :, c0:c1, :]) for a in range(2)]

        idx = load_list(offs, "idx")
        tab_s = kept([P, T], U8, "tab_s")
        for q in range(PACK):
            rows = tab_scales[:, 4 * q : 4 * q + 4, :].bitcast(I32)
            (nc.sync, nc.scalar)[q // 2].dma_start(quadrant(tab_s, q), rows.broadcast_to([QUAD // 4, 4, T // 4]))
        tab_w = load_words(page_bytes(U32, "tab_w", 2), tab_words[0])
        v_s = gather(kept([P, S], U8, "v_s"), tab_s, idx)
        v_w = gather(at(V_WORDS, [P, S], U32, "v_w"), tab_w, idx)
        quantize_w1(0)
        idx2 = load_list(offs2, "idx2")
        w2_head = load_w2(0, W_COLS)
        w2_s = load_scales(w2_scales, "w2_s", nc.scalar)
        tab2_s = kept([P, T], U8, "tab2_s")
        rows = tab2_scales.rearrange("a q t -> (a q) t").bitcast(I32).unsqueeze(1)
        nc.sync.dma_start(tab2_s[:].bitcast(I32), rows.broadcast_to([QUAD, PACK, T // 4]))
        v2_s_rows = gather(at(STAGE, [P, S], U8, "v2_s_rows"), tab2_s, idx2)
        tab2_w = [load_words(page_bytes(U32, "tab2_w%d" % a, a), tab2_words[a]) for a in range(2)]
        v2_w = [gather(at(V2_WORDS + 4 * S * a, [P, S], U32, "v2_w%d" % a), tab2_w[a], idx2) for a in range(2)]
        idx3 = load_list(offs3, "idx3")
        wg1_sb = kept([P, S], F32, "wg1_sb")
        nc.sync.dma_start(wg1_sb[:], wg1)
        ident = keep.tile([P, P], F32, name="ident")
        make_identity(nc, ident[:])
        load_w1(1)
        w3_head = load_w3(0, W_COLS)
        w3_s = load_scales(w3_scales, "w3_s", nc.sync)
        v2_s = kept([P, S], U8, "v2_s")
        for a in range(2):
            for q in range(PACK):
                first = 64 * a + 16 * q
                nc.sync.dma_start(
                    v2_s[QUAD * q + 4 * a : QUAD * q + 4 * (a + 1), :].bitcast(I32),
                    v2_s_rows[first : first + 16 : 4, :].bitcast(I32),
                )
        caps = {0: load_cap(0)}
        idx4 = load_list(offs4, "idx4")
        wg2_sb = kept([P, S], F32, "wg2_sb")
        nc.sync.dma_start(wg2_sb[:], wg2)
        w2_rest = load_w2(W_COLS, H)
        w3_rest = load_w3(W_COLS, H)

        def turn(acc, slot, src, start, stop, by=ident):
            nc.tensor.matmul(
                acc[:, slot * P : (slot + 1) * P], lhsT=src, rhs=by[:], is_transpose=True, start=start, stop=stop
            )

        def turn_sum(acc, sources):
            for k, src in enumerate(sources):
                for b in range(PACK):
                    closes = k == len(sources) - 1 and b == PACK - 1
                    turn(acc, b, src[:, b * P : (b + 1) * P], k == 0 and b == 0, closes)

        def gap_part(terms, sign):
            acc = next_bank()
            turn_sum(acc, terms)
            gap_t = ring.tile([P, BANK], F32, name="gap_t", tag="parts_a", bufs=4)
            nc.scalar.activation(gap_t[:], acc[:], RELU, scale=sign)
            return gap_t

        def base_part(term, sign, base_t=None):
            acc = next_bank()
            turn_sum(acc, [term])
            if base_t is None:
                base_t = ring.tile([P, BANK], F32, name="base_t", tag="parts_b", bufs=4)
            nc.scalar.activation(base_t[:], acc[:], COPY, scale=sign)
            return base_t

        neg_pages = {}

        def scatter(i, lst, values, weights, j0, j1):
            if i not in neg_pages:
                neg_pages[i] = page_bytes(F32, "neg_page", i)
            nc.vector.tensor_tensor(
                neg_pages[i][:].indirect(lst[:, j0 // 16 : j1 // 16]), values, weights[:, j0:j1], ALU.mult
            )

        neg_h1 = {}
        liquid_parts = {}
        b_sb = {}
        neg_a = {}

        def w1_cols(i):
            g, c0 = divmod(i * P, W_COLS)
            return w1_w[g][:, c0 : c0 + P].bitcast(FP8X4), w1_s[g][:, c0 : c0 + P]

        def w2_cols(i):
            words, c0 = (w2_head, i * P) if i < HEAD_PAGES else (w2_rest, i * P - W_COLS)
            return words[:, 2 * c0 : 2 * (c0 + P)].bitcast(FP4X4), w2_s[:, i * P : (i + 1) * P]

        def liquid_tile(name):
            return ring.tile([P, BANK], F32, name=name, tag="liquid", bufs=4, align_bytes=64)

        def cells_times(s, operands):
            acc = next_bank()
            for b in range(PACK):
                cells = slice(s * BANK + b * P, s * BANK + (b + 1) * P)
                for k, (words, scales) in enumerate(operands):
                    nc.tensor.matmul_mx(
                        acc[:, b * P : (b + 1) * P], lhsT=v_w[:, cells].bitcast(FP8X4), lhsT_scale=v_s[:, cells],
                        rhs=words, rhs_scale=scales, start=(k == 0), stop=(k == len(operands) - 1),
                    )
            return acc

        def times_cells(s, words, scales):
            acc = next_bank()
            cells = slice(s * BANK, (s + 1) * BANK)
            nc.tensor.matmul_mx(
                acc[:], lhsT=words, lhsT_scale=scales,
                rhs=v_w[:, cells].bitcast(FP8X4), rhs_scale=v_s[:, cells], start=True, stop=True,
            )
            return acc

        def liquid_open(i, s):
            if i in TURNED_PAGES:
                acc = cells_times(s, [w1_cols(i), w2_cols(i)])
                lead_t = liquid_tile("lead_t")
                nc.scalar.activation(lead_t[:], acc[:], RELU)
                liquid_parts.setdefault((i, s), []).append(lead_t)
            else:
                acc = times_cells(s, *w2_cols(i))
                b_sb[i, s] = liquid_tile("b_sb")
                nc.scalar.copy(b_sb[i, s][:], acc[:])
                liquid_parts[i, s] = []

        def liquid_close(i, s):
            if i in TURNED_PAGES:
                acc = cells_times(s, [w1_cols(i)])
                a_t = liquid_tile("a_t")
                nc.scalar.activation(a_t[:], acc[:], COPY, scale=-1.0)
                liquid_parts.setdefault((i, s), []).append(a_t)
            else:
                acc = times_cells(s, *w1_cols(i))
                neg_a[i, s] = ring.tile([P, BANK], F32, name="neg_a", tag="sums", bufs=4)
                nc.scalar.copy(neg_a[i, s][:], acc[:])

        def liquid_gap(i, s):
            liquid_parts[i, s].append(gap_part([b_sb[i, s], neg_a[i, s]], 1.0))

        def liquid_base(i, s):
            liquid_parts[i, s].append(base_part(neg_a[i, s], -1.0))

        def liquid_join(i, s):
            if s == 0:
                neg_h1[i] = ring.tile([P, S], F32, name="neg_h1", tag="neg_h1_%d" % (i % 2), bufs=1)
            both = next_bank()
            turn_sum(both, liquid_parts[i, s])
            nc.scalar.activation(neg_h1[i][:, s * BANK : (s + 1) * BANK], both[:], COPY, scale=-1.0)
            if i >= HEAD_PAGES and s == 1:
                scatter(i, idx3, neg_h1[i][:], wg1_sb, 0, S)

        def liquid(i):
            steps = [(f, i, s) for s in range(2) for f in (liquid_open, liquid_close)]
            if i not in TURNED_PAGES:
                steps += [(f, i, s) for s in range(2) for f in (liquid_gap, liquid_base)]
            return steps + [(liquid_join, i, s) for s in range(2)]

        neg_h2 = {}
        neg_sum = {}
        vapour_parts = {}

        def vapour_product(i, s):
            cells = slice(s * BANK, (s + 1) * BANK)
            if i not in caps:
                caps[i] = load_cap(i)
            acc = next_bank()
            for a in range(2):
                if i < HEAD_PAGES:
                    w3_cols = w3_head[a][:, i * P : (i + 1) * P]
                else:
                    w3_cols = w3_rest[a][:, i * P - W_COLS : (i + 1) * P - W_COLS]
                nc.tensor.matmul_mx(
                    acc[:], lhsT=w3_cols.bitcast(FP8X4), lhsT_scale=w3_s[4 * a :, i * P : (i + 1) * P],
                    rhs=v2_w[a][:, cells].bitcast(FP8X4), rhs_scale=v2_s[4 * a :, cells],
                    start=(a == 0), stop=(a == 1),
                )
            neg_sum[i, s] = ring.tile([P, BANK], F32, name="neg_sum", tag="sums", bufs=4)
            nc.scalar.activation(neg_sum[i, s][:], acc[:], COPY, scale=-1.0)

        def vapour_gap(i, s):
            vapour_parts[i, s] = [gap_part([caps[i][:, s * BANK : (s + 1) * BANK], neg_sum[i, s]], -1.0)]

        def vapour_base(i, s):
            own = at(WO_GROUPED, [P, BANK], F32, "base_last") if (i, s) == (LAST, 1) else None
            vapour_parts[i, s].append(base_part(neg_sum[i, s], 1.0, own))

        def vapour_join(i, s):
            if s == 0:
                neg_h2[i] = ring.tile([P, S], F32, name="neg_h2", tag="neg_h2_%d" % (i % 3), bufs=1)
            both = next_bank()
            turn_sum(both, vapour_parts[i, s])
            nc.scalar.copy(neg_h2[i][:, s * BANK : (s + 1) * BANK], both[:])
            if s == 1:
                scatter(i, idx4, neg_h2[i][:], wg2_sb, 0, S)

        def vapour(i):
            steps = [(vapour_product, i, s) for s in range(2)]
            steps += [(f, i, s) for s in range(2) for f in (vapour_gap, vapour_base)]
            return steps + [(vapour_join, i, s) for s in range(2)]

        def part_of(t, k):
            return t[:, k * PACKED : (k + 1) * PACKED]

        def codes_of(t, c0=0, c1=COLS):
            return t[:, c0:c1].bitcast(FP8X4)

        def scales_of(t, c0=0, c1=COLS):
            return t[:, COLS:].bitcast(U8)[:, c0:c1]

        def quantize(packed, grouped):
            nc.vector.quantize_mx(out=codes_of(packed), scales=scales_of(packed), in_=grouped)

        def place(i, c):
            if i == LAST:
                return c
            if i == PACK + c:
                return PACK - 1
            return i % PACK

        wo_q = {1: kept([P, PACKED], U32, "wo_q1")}
        wo_last = [kept([P, PACKED], U32, "wo_last%d" % c) for c in range(PACK - 1)] + [wo_q[1]]
        wo_raw = []

        def load_wo():
            wo_raw.append(at(RAW, [P, 2, PACK, N], F32, "wo_raw"))
            nc.sync.dma_start(wo_raw[0][:], wo.rearrange("(a p j) n -> p a j n", a=2, j=PACK))

        wo_grouped = {}

        def round_wo(a):
            wo_grouped[a] = at((ref_spot(LAST - 2), WO_GROUPED)[a], [P, N, PACK], BF16, "wo_grouped%d" % a)
            round_rows(wo_raw[0][:, a], wo_grouped[a][:])

        def quantize_wo(a):
            quantize(wo_q[a][:, :], wo_grouped[a][:].rearrange("p n j -> p (n j)"))
            if a == 1:
                for c in range(PACK - 1):
                    for q in range(PACK):
                        nc.sync.dma_start(quadrant(wo_last[c], place(PACK + q, c)), quadrant(wo_q[1], q))

        refs = {}
        stage = {
            (a, h, d): at(
                STAGE + 2 * STAGE_UNITS * UNIT * (PACK * a + 2 * h + d), [P, STAGE_UNITS, UNIT], BF16,
                "stage%d%d%d" % (a, h, d),
            )
            for a in range(2) for h in range(2) for d in range(2)
        }
        for h in range(2):
            for c in range(PACK):
                first = RANGE_UNITS * (c % 2) + place(LAST, c)
                nc.gpsimd.memset(stage[1, h, c // 2][:, first : first + 3 * PACK + 1 : PACK, :], 0.0)
        grouped_z = {}
        operand = {}
        opened = {}

        def turn_blocks(acc, src, h, d, opens):
            for k in range(PACK):
                m0 = h * HALF + d * BANK + k * P
                turn(acc, k, src[:, m0 : m0 + P], opens and k == 0, not opens and k == PACK - 1)

        def open_depart(i, h, d):
            opened[i, h, d] = next_bank()
            if i not in refs:
                refs[i] = load_ref(i)
            turn_blocks(opened[i, h, d], refs[i], h, d, True)

        def depart(i, h, d):
            if (i, h, d) not in opened:
                open_depart(i, h, d)
            acc = opened[i, h, d]
            turn_blocks(acc, neg_pages[i], h, d, False)
            first, second = place(i, 2 * d), place(i, 2 * d + 1)
            step = RANGE_UNITS + second - first
            both = stage[i // PACK, h, d][:, first : first + 2 * step, :].rearrange("m (c y) w -> m c y w", c=2)
            dst = both[:, :, 0 : 3 * PACK + 1 : PACK, :]
            nc.scalar.copy(
                dst.rearrange("m c (b u) (q e) -> m c b u q e", u=2, e=2),
                acc[:].rearrange("m (c b q u e) -> m c b u q e", c=2, b=2, u=2, e=2),
            )

        def departs(i):
            return [(depart, i, h, d) for h in range(2) for d in range(2)]

        def turn_back(planes, acc, grouped):
            for slot, words in enumerate(planes):
                nc.tensor.transpose(acc[:, slot * P : (slot + 1) * P], words, ident[:])
            nc.scalar.copy(
                grouped.bitcast(F32).rearrange("p (b n u) -> p b n u", n=P, u=2),
                acc[:, : len(planes) * P].rearrange("p (b u n) -> p b n u", n=P, u=2),
            )

        def regroup(a, h, c):
            if a == 0:
                grouped_z[a, h, c] = kept([P, HALF], BF16, "grouped0%d%d" % (h, c))
            else:
                spot = V2_WORDS + 2 * HALF * (PACK * h + c)
                grouped_z[a, h, c] = at(spot, [P, HALF], BF16, "grouped1%d%d" % (h, c))
            words = stage[a, h, c // 2][:].rearrange("m x w -> m (x w)").bitcast(F32)
            w0 = (c % 2) * BANK
            planes = [words[:, w0 + k * P : w0 + (k + 1) * P] for k in range(PACK)]
            turn_back(planes, next_bank(), grouped_z[a, h, c][:])

        def quantize_z(a, h, c):
            quantize(operand[a, h, c], grouped_z[a, h, c][:])

        def regroups(a):
            return [(regroup, a, h, c) for h in range(2) for c in range(PACK)]

        def project(acc, a, h, c):
            wo_cols = wo_last[c] if a == 1 else wo_q[0]
            apart = acc[0] is not acc[1]
            for nh in range(N // P):
                nc.tensor.matmul_mx(
                    acc[nh][:, nh * COLS : (nh + 1) * COLS],
                    lhsT=codes_of(wo_cols, nh * P, (nh + 1) * P), lhsT_scale=scales_of(wo_cols, nh * P, (nh + 1) * P),
                    rhs=codes_of(operand[a, h, c]), rhs_scale=scales_of(operand[a, h, c]),
                    start=(a == 0 and (apart or nh == 0)), stop=(a == 1 and (apart or nh == 1)),
                )

        staged = {}

        def store(acc, h, c, nh0, nh1):
            if (h, c) not in staged:
                staged[h, c] = ring.tile([P, 2, COLS], F32, name="result", tag=("parts_a", "parts_b")[c % 2], bufs=4)
            result = staged[h, c]
            on_vector = (h, c, nh0) in ((1, PACK - 2, 0), (1, PACK - 1, 1))
            copy = nc.vector.tensor_copy if on_vector else nc.scalar.copy
            m0 = h * HALF + c * COLS
            rows = out[:, m0 : m0 + COLS].rearrange("(nh p) m -> p nh m", p=P)
            copy(result[:, nh0:nh1].rearrange("p nh m -> p (nh m)"), acc[nh0][:, nh0 * COLS : nh1 * COLS])
            nc.sync.dma_start(rows[:, nh0:nh1], result[:, nh0:nh1])

        def run(steps):
            for step in steps:
                step[0](*step[1:])

        run([
            (liquid_close, 0, 0), (liquid_open, 0, 0), (liquid_close, 1, 0), (liquid_join, 0, 0),
            (liquid_open, 1, 0), (liquid_open, 0, 1), (liquid_join, 1, 0),
            (liquid_close, 0, 1), (liquid_open, 1, 1), (liquid_join, 0, 1), (liquid_close, 1, 1),
            (quantize_w1, 1), (vapour_product, 0, 0), (vapour_product, 0, 1), (liquid_join, 1, 1),
        ])
        for s in range(2):
            for i in range(HEAD_PAGES):
                scatter(i, idx3, neg_h1[i][:, s * BANK : (s + 1) * BANK], wg1_sb, s * BANK, (s + 1) * BANK)

        def products(stream):
            return [step for step in stream if step[0] in (vapour_product, liquid_open, liquid_close)]

        def parts(stream):
            return [step for step in stream if step[0] in (vapour_gap, vapour_base, liquid_gap, liquid_base)]

        def joins(stream):
            return stream[-2:]

        def slot(stream, before, beside):
            if beside and beside[0][0] is depart:
                run(products(stream) + joins(before)[:1] + weave(beside, parts(stream)) + joins(before)[1:])
            else:
                run(products(stream) + joins(before) + weave(beside, parts(stream)))

        run(parts(vapour(0)))
        slot(vapour(1), vapour(0), [])
        run(products(liquid(2)) + joins(vapour(1))[:1] + joins(liquid(2)) + [(quantize_w1, 2)])
        run(products(liquid(3)) + joins(vapour(1))[1:])
        for i in range(3):
            slot(vapour(i + 2), liquid(i + 3), [(quantize_w1, 3), (load_wo,)] if i == 0 else [])
            slot(liquid(i + 4), vapour(i + 2), departs(i))
        slot(vapour(5), liquid(6), [])
        slot(vapour(6), vapour(5), departs(3))
        slot(vapour(LAST), vapour(6), [])

        last_slot = products(liquid(LAST)) + joins(vapour(LAST))[:1] + weave(departs(4), parts(liquid(LAST)))
        run(last_slot[:-1])
        lower, upper = list(range(PACK)), list(range(PACK, BANKS))
        turn_of[0] = upper
        run(last_slot[-1:] + joins(vapour(LAST))[1:] + [(round_wo, 1), (quantize_wo, 1)])
        refs[LAST] = load_ref(LAST)
        run(joins(liquid(LAST)))
        run([(open_depart,) + step[1:] for step in departs(6)])
        turn_of[0] = lower
        run(regroups(0)[:PACK] + weave(departs(5), regroups(0)[PACK:]) + [(round_wo, 0)])
        run(departs(6)[:3] + regroups(1)[:1] + departs(6)[3:] + regroups(1)[1:PACK])
        result_banks = [next_number() for k in range(PACK)]
        turn_of[0] = upper
        run(regroups(1)[PACK:])

        def turn_onto(acc, src, h, b, opens, by):
            for c in range(PACK):
                m0 = h * HALF + c * COLS + b * P
                turn(acc, c, src[:, m0 : m0 + P], opens and c == 0, not opens and c == PACK - 1, by)

        sum_banks = upper
        sums = {(h, b): bank(sum_banks[2 * h + b]) for h in range(2) for b in range(2)}
        for (h, b), acc in sums.items():
            turn_onto(acc, refs[LAST], h, b, True, ident)
        ident_last = at(ref_spot(LAST), [P, P], F32, "ident_last")
        nc.scalar.copy(ident_last[:], ident[:])

        results = {}
        last_grouped = [kept([P, HALF], BF16, "last_grouped%d" % h) for h in range(2)]
        free = [(a, 0, c) for c in range(PACK) for a in range(2)] + [(a, 1, c) for c in range(2) for a in range(2)]
        late = at(LATE, [P, (len(free) + 1) * PACKED], U32, "z_q_late")
        wo_q[0] = part_of(late, 0)
        for k, key in enumerate(free):
            operand[key] = part_of(late, k + 1)

        def regroup_last(h):
            last_t = []
            for b in range(2):
                last_t.append(at(STAGE + 2 * BANK * (3 - 2 * h - b), [P, BANK], BF16, "last_t%d%d" % (h, b)))
                turn_onto(sums[h, b], neg_pages[LAST], h, b, False, ident_last)
                nc.scalar.copy(
                    last_t[b][:].rearrange("m (u cq e) -> m u cq e", u=2, e=2),
                    sums[h, b][:].rearrange("m (cq u e) -> m u cq e", u=2, e=2),
                )
            for b in range(2):
                words = last_t[b][:].bitcast(F32)
                turn_back(
                    [words[:, u * P : (u + 1) * P] for u in range(2)], bank(sum_banks[2 * h + b]),
                    last_grouped[h][:, b * BANK : (b + 1) * BANK],
                )

        def quantize_rows(h, c, grouped, rows):
            own = operand[1, h, c]
            for b in range(2):
                nc.vector.quantize_mx(
                    out=codes_of(own, b * P, (b + 1) * P)[:rows], scales=scales_of(own, b * P, (b + 1) * P)[:rows],
                    in_=grouped[:rows, b * BANK : (b + 1) * BANK],
                )

        def close_range(h, c):
            if c == 0:
                quantize_rows(h, 0, last_grouped[h], QUAD)
            elif c == PACK - 1:
                quantize_rows(h, c, grouped_z[1, h, c], P - QUAD)
            else:
                if c == 1:
                    quantize(operand[1, h, PACK - 1], last_grouped[h][:])
                nc.vector.tensor_copy(quadrant(operand[1, h, c], c), quadrant(operand[1, h, PACK - 1], c))
            project(results[h, c], 1, h, c)
            if (h, c) == (0, 0):
                store(results[h, c], h, c, 0, 1)
                regroup_last(1)
                store(results[h, c], h, c, 1, 2)
            elif (h, c) == (1, PACK - 1):
                store(results[h, c], h, c, 0, 1)
                store(results[h, c], h, c, 1, 2)
            else:
                store(results[h, c], h, c, 0, 2)

        regroup_last(0)
        quantize_wo(0)
        held = [(a, 1, c) for c in range(2, PACK) for a in range(2)]
        later = at(STAGE + 2 * BANK * 3, [P, len(held) * PACKED], U32, "z_q_later")
        for k, key in enumerate(held):
            operand[key] = part_of(later, k)
        for h in range(2):
            for c in range(PACK):
                quantize_z(0, h, c)
                if c < PACK - 1:
                    quantize_z(1, h, c)
                results[h, c] = [bank((result_banks, sum_banks)[h][c])] * 2
                if (h, c) == (1, PACK - 1):
                    results[h, c][1] = bank(result_banks[0])
                project(results[h, c], 0, h, c)
                close_range(h, c)
